import numpy as np
import ml_dtypes


def mxq(x, axis, fmt="e4m3"):
    dtype, down = {"e4m3": (ml_dtypes.float8_e4m3fn, 7), "e5m2": (ml_dtypes.float8_e5m2, 14)}[fmt]
    v = np.moveaxis(np.asarray(x, np.float32).astype(ml_dtypes.bfloat16).astype(np.float64), axis, -1)
    blocks = v.reshape(v.shape[:-1] + (-1, 32))
    amax = np.abs(blocks).max(-1, keepdims=True)
    byte = np.maximum(np.where(amax > 0, np.frexp(amax)[1] - 1 + 127, 0) - down, 1)
    scale = np.exp2(byte - 127.0)
    codes = (blocks / scale).astype(np.float32).astype(dtype).astype(np.float64)
    return np.moveaxis((codes * scale).reshape(v.shape), -1, axis)


WIDE = False


def mx_kscale(k):
    if not WIDE:
        return np.ones(k)
    levels = np.array([30, -30])
    if k % 512:
        return np.exp2(np.random.permutation(np.resize(levels, k // 32))).repeat(32)
    a = np.empty((k // 512, 16))
    for p in range(k // 512):
        a[p, :8] = np.random.permutation(np.resize(levels, 8))
        for g in range(8):
            far = levels[np.abs(levels - a[p, g]) >= 10]
            a[p, g + 8] = far[np.random.randint(len(far))]
    return np.exp2(a.ravel()).repeat(32)


def f64(x):
    return np.asarray(x).astype(np.float64)


def striped(idx):
    return np.tile(idx.reshape(-1, 16).T, (8, 1)).astype(np.uint16)


def unstriped(offs):
    return offs[:16].T.reshape(-1).astype(np.int64)


E2M1 = np.array([0.0, 0.5, 1.0, 1.5, 2.0, 3.0, 4.0, 6.0, -0.0, -0.5, -1.0, -1.5, -2.0, -3.0, -4.0, -6.0])


def pack_weight(w, fmt):
    k, n = w.shape
    w = f64(np.asarray(w, np.float32).astype(ml_dtypes.bfloat16)).reshape(k // 32, 32, n)
    amax = np.abs(w).max(1)
    if fmt == "e4m3":
        byte = np.frexp(amax)[1] - 1 + 127 - 7
    elif fmt == "e5m2":
        byte = np.frexp(amax)[1] - 1 + 127 - 14
    else:
        mant, ex = np.frexp(amax / 6.0)
        byte = np.where(mant > 0.5, ex, ex - 1) + 127
    byte = np.clip(np.where(amax > 0, byte, 1), 1, 254)
    scaled = (w * np.exp2(127.0 - byte)[:, None, :]).reshape(k, n).astype(np.float32)
    by_word = np.ascontiguousarray(scaled.reshape(k // 512, 128, 4, n).transpose(0, 1, 3, 2))
    if fmt == "e4m3":
        words = by_word.astype(ml_dtypes.float8_e4m3fn).view(np.uint8)
    elif fmt == "e5m2":
        words = by_word.astype(ml_dtypes.float8_e5m2).view(np.uint8)
    else:
        c = by_word.astype(ml_dtypes.float4_e2m1fn).view(np.uint8) & 0xF
        words = (c[..., 0::2] | (c[..., 1::2] << 4)).reshape(k // 512, 128, 2 * n)
    return np.ascontiguousarray(words), np.ascontiguousarray(byte.astype(np.uint8).reshape(k // 512, 16, n))


def unpack_weight(words, scales, fmt):
    g, _, n = scales.shape
    words = np.ascontiguousarray(words).reshape(g, 128, n, -1)
    if fmt == "e4m3":
        vals = words.view(ml_dtypes.float8_e4m3fn).astype(np.float64)
    elif fmt == "e5m2":
        vals = words.view(ml_dtypes.float8_e5m2).astype(np.float64)
    else:
        nib = np.empty((g, 128, n, 4), np.uint8)
        nib[..., 0::2] = words & 0xF
        nib[..., 1::2] = words >> 4
        vals = E2M1[nib]
    vals = vals * np.repeat(np.exp2(scales.astype(np.float64) - 127.0), 8, axis=1)[..., None]
    return vals.transpose(0, 1, 3, 2).reshape(g * 512, n)


def d_relu(v):
    return (v > 0).astype(np.float64)


K, T, E, C, H, N = 512, 1024, 4, 512, 512, 512


def by_expert(wq, xq):
    return np.concatenate([wq[e].T @ xq[:, e * C:(e + 1) * C] for e in range(E)], axis=1)


def setup_inputs():
    n = np.random.standard_normal
    v = mx_kscale(N)
    u = mx_kscale(H)
    first = np.random.permutation(np.repeat(np.arange(E), T // E))
    second = (first + 1 + np.random.permutation(np.repeat(np.arange(E - 1), -(-T // (E - 1)))[:T])) % E
    while np.bincount(second, minlength=E).max() != T // E:
        load = np.bincount(second, minlength=E); hi, lo = int(load.argmax()), int(load.argmin())
        t = np.flatnonzero((second == hi) & (first != lo))[0]; second[t] = lo
    slot_token = np.empty(E * C, np.int64); pos = np.empty((2, T), np.int64); fill = np.zeros(E, np.int64)
    place = np.stack([np.random.permutation(C) for _ in range(E)])
    for r, deal in enumerate((first, second)):
        for t in np.random.permutation(T):
            e = deal[t]; j = e * C + place[e, fill[e]]; fill[e] += 1; slot_token[j] = t; pos[r, t] = j
    g = np.random.uniform(0.2, 0.8, T)
    w_slot = np.empty(E * C); w_slot[pos[0]] = g; w_slot[pos[1]] = 1.0 - g
    dy = pack_weight(n((N, T)) * v[:, None], "e5m2")
    w2t = pack_weight(n((N, H)) / np.sqrt(N) / v[:, None] * u, "e4m3")
    w1t = [pack_weight(m, "e2m1") for m in n((E, H, K)) / np.sqrt(H) / u[None, :, None]]
    return {
        "dy_words": dy[0],
        "dy_scales": dy[1],
        "w2t_words": w2t[0],
        "w2t_scales": w2t[1],
        "w1t_words": np.stack([m[0] for m in w1t]),
        "w1t_scales": np.stack([m[1] for m in w1t]),
        "a": (n((H, E * C))).astype(np.float32),
        "gate": (np.tile(w_slot, (128, 1))).astype(np.float32),
        "offs": striped(slot_token),
        "pos1": striped(pos[0]),
        "pos2": striped(pos[1]),
    }


def reference(dy_words, dy_scales, w2t_words, w2t_scales, w1t_words, w1t_scales, a, gate, offs, pos1, pos2):
    w2t = unpack_weight(w2t_words, w2t_scales, "e4m3")
    w1t = np.stack([unpack_weight(w1t_words[e], w1t_scales[e], "e2m1") for e in range(E)])
    idx = unstriped(offs)
    dc = w2t.T @ unpack_weight(dy_words, dy_scales, "e5m2")
    da = f64(gate[:1]) * dc[:, idx] * d_relu(f64(a))
    dx = by_expert(w1t, mxq(da, 0, "e5m2"))
    out = dx[:, unstriped(pos1)] + dx[:, unstriped(pos2)]
    return out

@@ -1,0 +1,149 @@
+from contextlib import ExitStack
+
+import concourse.mybir as mybir
+
+K, T, E, C, H, N = 512, 1024, 4, 512, 512, 512
+S = E * C
+FLOPS = 2 * N * H * T + 2 * H * K * S
+
+F32 = mybir.dt.float32
+BF16 = mybir.dt.bfloat16
+I32 = mybir.dt.int32
+U16 = mybir.dt.uint16
+U8 = mybir.dt.uint8
+E4M3 = mybir.dt.float8_e4m3fn_x4
+E5M2 = mybir.dt.float8_e5m2_x4
+E2M1 = mybir.dt.float4_e2m1fn_x4
+ALU = mybir.AluOpType
+P = 128
+PACK = 4
+BANK = 512
+
+
+def tile_moe_sdb_relu_kernel(
+    tc, dy_words, dy_scales, w2t_words, w2t_scales, w1t_words, w1t_scales, a, gate, offs, pos1, pos2, out
+):
+    nc = tc.nc
+    with ExitStack() as ctx:
+        keep = ctx.enter_context(tc.tile_pool(name="keep", bufs=1))
+        psum = ctx.enter_context(tc.psum_pool(name="psum", bufs=4))
+
+        offs_t = keep.tile([P, S // 16], U16, name="offs_t")
+        pos1_t = keep.tile([P, T // 16], U16, name="pos1_t")
+        pos2_t = keep.tile([P, T // 16], U16, name="pos2_t")
+
+        w2_raw = keep.tile([P, H], I32, name="w2_raw", align_bytes=64)
+        w2s_raw = keep.tile([P, H], U8, name="w2s_raw", align_bytes=64)
+        w2 = keep.tile([P, H], I32, name="w2", align_bytes=64)
+        w2s = keep.tile([P, H], U8, name="w2s", align_bytes=64)
+        dy = keep.tile([P, T], I32, name="dy", align_bytes=64)
+        dys = keep.tile([P, T], U8, name="dys", align_bytes=64)
+        w1 = keep.tile([P, E, 2 * K], U8, name="w1", align_bytes=64)
+        w1s = keep.tile([P, E, K], U8, name="w1s", align_bytes=64)
+
+        nc.vector.memset(w2s_raw[:].bitcast(I32), 0)
+        nc.vector.memset(dys[:].bitcast(I32), 0)
+        nc.vector.memset(w1s[:].rearrange("p e k -> p (e k)").bitcast(I32), 0)
+
+        nc.sync.dma_start(w2_raw[:], w2t_words[0].rearrange("p n t -> p (n t)").bitcast(I32))
+        for q in range(4):
+            nc.sync.dma_start(w2s_raw[32 * q : 32 * q + 4, :].bitcast(I32), w2t_scales[0, 4 * q : 4 * q + 4, :].bitcast(I32))
+        nc.sync.dma_start(dy[:], dy_words[0].rearrange("p n t -> p (n t)").bitcast(I32))
+        for q in range(4):
+            eng = nc.scalar if q < 2 else nc.gpsimd
+            eng.dma_start(dys[32 * q : 32 * q + 4, :].bitcast(I32), dy_scales[0, 4 * q : 4 * q + 4, :].bitcast(I32))
+        nc.sync.dma_start(offs_t[:], offs)
+        gates = []
+        saved = []
+        for e in range(E):
+            g = keep.tile([P, C], F32, name=f"gate{e}")
+            nc.sync.dma_start(g[:], gate[:, e * C : (e + 1) * C])
+            gates.append(g)
+            s = keep.tile([P, PACK, C], F32, name=f"saved{e}")
+            nc.sync.dma_start(s[:], a[:, e * C : (e + 1) * C].rearrange("(p t) j -> p t j", t=PACK))
+            saved.append(s)
+            if e == 1:
+                nc.sync.dma_start(w1[:].bitcast(I32), w1t_words[:, 0].rearrange("e p k -> p e k").bitcast(I32))
+                for q in range(4):
+                    nc.sync.dma_start(
+                        w1s[32 * q : 32 * q + 4].bitcast(I32),
+                        w1t_scales[:, 0, 4 * q : 4 * q + 4, :].rearrange("e r k -> r e k").bitcast(I32),
+                    )
+        nc.sync.dma_start(pos1_t[:], pos1)
+        nc.sync.dma_start(pos2_t[:], pos2)
+
+        nc.vector.tensor_copy(w2[:].rearrange("p (t m) -> p t m", t=PACK), w2_raw[:].rearrange("p (m t) -> p t m", t=PACK))
+        nc.vector.tensor_copy(w2s[:].rearrange("p (t m) -> p t m", t=PACK), w2s_raw[:].rearrange("p (m t) -> p t m", t=PACK))
+
+        dc = []
+        for t in range(PACK):
+            plane = keep.tile([P, T], F32, name=f"dc{t}")
+            for h in range(T // BANK):
+                cols = slice(h * BANK, (h + 1) * BANK)
+                acc = psum.tile([P, BANK], F32, name="dc_acc")
+                nc.tensor.matmul_mx(
+                    out=acc[:],
+                    lhsT=w2[:, t * P : (t + 1) * P].bitcast(E4M3),
+                    lhsT_scale=w2s[:, t * P : (t + 1) * P],
+                    rhs=dy[:, cols].bitcast(E5M2),
+                    rhs_scale=dys[:, cols],
+                    start=True,
+                    stop=True,
+                )
+                if t == 0 and h == 1:
+                    nc.vector.tensor_copy(plane[:, cols], acc[:])
+                else:
+                    nc.scalar.copy(plane[:, cols], acc[:])
+            dc.append(plane)
+
+        dx = [keep.tile([P, S], F32, name=f"dx{b}") for b in range(K // P)]
+        codes = []
+        scales = []
+
+        def expert_product(e, b):
+            acc = psum.tile([P, BANK], F32, name="dx_acc")
+            nc.tensor.matmul_mx(
+                out=acc[:],
+                lhsT=w1[:, e, 2 * b * P : 2 * (b + 1) * P].bitcast(E2M1),
+                lhsT_scale=w1s[:, e, b * P : (b + 1) * P],
+                rhs=codes[e][:].bitcast(E5M2),
+                rhs_scale=scales[e][:],
+                start=True,
+                stop=True,
+            )
+            nc.scalar.copy(dx[b][:, e * C : (e + 1) * C], acc[:])
+
+        for e in range(E):
+            slots = offs_t[:, e * C // 16 : (e + 1) * C // 16]
+            da = keep.tile([P, PACK, C], F32, name=f"da{e}")
+            if e > 0:
+                nc.vector.scalar_tensor_tensor(
+                    saved[e][:], saved[e][:], 0.0, gates[e][:].unsqueeze(1).to_broadcast([P, PACK, C]), ALU.is_gt, ALU.mult
+                )
+            for t in range(PACK):
+                other = saved[e][:, t, :] if e > 0 else gates[e][:]
+                nc.vector.tensor_tensor(da[:, t, :], dc[t][:].indirect(slots), other, ALU.mult)
+            if e == 0:
+                nc.vector.scalar_tensor_tensor(da[:], saved[e][:], 0.0, da[:], ALU.is_gt, ALU.mult)
+            woven = keep.tile([P, C, PACK], BF16, name=f"woven{e}", align_bytes=64)
+            nc.scalar.copy(
+                woven[:].rearrange("p (c i) t -> p c t i", i=4), da[:].rearrange("p t (c i) -> p c t i", i=4)
+            )
+            cw = keep.tile([P, C], I32, name=f"codes{e}", align_bytes=64)
+            cs = keep.tile([P, C], U8, name=f"scales{e}", align_bytes=64)
+            nc.vector.quantize_mx(out=cw[:].bitcast(E5M2), scales=cs[:], in_=woven[:].rearrange("p c t -> p (c t)"))
+            codes.append(cw)
+            scales.append(cs)
+            expert_product(e, 0)
+        for b in range(1, K // P):
+            for e in range(E):
+                expert_product(e, b)
+
+        for b in range(K // P):
+            first = keep.tile([P, T], F32, name=f"first{b}")
+            nc.vector.tensor_copy(first[:], dx[b][:].indirect(pos1_t[:]))
+            cuts = [0, T] if b < K // P - 1 else [0, 512, 768, T]
+            for lo, hi in zip(cuts, cuts[1:]):
+                res = keep.tile([P, hi - lo], F32, name=f"res{b}_{lo}")
+                nc.vector.tensor_tensor(res[:], dx[b][:].indirect(pos2_t[:, lo // 16 : hi // 16]), first[:, lo:hi], ALU.add)
+                nc.sync.dma_start(out[b * P : (b + 1) * P, lo:hi], res[:])

@@ -15,6 +15,7 @@ E4M3 = mybir.dt.float8_e4m3fn_x4
 E5M2 = mybir.dt.float8_e5m2_x4
 E2M1 = mybir.dt.float4_e2m1fn_x4
 ALU = mybir.AluOpType
+ACT = mybir.ActivationFunctionType
 P = 128
 PACK = 4
 BANK = 512
@@ -41,17 +42,19 @@ def tile_moe_sdb_relu_kernel(
         w1 = keep.tile([P, E, 2 * K], U8, name="w1", align_bytes=64)
         w1s = keep.tile([P, E, K], U8, name="w1s", align_bytes=64)
 
-        nc.vector.memset(w2s_raw[:].bitcast(I32), 0)
-        nc.vector.memset(dys[:].bitcast(I32), 0)
-        nc.vector.memset(w1s[:].rearrange("p e k -> p (e k)").bitcast(I32), 0)
+        nc.gpsimd.memset(w2s_raw[:].bitcast(I32), 0)
 
+        def load_scale_rows(plane, rows, q):
+            nc.sync.dma_start(plane[32 * q : 32 * q + 4, :].bitcast(I32), rows[4 * q : 4 * q + 4, :].bitcast(I32))
+
+        for q in (0, 1):
+            load_scale_rows(dys, dy_scales[0], q)
         nc.sync.dma_start(w2_raw[:], w2t_words[0].rearrange("p n t -> p (n t)").bitcast(I32))
-        for q in range(4):
-            nc.sync.dma_start(w2s_raw[32 * q : 32 * q + 4, :].bitcast(I32), w2t_scales[0, 4 * q : 4 * q + 4, :].bitcast(I32))
         nc.sync.dma_start(dy[:], dy_words[0].rearrange("p n t -> p (n t)").bitcast(I32))
+        for q in (2, 3):
+            load_scale_rows(dys, dy_scales[0], q)
         for q in range(4):
-            eng = nc.scalar if q < 2 else nc.gpsimd
-            eng.dma_start(dys[32 * q : 32 * q + 4, :].bitcast(I32), dy_scales[0, 4 * q : 4 * q + 4, :].bitcast(I32))
+            load_scale_rows(w2s_raw, w2t_scales[0], q)
         nc.sync.dma_start(offs_t[:], offs)
         gates = []
         saved = []
@@ -62,7 +65,7 @@ def tile_moe_sdb_relu_kernel(
             s = keep.tile([P, PACK, C], F32, name=f"saved{e}")
             nc.sync.dma_start(s[:], a[:, e * C : (e + 1) * C].rearrange("(p t) j -> p t j", t=PACK))
             saved.append(s)
-            if e == 1:
+            if e == E - 1:
                 nc.sync.dma_start(w1[:].bitcast(I32), w1t_words[:, 0].rearrange("e p k -> p e k").bitcast(I32))
                 for q in range(4):
                     nc.sync.dma_start(
@@ -111,27 +114,45 @@ def tile_moe_sdb_relu_kernel(
                 start=True,
                 stop=True,
             )
-            nc.scalar.copy(dx[b][:, e * C : (e + 1) * C], acc[:])
+            if (e, b) == (E - 1, 0):
+                nc.vector.tensor_copy(dx[b][:, e * C : (e + 1) * C], acc[:])
+            else:
+                nc.scalar.copy(dx[b][:, e * C : (e + 1) * C], acc[:])
 
+        def weave_out(x):
+            return x[:].rearrange("p (c i) t -> p c t i", i=4)
+
+        def weave_in(x):
+            return x[:].rearrange("p t (c i) -> p c t i", i=4)
+
+        woven = []
+        keepers = []
         for e in range(E):
             slots = offs_t[:, e * C // 16 : (e + 1) * C // 16]
             da = keep.tile([P, PACK, C], F32, name=f"da{e}")
-            if e > 0:
+            last = e == E - 1
+            if last:
                 nc.vector.scalar_tensor_tensor(
                     saved[e][:], saved[e][:], 0.0, gates[e][:].unsqueeze(1).to_broadcast([P, PACK, C]), ALU.is_gt, ALU.mult
                 )
             for t in range(PACK):
-                other = saved[e][:, t, :] if e > 0 else gates[e][:]
+                other = saved[e][:, t, :] if last else gates[e][:]
                 nc.vector.tensor_tensor(da[:, t, :], dc[t][:].indirect(slots), other, ALU.mult)
-            if e == 0:
-                nc.vector.scalar_tensor_tensor(da[:], saved[e][:], 0.0, da[:], ALU.is_gt, ALU.mult)
-            woven = keep.tile([P, C, PACK], BF16, name=f"woven{e}", align_bytes=64)
-            nc.scalar.copy(
-                woven[:].rearrange("p (c i) t -> p c t i", i=4), da[:].rearrange("p t (c i) -> p c t i", i=4)
-            )
+            if not last:
+                mask = keep.tile([P, C, PACK], BF16, name=f"mask{e}")
+                nc.scalar.activation(weave_out(mask), weave_in(saved[e]), ACT.Sign)
+                nc.scalar.activation(mask[:], mask[:], ACT.Relu)
+                keepers.append(mask)
+            w = keep.tile([P, C, PACK], BF16, name=f"woven{e}", align_bytes=64)
+            nc.scalar.copy(weave_out(w), weave_in(da))
+            woven.append(w)
+        nc.vector.tensor_tensor(woven[0][:], woven[0][:], keepers[0][:], ALU.mult)
+        for e in range(E):
+            if e + 1 < E - 1:
+                nc.vector.tensor_tensor(woven[e + 1][:], woven[e + 1][:], keepers[e + 1][:], ALU.mult)
             cw = keep.tile([P, C], I32, name=f"codes{e}", align_bytes=64)
             cs = keep.tile([P, C], U8, name=f"scales{e}", align_bytes=64)
-            nc.vector.quantize_mx(out=cw[:].bitcast(E5M2), scales=cs[:], in_=woven[:].rearrange("p c t -> p (c t)"))
+            nc.vector.quantize_mx(out=cw[:].bitcast(E5M2), scales=cs[:], in_=woven[e][:].rearrange("p c t -> p (c t)"))
             codes.append(cw)
             scales.append(cs)
             expert_product(e, 0)

@@ -19,6 +19,9 @@ ACT = mybir.ActivationFunctionType
 P = 128
 PACK = 4
 BANK = 512
+SPARE = 16
+GROUPS = [(0, 2 * C), (2 * C, 3 * C), (3 * C, S)]
+TAIL_CUTS = [0, 640, 896, T]
 
 
 def tile_moe_sdb_relu_kernel(
@@ -33,57 +36,56 @@ def tile_moe_sdb_relu_kernel(
         pos1_t = keep.tile([P, T // 16], U16, name="pos1_t")
         pos2_t = keep.tile([P, T // 16], U16, name="pos2_t")
 
-        w2_raw = keep.tile([P, H], I32, name="w2_raw", align_bytes=64)
-        w2s_raw = keep.tile([P, H], U8, name="w2s_raw", align_bytes=64)
+        w2_raw = keep.tile([P, H], I32, name="w2_raw")
+        w2s_raw = keep.tile([P, H], U8, name="w2s_raw")
         w2 = keep.tile([P, H], I32, name="w2", align_bytes=64)
         w2s = keep.tile([P, H], U8, name="w2s", align_bytes=64)
         dy = keep.tile([P, T], I32, name="dy", align_bytes=64)
         dys = keep.tile([P, T], U8, name="dys", align_bytes=64)
         w1 = keep.tile([P, E, 2 * K], U8, name="w1", align_bytes=64)
         w1s = keep.tile([P, E, K], U8, name="w1s", align_bytes=64)
+        dc = [keep.tile([P, T + SPARE], F32, name=f"dc{t}") for t in range(PACK)]
 
         nc.gpsimd.memset(w2s_raw[:].bitcast(I32), 0)
+        for plane in dc:
+            nc.vector.memset(plane[:, T:], 0.0)
 
         def load_scale_rows(plane, rows, q):
-            nc.sync.dma_start(plane[32 * q : 32 * q + 4, :].bitcast(I32), rows[4 * q : 4 * q + 4, :].bitcast(I32))
+            nc.sync.dma_start(plane[32 * q : 32 * q + 4].bitcast(I32), rows[4 * q : 4 * q + 4].bitcast(I32))
 
-        for q in (0, 1):
+        for q in range(4):
             load_scale_rows(dys, dy_scales[0], q)
         nc.sync.dma_start(w2_raw[:], w2t_words[0].rearrange("p n t -> p (n t)").bitcast(I32))
         nc.sync.dma_start(dy[:], dy_words[0].rearrange("p n t -> p (n t)").bitcast(I32))
-        for q in (2, 3):
-            load_scale_rows(dys, dy_scales[0], q)
         for q in range(4):
             load_scale_rows(w2s_raw, w2t_scales[0], q)
         nc.sync.dma_start(offs_t[:], offs)
         gates = []
         saved = []
-        for e in range(E):
-            g = keep.tile([P, C], F32, name=f"gate{e}")
-            nc.sync.dma_start(g[:], gate[:, e * C : (e + 1) * C])
-            gates.append(g)
-            s = keep.tile([P, PACK, C], F32, name=f"saved{e}")
-            nc.sync.dma_start(s[:], a[:, e * C : (e + 1) * C].rearrange("(p t) j -> p t j", t=PACK))
-            saved.append(s)
-            if e == E - 1:
-                nc.sync.dma_start(w1[:].bitcast(I32), w1t_words[:, 0].rearrange("e p k -> p e k").bitcast(I32))
-                for q in range(4):
-                    nc.sync.dma_start(
-                        w1s[32 * q : 32 * q + 4].bitcast(I32),
-                        w1t_scales[:, 0, 4 * q : 4 * q + 4, :].rearrange("e r k -> r e k").bitcast(I32),
-                    )
+        for lo, hi in GROUPS:
+            gates.append(keep.tile([P, hi - lo], F32, name=f"gate{lo}"))
+            nc.sync.dma_start(gates[-1][:], gate[:, lo:hi])
+            saved.append(keep.tile([P, PACK, hi - lo], F32, name=f"saved{lo}"))
+            for first in range(lo, hi, C):
+                nc.sync.dma_start(
+                    saved[-1][:, :, first - lo : first - lo + C], a[:, first : first + C].rearrange("(p t) j -> p t j", t=PACK)
+                )
+        nc.sync.dma_start(w1[:].bitcast(I32), w1t_words[:, 0].rearrange("e p k -> p e k").bitcast(I32))
+        for q in range(4):
+            load_scale_rows(w1s, w1t_scales[:, 0].rearrange("e b k -> b e k"), q)
         nc.sync.dma_start(pos1_t[:], pos1)
         nc.sync.dma_start(pos2_t[:], pos2)
 
         nc.vector.tensor_copy(w2[:].rearrange("p (t m) -> p t m", t=PACK), w2_raw[:].rearrange("p (m t) -> p t m", t=PACK))
-        nc.vector.tensor_copy(w2s[:].rearrange("p (t m) -> p t m", t=PACK), w2s_raw[:].rearrange("p (m t) -> p t m", t=PACK))
+        for lo, hi in ((0, 1), (1, PACK)):
+            nc.vector.tensor_copy(
+                w2s[:].rearrange("p (t m) -> p t m", t=PACK)[:, lo:hi], w2s_raw[:].rearrange("p (m t) -> p t m", t=PACK)[:, lo:hi]
+            )
 
-        dc = []
         for t in range(PACK):
-            plane = keep.tile([P, T], F32, name=f"dc{t}")
             for h in range(T // BANK):
                 cols = slice(h * BANK, (h + 1) * BANK)
-                acc = psum.tile([P, BANK], F32, name="dc_acc")
+                acc = psum.tile([P, BANK], F32, name="acc")
                 nc.tensor.matmul_mx(
                     out=acc[:],
                     lhsT=w2[:, t * P : (t + 1) * P].bitcast(E4M3),
@@ -93,31 +95,10 @@ def tile_moe_sdb_relu_kernel(
                     start=True,
                     stop=True,
                 )
-                if t == 0 and h == 1:
-                    nc.vector.tensor_copy(plane[:, cols], acc[:])
+                if (t, h) == (0, 1):
+                    nc.vector.tensor_copy(dc[t][:, cols], acc[:])
                 else:
-                    nc.scalar.copy(plane[:, cols], acc[:])
-            dc.append(plane)
-
-        dx = [keep.tile([P, S], F32, name=f"dx{b}") for b in range(K // P)]
-        codes = []
-        scales = []
-
-        def expert_product(e, b):
-            acc = psum.tile([P, BANK], F32, name="dx_acc")
-            nc.tensor.matmul_mx(
-                out=acc[:],
-                lhsT=w1[:, e, 2 * b * P : 2 * (b + 1) * P].bitcast(E2M1),
-                lhsT_scale=w1s[:, e, b * P : (b + 1) * P],
-                rhs=codes[e][:].bitcast(E5M2),
-                rhs_scale=scales[e][:],
-                start=True,
-                stop=True,
-            )
-            if (e, b) == (E - 1, 0):
-                nc.vector.tensor_copy(dx[b][:, e * C : (e + 1) * C], acc[:])
-            else:
-                nc.scalar.copy(dx[b][:, e * C : (e + 1) * C], acc[:])
+                    nc.scalar.copy(dc[t][:, cols], acc[:])
 
         def weave_out(x):
             return x[:].rearrange("p (c i) t -> p c t i", i=4)
@@ -126,44 +107,67 @@ def tile_moe_sdb_relu_kernel(
             return x[:].rearrange("p t (c i) -> p c t i", i=4)
 
         woven = []
-        keepers = []
-        for e in range(E):
-            slots = offs_t[:, e * C // 16 : (e + 1) * C // 16]
-            da = keep.tile([P, PACK, C], F32, name=f"da{e}")
-            last = e == E - 1
+        active = []
+        for g, (lo, hi) in enumerate(GROUPS):
+            width = hi - lo
+            last = hi == S
+            picked = keep.tile([P, PACK, width], F32, name=f"picked{g}")
             if last:
-                nc.vector.scalar_tensor_tensor(
-                    saved[e][:], saved[e][:], 0.0, gates[e][:].unsqueeze(1).to_broadcast([P, PACK, C]), ALU.is_gt, ALU.mult
-                )
+                spread = gates[g][:].unsqueeze(1).to_broadcast([P, PACK, width])
+                nc.vector.scalar_tensor_tensor(saved[g][:], saved[g][:], 0.0, spread, ALU.is_gt, ALU.mult)
             for t in range(PACK):
-                other = saved[e][:, t, :] if last else gates[e][:]
-                nc.vector.tensor_tensor(da[:, t, :], dc[t][:].indirect(slots), other, ALU.mult)
+                factor = saved[g][:, t, :] if last else gates[g][:]
+                nc.vector.tensor_tensor(picked[:, t, :], dc[t][:].indirect(offs_t[:, lo // 16 : hi // 16]), factor, ALU.mult)
             if not last:
-                mask = keep.tile([P, C, PACK], BF16, name=f"mask{e}")
-                nc.scalar.activation(weave_out(mask), weave_in(saved[e]), ACT.Sign)
-                nc.scalar.activation(mask[:], mask[:], ACT.Relu)
-                keepers.append(mask)
-            w = keep.tile([P, C, PACK], BF16, name=f"woven{e}", align_bytes=64)
-            nc.scalar.copy(weave_out(w), weave_in(da))
-            woven.append(w)
-        nc.vector.tensor_tensor(woven[0][:], woven[0][:], keepers[0][:], ALU.mult)
-        for e in range(E):
-            if e + 1 < E - 1:
-                nc.vector.tensor_tensor(woven[e + 1][:], woven[e + 1][:], keepers[e + 1][:], ALU.mult)
-            cw = keep.tile([P, C], I32, name=f"codes{e}", align_bytes=64)
-            cs = keep.tile([P, C], U8, name=f"scales{e}", align_bytes=64)
-            nc.vector.quantize_mx(out=cw[:].bitcast(E5M2), scales=cs[:], in_=woven[e][:].rearrange("p c t -> p (c t)"))
-            codes.append(cw)
-            scales.append(cs)
-            expert_product(e, 0)
-        for b in range(1, K // P):
+                active.append(keep.tile([P, width, PACK], BF16, name=f"active{g}"))
+                nc.scalar.activation(weave_out(active[g]), weave_in(saved[g]), ACT.Sign)
+                if g == 0:
+                    nc.scalar.activation(active[g][:], active[g][:], ACT.Relu)
+            woven.append(keep.tile([P, width, PACK], BF16, name=f"woven{g}", align_bytes=64))
+            nc.scalar.copy(weave_out(woven[g]), weave_in(picked))
+
+        codes = keep.tile([P, S], I32, name="codes", align_bytes=64)
+        scales = keep.tile([P, S], U8, name="scales", align_bytes=64)
+
+        def expert_product(e, b, target):
+            cols = slice(e * C, (e + 1) * C)
+            acc = psum.tile([P, BANK], F32, name="product", tag="acc" if b else "first")
+            nc.tensor.matmul_mx(
+                out=acc[:],
+                lhsT=w1[:, e, 2 * b * P : 2 * (b + 1) * P].bitcast(E2M1),
+                lhsT_scale=w1s[:, e, b * P : (b + 1) * P],
+                rhs=codes[:, cols].bitcast(E5M2),
+                rhs_scale=scales[:, cols],
+                start=True,
+                stop=True,
+            )
+            if (e, b) == (E - 1, 0):
+                nc.vector.tensor_copy(target[:, cols], acc[:])
+            else:
+                nc.scalar.copy(target[:, cols], acc[:])
+
+        for g, (lo, hi) in enumerate(GROUPS):
+            if hi < S:
+                if g == 1:
+                    nc.vector.tensor_scalar(active[g][:], active[g][:], 0.0, None, ALU.max)
+                nc.vector.tensor_tensor(woven[g][:], woven[g][:], active[g][:], ALU.mult)
+            nc.vector.quantize_mx(
+                out=codes[:, lo:hi].bitcast(E5M2), scales=scales[:, lo:hi], in_=woven[g][:].rearrange("p c t -> p (c t)")
+            )
+        dx = [
+            keep.tile([P, S], F32, name="dx0", tag="picked2"),
+            keep.tile([P, S], F32, name="dx1", tag="woven2", align_bytes=64),
+            keep.tile([P, S], F32, name="dx2", tag="woven1", align_bytes=64),
+            keep.tile([P, S], F32, name="dx3"),
+        ]
+        for b in range(K // P):
             for e in range(E):
-                expert_product(e, b)
+                expert_product(e, b, dx[b])
 
         for b in range(K // P):
             first = keep.tile([P, T], F32, name=f"first{b}")
             nc.vector.tensor_copy(first[:], dx[b][:].indirect(pos1_t[:]))
-            cuts = [0, T] if b < K // P - 1 else [0, 512, 768, T]
+            cuts = [0, T] if b < K // P - 1 else TAIL_CUTS
             for lo, hi in zip(cuts, cuts[1:]):
                 res = keep.tile([P, hi - lo], F32, name=f"res{b}_{lo}")
                 nc.vector.tensor_tensor(res[:], dx[b][:].indirect(pos2_t[:, lo // 16 : hi // 16]), first[:, lo:hi], ALU.add)

@@ -16,12 +16,16 @@ E5M2 = mybir.dt.float8_e5m2_x4
 E2M1 = mybir.dt.float4_e2m1fn_x4
 ALU = mybir.AluOpType
 ACT = mybir.ActivationFunctionType
+
 P = 128
 PACK = 4
+QUADRANTS = 4
 BANK = 512
+LIST_ROWS = 16
+RUN = 4
 SPARE = 16
 GROUPS = [(0, 2 * C), (2 * C, 3 * C), (3 * C, S)]
-TAIL_CUTS = [0, 640, 896, T]
+TAIL_CUTS = [0, 512, 896, T]
 
 
 def tile_moe_sdb_relu_kernel(
@@ -32,9 +36,9 @@ def tile_moe_sdb_relu_kernel(
         keep = ctx.enter_context(tc.tile_pool(name="keep", bufs=1))
         psum = ctx.enter_context(tc.psum_pool(name="psum", bufs=4))
 
-        offs_t = keep.tile([P, S // 16], U16, name="offs_t")
-        pos1_t = keep.tile([P, T // 16], U16, name="pos1_t")
-        pos2_t = keep.tile([P, T // 16], U16, name="pos2_t")
+        offs_t = keep.tile([P, S // LIST_ROWS], U16, name="offs_t")
+        pos1_t = keep.tile([P, T // LIST_ROWS], U16, name="pos1_t")
+        pos2_t = keep.tile([P, T // LIST_ROWS], U16, name="pos2_t")
 
         w2_raw = keep.tile([P, H], I32, name="w2_raw")
         w2s_raw = keep.tile([P, H], U8, name="w2s_raw")
@@ -50,14 +54,14 @@ def tile_moe_sdb_relu_kernel(
         for plane in dc:
             nc.vector.memset(plane[:, T:], 0.0)
 
-        def load_scale_rows(plane, rows, q):
-            nc.sync.dma_start(plane[32 * q : 32 * q + 4].bitcast(I32), rows[4 * q : 4 * q + 4].bitcast(I32))
+        def load_scale_rows(tile, rows, q):
+            nc.sync.dma_start(tile[32 * q : 32 * q + 4].bitcast(I32), rows[4 * q : 4 * q + 4].bitcast(I32))
 
-        for q in range(4):
+        for q in range(QUADRANTS):
             load_scale_rows(dys, dy_scales[0], q)
         nc.sync.dma_start(w2_raw[:], w2t_words[0].rearrange("p n t -> p (n t)").bitcast(I32))
         nc.sync.dma_start(dy[:], dy_words[0].rearrange("p n t -> p (n t)").bitcast(I32))
-        for q in range(4):
+        for q in range(QUADRANTS):
             load_scale_rows(w2s_raw, w2t_scales[0], q)
         nc.sync.dma_start(offs_t[:], offs)
         gates = []
@@ -66,12 +70,12 @@ def tile_moe_sdb_relu_kernel(
             gates.append(keep.tile([P, hi - lo], F32, name=f"gate{lo}"))
             nc.sync.dma_start(gates[-1][:], gate[:, lo:hi])
             saved.append(keep.tile([P, PACK, hi - lo], F32, name=f"saved{lo}"))
-            for first in range(lo, hi, C):
+            for start in range(lo, hi, C):
                 nc.sync.dma_start(
-                    saved[-1][:, :, first - lo : first - lo + C], a[:, first : first + C].rearrange("(p t) j -> p t j", t=PACK)
+                    saved[-1][:, :, start - lo : start - lo + C], a[:, start : start + C].rearrange("(p t) j -> p t j", t=PACK)
                 )
         nc.sync.dma_start(w1[:].bitcast(I32), w1t_words[:, 0].rearrange("e p k -> p e k").bitcast(I32))
-        for q in range(4):
+        for q in range(QUADRANTS):
             load_scale_rows(w1s, w1t_scales[:, 0].rearrange("e b k -> b e k"), q)
         nc.sync.dma_start(pos1_t[:], pos1)
         nc.sync.dma_start(pos2_t[:], pos2)
@@ -101,10 +105,10 @@ def tile_moe_sdb_relu_kernel(
                     nc.scalar.copy(dc[t][:, cols], acc[:])
 
         def weave_out(x):
-            return x[:].rearrange("p (c i) t -> p c t i", i=4)
+            return x[:].rearrange("p (c i) t -> p c t i", i=RUN)
 
         def weave_in(x):
-            return x[:].rearrange("p t (c i) -> p c t i", i=4)
+            return x[:].rearrange("p t (c i) -> p c t i", i=RUN)
 
         woven = []
         active = []
@@ -113,11 +117,14 @@ def tile_moe_sdb_relu_kernel(
             last = hi == S
             picked = keep.tile([P, PACK, width], F32, name=f"picked{g}")
             if last:
-                spread = gates[g][:].unsqueeze(1).to_broadcast([P, PACK, width])
-                nc.vector.scalar_tensor_tensor(saved[g][:], saved[g][:], 0.0, spread, ALU.is_gt, ALU.mult)
+                spread = gates[g][:].unsqueeze(1).to_broadcast([P, PACK // 2, width])
+                for t in (0, PACK // 2):
+                    part = saved[g][:, t : t + PACK // 2, :]
+                    nc.vector.scalar_tensor_tensor(part, part, 0.0, spread, ALU.is_gt, ALU.mult)
+            entries = offs_t[:, lo // LIST_ROWS : hi // LIST_ROWS]
             for t in range(PACK):
                 factor = saved[g][:, t, :] if last else gates[g][:]
-                nc.vector.tensor_tensor(picked[:, t, :], dc[t][:].indirect(offs_t[:, lo // 16 : hi // 16]), factor, ALU.mult)
+                nc.vector.tensor_tensor(picked[:, t, :], dc[t][:].indirect(entries), factor, ALU.mult)
             if not last:
                 active.append(keep.tile([P, width, PACK], BF16, name=f"active{g}"))
                 nc.scalar.activation(weave_out(active[g]), weave_in(saved[g]), ACT.Sign)
@@ -129,31 +136,21 @@ def tile_moe_sdb_relu_kernel(
         codes = keep.tile([P, S], I32, name="codes", align_bytes=64)
         scales = keep.tile([P, S], U8, name="scales", align_bytes=64)
 
-        def expert_product(e, b, target):
-            cols = slice(e * C, (e + 1) * C)
-            acc = psum.tile([P, BANK], F32, name="product", tag="acc" if b else "first")
-            nc.tensor.matmul_mx(
-                out=acc[:],
-                lhsT=w1[:, e, 2 * b * P : 2 * (b + 1) * P].bitcast(E2M1),
-                lhsT_scale=w1s[:, e, b * P : (b + 1) * P],
-                rhs=codes[:, cols].bitcast(E5M2),
-                rhs_scale=scales[:, cols],
-                start=True,
-                stop=True,
-            )
-            if (e, b) == (E - 1, 0):
-                nc.vector.tensor_copy(target[:, cols], acc[:])
-            else:
-                nc.scalar.copy(target[:, cols], acc[:])
-
         for g, (lo, hi) in enumerate(GROUPS):
             if hi < S:
                 if g == 1:
                     nc.vector.tensor_scalar(active[g][:], active[g][:], 0.0, None, ALU.max)
-                nc.vector.tensor_tensor(woven[g][:], woven[g][:], active[g][:], ALU.mult)
-            nc.vector.quantize_mx(
-                out=codes[:, lo:hi].bitcast(E5M2), scales=scales[:, lo:hi], in_=woven[g][:].rearrange("p c t -> p (c t)")
-            )
+                parts = [slice(0, (hi - lo) // 2), slice((hi - lo) // 2, hi - lo)]
+                for part in parts:
+                    nc.vector.tensor_tensor(woven[g][:, part], woven[g][:, part], active[g][:, part], ALU.mult)
+            else:
+                parts = [slice(0, hi - lo)]
+            for part in parts:
+                cols = slice(lo + part.start, lo + part.stop)
+                nc.vector.quantize_mx(
+                    out=codes[:, cols].bitcast(E5M2), scales=scales[:, cols], in_=woven[g][:, part].rearrange("p c t -> p (c t)")
+                )
+
         dx = [
             keep.tile([P, S], F32, name="dx0", tag="picked2"),
             keep.tile([P, S], F32, name="dx1", tag="woven2", align_bytes=64),
@@ -162,13 +159,29 @@ def tile_moe_sdb_relu_kernel(
         ]
         for b in range(K // P):
             for e in range(E):
-                expert_product(e, b, dx[b])
+                cols = slice(e * C, (e + 1) * C)
+                product = psum.tile([P, BANK], F32, name="product", tag="acc" if b else "first")
+                nc.tensor.matmul_mx(
+                    out=product[:],
+                    lhsT=w1[:, e, 2 * b * P : 2 * (b + 1) * P].bitcast(E2M1),
+                    lhsT_scale=w1s[:, e, b * P : (b + 1) * P],
+                    rhs=codes[:, cols].bitcast(E5M2),
+                    rhs_scale=scales[:, cols],
+                    start=True,
+                    stop=True,
+                )
+                if (e, b) == (E - 1, 0):
+                    nc.vector.tensor_copy(dx[b][:, cols], product[:])
+                else:
+                    nc.scalar.copy(dx[b][:, cols], product[:])
 
         for b in range(K // P):
             first = keep.tile([P, T], F32, name=f"first{b}")
-            nc.vector.tensor_copy(first[:], dx[b][:].indirect(pos1_t[:]))
-            cuts = [0, T] if b < K // P - 1 else TAIL_CUTS
+            for lo, hi in ((0, T // 2), (T // 2, T)):
+                nc.vector.tensor_copy(first[:, lo:hi], dx[b][:].indirect(pos1_t[:, lo // LIST_ROWS : hi // LIST_ROWS]))
+            cuts = [0, T // 2, T] if b < K // P - 1 else TAIL_CUTS
             for lo, hi in zip(cuts, cuts[1:]):
-                res = keep.tile([P, hi - lo], F32, name=f"res{b}_{lo}")
-                nc.vector.tensor_tensor(res[:], dx[b][:].indirect(pos2_t[:, lo // 16 : hi // 16]), first[:, lo:hi], ALU.add)
-                nc.sync.dma_start(out[b * P : (b + 1) * P, lo:hi], res[:])
+                total = keep.tile([P, hi - lo], F32, name=f"res{b}_{lo}")
+                second = dx[b][:].indirect(pos2_t[:, lo // LIST_ROWS : hi // LIST_ROWS])
+                nc.vector.tensor_tensor(total[:], second, first[:, lo:hi], ALU.add)
+                nc.sync.dma_start(out[b * P : (b + 1) * P, lo:hi], total[:])

@@ -25,7 +25,7 @@ LIST_ROWS = 16
 RUN = 4
 SPARE = 16
 GROUPS = [(0, 2 * C), (2 * C, 3 * C), (3 * C, S)]
-TAIL_CUTS = [0, 512, 896, T]
+TAIL_CUTS = [0, 512, 832, 960, T]
 
 
 def tile_moe_sdb_relu_kernel(
@@ -50,19 +50,21 @@ def tile_moe_sdb_relu_kernel(
         w1s = keep.tile([P, E, K], U8, name="w1s", align_bytes=64)
         dc = [keep.tile([P, T + SPARE], F32, name=f"dc{t}") for t in range(PACK)]
 
-        nc.gpsimd.memset(w2s_raw[:].bitcast(I32), 0)
+        nc.vector.memset(w2s_raw[:].bitcast(I32), 0)
         for plane in dc:
             nc.vector.memset(plane[:, T:], 0.0)
 
         def load_scale_rows(tile, rows, q):
             nc.sync.dma_start(tile[32 * q : 32 * q + 4].bitcast(I32), rows[4 * q : 4 * q + 4].bitcast(I32))
 
-        for q in range(QUADRANTS):
+        for q in range(QUADRANTS // 2):
             load_scale_rows(dys, dy_scales[0], q)
         nc.sync.dma_start(w2_raw[:], w2t_words[0].rearrange("p n t -> p (n t)").bitcast(I32))
-        nc.sync.dma_start(dy[:], dy_words[0].rearrange("p n t -> p (n t)").bitcast(I32))
         for q in range(QUADRANTS):
             load_scale_rows(w2s_raw, w2t_scales[0], q)
+        nc.sync.dma_start(dy[:], dy_words[0].rearrange("p n t -> p (n t)").bitcast(I32))
+        for q in range(QUADRANTS // 2, QUADRANTS):
+            load_scale_rows(dys, dy_scales[0], q)
         nc.sync.dma_start(offs_t[:], offs)
         gates = []
         saved = []

@@ -76,7 +76,11 @@ def tile_moe_sdb_relu_kernel(
                 nc.sync.dma_start(
                     saved[-1][:, :, start - lo : start - lo + C], a[:, start : start + C].rearrange("(p t) j -> p t j", t=PACK)
                 )
-        nc.sync.dma_start(w1[:].bitcast(I32), w1t_words[:, 0].rearrange("e p k -> p e k").bitcast(I32))
+        w1_words = w1t_words[:, 0].rearrange("e p k -> p e k").bitcast(I32)
+        nc.sync.dma_start(w1[:, : E - 1].bitcast(I32), w1_words[:, : E - 1])
+        nc.sync.dma_start(w1[:, E - 1, 2 * P :].bitcast(I32), w1_words[:, E - 1, P // 2 :])
+        w1_last = keep.tile([P, 2 * P], U8, name="w1_last", align_bytes=64)
+        nc.sync.dma_start(w1_last[:].bitcast(I32), w1_words[:, E - 1, : P // 2])
         for q in range(QUADRANTS):
             load_scale_rows(w1s, w1t_scales[:, 0].rearrange("e b k -> b e k"), q)
         nc.sync.dma_start(pos1_t[:], pos1)
@@ -101,7 +105,7 @@ def tile_moe_sdb_relu_kernel(
                     start=True,
                     stop=True,
                 )
-                if (t, h) == (0, 1):
+                if h == 0 and t < 2:
                     nc.vector.tensor_copy(dc[t][:, cols], acc[:])
                 else:
                     nc.scalar.copy(dc[t][:, cols], acc[:])
@@ -127,11 +131,14 @@ def tile_moe_sdb_relu_kernel(
             for t in range(PACK):
                 factor = saved[g][:, t, :] if last else gates[g][:]
                 nc.vector.tensor_tensor(picked[:, t, :], dc[t][:].indirect(entries), factor, ALU.mult)
-            if not last:
-                active.append(keep.tile([P, width, PACK], BF16, name=f"active{g}"))
-                nc.scalar.activation(weave_out(active[g]), weave_in(saved[g]), ACT.Sign)
-                if g == 0:
-                    nc.scalar.activation(active[g][:], active[g][:], ACT.Relu)
+            if g == 0:
+                for m in range(2):
+                    active.append(keep.tile([P, GROUPS[m][1] - GROUPS[m][0], PACK], BF16, name=f"active{m}"))
+                    nc.scalar.activation(weave_out(active[m]), weave_in(saved[m]), ACT.Sign)
+                    if m == 0:
+                        nc.scalar.activation(active[m][:], active[m][:], ACT.Relu)
+            if g == 1:
+                nc.scalar.activation(active[1][:], active[1][:], ACT.Relu)
             woven.append(keep.tile([P, width, PACK], BF16, name=f"woven{g}", align_bytes=64))
             nc.scalar.copy(weave_out(woven[g]), weave_in(picked))
 
@@ -140,8 +147,6 @@ def tile_moe_sdb_relu_kernel(
 
         for g, (lo, hi) in enumerate(GROUPS):
             if hi < S:
-                if g == 1:
-                    nc.vector.tensor_scalar(active[g][:], active[g][:], 0.0, None, ALU.max)
                 parts = [slice(0, (hi - lo) // 2), slice((hi - lo) // 2, hi - lo)]
                 for part in parts:
                     nc.vector.tensor_tensor(woven[g][:, part], woven[g][:, part], active[g][:, part], ALU.mult)
@@ -155,7 +160,7 @@ def tile_moe_sdb_relu_kernel(
 
         dx = [
             keep.tile([P, S], F32, name="dx0", tag="picked2"),
-            keep.tile([P, S], F32, name="dx1", tag="woven2", align_bytes=64),
+            keep.tile([P, S], F32, name="dx1", tag="w1_last", align_bytes=64),
             keep.tile([P, S], F32, name="dx2", tag="woven1", align_bytes=64),
             keep.tile([P, S], F32, name="dx3"),
         ]
@@ -165,14 +170,14 @@ def tile_moe_sdb_relu_kernel(
                 product = psum.tile([P, BANK], F32, name="product", tag="acc" if b else "first")
                 nc.tensor.matmul_mx(
                     out=product[:],
-                    lhsT=w1[:, e, 2 * b * P : 2 * (b + 1) * P].bitcast(E2M1),
+                    lhsT=(w1_last[:] if (e, b) == (E - 1, 0) else w1[:, e, 2 * b * P : 2 * (b + 1) * P]).bitcast(E2M1),
                     lhsT_scale=w1s[:, e, b * P : (b + 1) * P],
                     rhs=codes[:, cols].bitcast(E5M2),
                     rhs_scale=scales[:, cols],
                     start=True,
                     stop=True,
                 )
-                if (e, b) == (E - 1, 0):
+                if (e, b) == (E - 2, 0):
                     nc.vector.tensor_copy(dx[b][:, cols], product[:])
                 else:
                     nc.scalar.copy(dx[b][:, cols], product[:])

@@ -105,7 +105,7 @@ def tile_moe_sdb_relu_kernel(
                     start=True,
                     stop=True,
                 )
-                if h == 0 and t < 2:
+                if h == 0 and t == 0:
                     nc.vector.tensor_copy(dc[t][:, cols], acc[:])
                 else:
                     nc.scalar.copy(dc[t][:, cols], acc[:])

@@ -1,6 +1,7 @@
 from contextlib import ExitStack
 
 import concourse.mybir as mybir
+from concourse.masks import make_identity
 
 K, T, E, C, H, N = 512, 1024, 4, 512, 512, 512
 S = E * C
@@ -23,8 +24,9 @@ QUADRANTS = 4
 BANK = 512
 LIST_ROWS = 16
 RUN = 4
-SPARE = 16
-GROUPS = [(0, 2 * C), (2 * C, 3 * C), (3 * C, S)]
+TURNED = [(0, 512), (512, 1024), (1024, 1536), (1536, 1792)]
+DIRECT = (1792, S)
+SCALAR_MASKS = [(1, 1), (2, 1)]
 TAIL_CUTS = [0, 512, 832, 960, T]
 
 
@@ -35,6 +37,7 @@ def tile_moe_sdb_relu_kernel(
     with ExitStack() as ctx:
         keep = ctx.enter_context(tc.tile_pool(name="keep", bufs=1))
         psum = ctx.enter_context(tc.psum_pool(name="psum", bufs=4))
+        banks = ctx.enter_context(tc.psum_pool(name="banks", bufs=1))
 
         offs_t = keep.tile([P, S // LIST_ROWS], U16, name="offs_t")
         pos1_t = keep.tile([P, T // LIST_ROWS], U16, name="pos1_t")
@@ -48,11 +51,11 @@ def tile_moe_sdb_relu_kernel(
         dys = keep.tile([P, T], U8, name="dys", align_bytes=64)
         w1 = keep.tile([P, E, 2 * K], U8, name="w1", align_bytes=64)
         w1s = keep.tile([P, E, K], U8, name="w1s", align_bytes=64)
-        dc = [keep.tile([P, T + SPARE], F32, name=f"dc{t}") for t in range(PACK)]
+        dc = [keep.tile([P, T], F32, name=f"dc{t}", align_bytes=64) for t in range(PACK)]
+        identity = keep.tile([P, P], F32, name="identity")
+        make_identity(nc, identity[:])
 
         nc.vector.memset(w2s_raw[:].bitcast(I32), 0)
-        for plane in dc:
-            nc.vector.memset(plane[:, T:], 0.0)
 
         def load_scale_rows(tile, rows, q):
             nc.sync.dma_start(tile[32 * q : 32 * q + 4].bitcast(I32), rows[4 * q : 4 * q + 4].bitcast(I32))
@@ -65,17 +68,22 @@ def tile_moe_sdb_relu_kernel(
         nc.sync.dma_start(dy[:], dy_words[0].rearrange("p n t -> p (n t)").bitcast(I32))
         for q in range(QUADRANTS // 2, QUADRANTS):
             load_scale_rows(dys, dy_scales[0], q)
+        a_planes = a.rearrange("(p t) j -> p t j", t=PACK)
+        groups = TURNED + [DIRECT]
+        saved = [[keep.tile([P, 2, hi - lo], F32, name=f"saved{lo}_{h}") for h in range(2)] for lo, hi in groups]
+        first_planes = [keep.tile([P, TURNED[0][1]], F32, name=f"first_plane{t}") for t in range(2)]
+        nc.sync.dma_start(first_planes[0][:], a_planes[:, 0, : TURNED[0][1]])
         nc.sync.dma_start(offs_t[:], offs)
-        gates = []
-        saved = []
-        for lo, hi in GROUPS:
-            gates.append(keep.tile([P, hi - lo], F32, name=f"gate{lo}"))
-            nc.sync.dma_start(gates[-1][:], gate[:, lo:hi])
-            saved.append(keep.tile([P, PACK, hi - lo], F32, name=f"saved{lo}"))
-            for start in range(lo, hi, C):
-                nc.sync.dma_start(
-                    saved[-1][:, :, start - lo : start - lo + C], a[:, start : start + C].rearrange("(p t) j -> p t j", t=PACK)
-                )
+        nc.sync.dma_start(first_planes[1][:], a_planes[:, 1, : TURNED[0][1]])
+        gate_rows = keep.tile([P, P], F32, name="gate_rows")
+        direct_gate = keep.tile([P, DIRECT[1] - DIRECT[0]], F32, name="direct_gate")
+        for g, (lo, hi) in enumerate(groups):
+            for h in (1, 0):
+                if (g, h) != (0, 0):
+                    nc.sync.dma_start(saved[g][h][:], a_planes[:, 2 * h : 2 * h + 2, lo:hi])
+            if g == 0:
+                nc.sync.dma_start(gate_rows[:], gate[: P * P // S].rearrange("r (c j) -> (r c) j", j=P))
+        nc.sync.dma_start(direct_gate[:], gate[:, DIRECT[0] : DIRECT[1]])
         w1_words = w1t_words[:, 0].rearrange("e p k -> p e k").bitcast(I32)
         nc.sync.dma_start(w1[:, : E - 1].bitcast(I32), w1_words[:, : E - 1])
         nc.sync.dma_start(w1[:, E - 1, 2 * P :].bitcast(I32), w1_words[:, E - 1, P // 2 :])
@@ -110,64 +118,102 @@ def tile_moe_sdb_relu_kernel(
                 else:
                     nc.scalar.copy(dc[t][:, cols], acc[:])
 
-        def weave_out(x):
-            return x[:].rearrange("p (c i) t -> p c t i", i=RUN)
+        gate_bank = banks.tile([P, P], F32, name="gate_bank", tag="bank3")
+        nc.tensor.transpose(gate_bank[:], gate_rows[:], identity[:])
+        slot_gate = keep.tile([P, S // P], F32, name="slot_gate")
+        nc.scalar.copy(slot_gate[:], gate_bank[:, : S // P])
 
-        def weave_in(x):
-            return x[:].rearrange("p t (c i) -> p c t i", i=RUN)
+        ring = [0]
 
-        woven = []
-        active = []
-        for g, (lo, hi) in enumerate(GROUPS):
-            width = hi - lo
-            last = hi == S
-            picked = keep.tile([P, PACK, width], F32, name=f"picked{g}")
-            if last:
-                spread = gates[g][:].unsqueeze(1).to_broadcast([P, PACK // 2, width])
-                for t in (0, PACK // 2):
-                    part = saved[g][:, t : t + PACK // 2, :]
-                    nc.vector.scalar_tensor_tensor(part, part, 0.0, spread, ALU.is_gt, ALU.mult)
+        def next_bank(shape):
+            ring[0] += 1
+            return banks.tile(shape, F32, name="turning", tag=f"bank{ring[0] % 3}")
+
+        def make_mask(g, h):
+            if (g, h) == (0, 0):
+                for plane in first_planes:
+                    nc.vector.tensor_scalar(plane[:], plane[:], 0.0, None, ALU.is_gt)
+            elif (g, h) in SCALAR_MASKS:
+                sign = keep.tile([P, 2, groups[g][1] - groups[g][0]], BF16, name="sign", tag=f"gated{g - 1}_0", align_bytes=64)
+                nc.scalar.activation(sign[:], saved[g][h][:], ACT.Sign)
+                nc.scalar.activation(saved[g][h][:], sign[:], ACT.Relu)
+            else:
+                nc.vector.tensor_scalar(saved[g][h][:], saved[g][h][:], 0.0, None, ALU.is_gt)
+
+        def gather(g):
+            lo, hi = groups[g]
+            picked = keep.tile([P, PACK, hi - lo], F32, name=f"picked{g}", tag=f"picked{g % 2}")
             entries = offs_t[:, lo // LIST_ROWS : hi // LIST_ROWS]
             for t in range(PACK):
-                factor = saved[g][:, t, :] if last else gates[g][:]
+                factor = first_planes[t][:] if g == 0 and t < 2 else saved[g][t // 2][:, t % 2, :]
                 nc.vector.tensor_tensor(picked[:, t, :], dc[t][:].indirect(entries), factor, ALU.mult)
-            if g == 0:
-                for m in range(2):
-                    active.append(keep.tile([P, GROUPS[m][1] - GROUPS[m][0], PACK], BF16, name=f"active{m}"))
-                    nc.scalar.activation(weave_out(active[m]), weave_in(saved[m]), ACT.Sign)
-                    if m == 0:
-                        nc.scalar.activation(active[m][:], active[m][:], ACT.Relu)
-            if g == 1:
-                nc.scalar.activation(active[1][:], active[1][:], ACT.Relu)
-            woven.append(keep.tile([P, width, PACK], BF16, name=f"woven{g}", align_bytes=64))
-            nc.scalar.copy(weave_out(woven[g]), weave_in(picked))
+            return picked
 
-        codes = keep.tile([P, S], I32, name="codes", align_bytes=64)
-        scales = keep.tile([P, S], U8, name="scales", align_bytes=64)
-
-        for g, (lo, hi) in enumerate(GROUPS):
-            if hi < S:
-                parts = [slice(0, (hi - lo) // 2), slice((hi - lo) // 2, hi - lo)]
-                for part in parts:
-                    nc.vector.tensor_tensor(woven[g][:, part], woven[g][:, part], active[g][:, part], ALU.mult)
-            else:
-                parts = [slice(0, hi - lo)]
-            for part in parts:
-                cols = slice(lo + part.start, lo + part.stop)
-                nc.vector.quantize_mx(
-                    out=codes[:, cols].bitcast(E5M2), scales=scales[:, cols], in_=woven[g][:, part].rearrange("p c t -> p (c t)")
+        def turn(g, picked):
+            lo, hi = groups[g]
+            rounded = keep.tile([P, hi - lo, PACK], BF16, name=f"woven{g}", align_bytes=64)
+            words = rounded[:].rearrange("p c t -> p (c t)").bitcast(F32)
+            gated = []
+            for blk in range((hi - lo) // P):
+                bank = next_bank([P, PACK, P])
+                for t in range(PACK):
+                    nc.tensor.transpose(bank[:, t, :], picked[:, t, blk * P : (blk + 1) * P], identity[:])
+                gated.append(keep.tile([P, 2, P, 2], BF16, name=f"gated{g}_{blk}", align_bytes=64))
+                col = lo // P + blk
+                nc.scalar.activation(
+                    gated[blk][:], bank[:].rearrange("s (u e) p -> s u p e", e=2), ACT.Copy, scale=slot_gate[:, col : col + 1]
                 )
+            for pair in range(len(gated) // 2):
+                bank = next_bank([P, 2, 2, P])
+                for j in range(2):
+                    pairs = gated[2 * pair + j][:].rearrange("s u p e -> s (u p e)").bitcast(F32)
+                    for u in range(2):
+                        nc.tensor.transpose(bank[:, j, u, :], pairs[:, u * P : (u + 1) * P], identity[:])
+                nc.scalar.copy(
+                    words[:, pair * BANK : (pair + 1) * BANK].rearrange("p (j s u) -> p j s u", j=2, u=2),
+                    bank[:].rearrange("p j u s -> p j s u"),
+                )
+            return rounded
+
+        woven = []
+        for h in range(2):
+            make_mask(0, h)
+        for g in range(len(TURNED)):
+            picked = gather(g)
+            if g + 1 < len(TURNED):
+                for h in range(2):
+                    make_mask(g + 1, h)
+            woven.append(turn(g, picked))
+        width = DIRECT[1] - DIRECT[0]
+        for h in range(2):
+            part = saved[-1][h][:]
+            nc.vector.scalar_tensor_tensor(part, part, 0.0, direct_gate[:].unsqueeze(1).to_broadcast([P, 2, width]), ALU.is_gt, ALU.mult)
+        picked = gather(len(TURNED))
+        woven.append(keep.tile([P, width, PACK], BF16, name="woven_direct", tag=f"gated{len(TURNED) - 1}_1", align_bytes=64))
+        nc.scalar.copy(
+            woven[-1][:].rearrange("p (c i) t -> p c t i", i=RUN), picked[:].rearrange("p t (c i) -> p c t i", i=RUN)
+        )
+
+        codes = keep.tile([P, S], I32, name="codes", tag=f"gated{len(TURNED) - 1}_0", align_bytes=64)
+        scales = keep.tile([P, S], U8, name="scales", align_bytes=64)
+        for g, (lo, hi) in enumerate(groups):
+            nc.vector.quantize_mx(
+                out=codes[:, lo:hi].bitcast(E5M2), scales=scales[:, lo:hi], in_=woven[g][:].rearrange("p c t -> p (c t)")
+            )
 
         dx = [
-            keep.tile([P, S], F32, name="dx0", tag="picked2"),
+            keep.tile([P, S], F32, name="dx0", tag=f"picked{len(TURNED) % 2}"),
             keep.tile([P, S], F32, name="dx1", tag="w1_last", align_bytes=64),
-            keep.tile([P, S], F32, name="dx2", tag="woven1", align_bytes=64),
+            keep.tile([P, S], F32, name="dx2", tag=f"woven{len(TURNED) - 1}", align_bytes=64),
             keep.tile([P, S], F32, name="dx3"),
         ]
         for b in range(K // P):
             for e in range(E):
                 cols = slice(e * C, (e + 1) * C)
-                product = psum.tile([P, BANK], F32, name="product", tag="acc" if b else "first")
+                if b:
+                    product = psum.tile([P, BANK], F32, name="product", tag="acc")
+                else:
+                    product = banks.tile([P, BANK], F32, name="product", tag=f"bank{e}")
                 nc.tensor.matmul_mx(
                     out=product[:],
                     lhsT=(w1_last[:] if (e, b) == (E - 1, 0) else w1[:, e, 2 * b * P : 2 * (b + 1) * P]).bitcast(E2M1),

@@ -24,9 +24,11 @@ QUADRANTS = 4
 BANK = 512
 LIST_ROWS = 16
 RUN = 4
-TURNED = [(0, 512), (512, 1024), (1024, 1536), (1536, 1792)]
-DIRECT = (1792, S)
-SCALAR_MASKS = [(1, 1), (2, 1)]
+HELD = 4
+TURNED = (0, 2 * C)
+MASKED = (TURNED[1], 3 * C + C // 2)
+FOLDED = (MASKED[1], S)
+RUNS = [[(0, 1), (1, 2), (2, PACK)], [(0, 2), (2, PACK)]]
 TAIL_CUTS = [0, 512, 832, 960, T]
 
 
@@ -36,7 +38,7 @@ def tile_moe_sdb_relu_kernel(
     nc = tc.nc
     with ExitStack() as ctx:
         keep = ctx.enter_context(tc.tile_pool(name="keep", bufs=1))
-        psum = ctx.enter_context(tc.psum_pool(name="psum", bufs=4))
+        psum = ctx.enter_context(tc.psum_pool(name="psum", bufs=HELD))
         banks = ctx.enter_context(tc.psum_pool(name="banks", bufs=1))
 
         offs_t = keep.tile([P, S // LIST_ROWS], U16, name="offs_t")
@@ -51,7 +53,7 @@ def tile_moe_sdb_relu_kernel(
         dys = keep.tile([P, T], U8, name="dys", align_bytes=64)
         w1 = keep.tile([P, E, 2 * K], U8, name="w1", align_bytes=64)
         w1s = keep.tile([P, E, K], U8, name="w1s", align_bytes=64)
-        dc = [keep.tile([P, T], F32, name=f"dc{t}", align_bytes=64) for t in range(PACK)]
+        dc = [keep.tile([P, T], F32, name=f"dc{t}") for t in range(PACK)]
         identity = keep.tile([P, P], F32, name="identity")
         make_identity(nc, identity[:])
 
@@ -69,24 +71,37 @@ def tile_moe_sdb_relu_kernel(
         for q in range(QUADRANTS // 2, QUADRANTS):
             load_scale_rows(dys, dy_scales[0], q)
         a_planes = a.rearrange("(p t) j -> p t j", t=PACK)
-        groups = TURNED + [DIRECT]
-        saved = [[keep.tile([P, 2, hi - lo], F32, name=f"saved{lo}_{h}") for h in range(2)] for lo, hi in groups]
-        first_planes = [keep.tile([P, TURNED[0][1]], F32, name=f"first_plane{t}") for t in range(2)]
-        nc.sync.dma_start(first_planes[0][:], a_planes[:, 0, : TURNED[0][1]])
-        nc.sync.dma_start(offs_t[:], offs)
-        nc.sync.dma_start(first_planes[1][:], a_planes[:, 1, : TURNED[0][1]])
         gate_rows = keep.tile([P, P], F32, name="gate_rows")
-        direct_gate = keep.tile([P, DIRECT[1] - DIRECT[0]], F32, name="direct_gate")
-        for g, (lo, hi) in enumerate(groups):
-            for h in (1, 0):
-                if (g, h) != (0, 0):
-                    nc.sync.dma_start(saved[g][h][:], a_planes[:, 2 * h : 2 * h + 2, lo:hi])
-            if g == 0:
-                nc.sync.dma_start(gate_rows[:], gate[: P * P // S].rearrange("r (c j) -> (r c) j", j=P))
-        nc.sync.dma_start(direct_gate[:], gate[:, DIRECT[0] : DIRECT[1]])
+        turned_mask = [
+            [keep.tile([P, t1 - t0, C], F32, name=f"turned_mask{e}_{t0}") for t0, t1 in runs] for e, runs in enumerate(RUNS)
+        ]
+        middle = MASKED[0] + C
+        pieces = [(MASKED[0], middle), (middle, MASKED[1]), FOLDED]
+        saved = [keep.tile([P, PACK, hi - lo], F32, name=f"saved{lo}", align_bytes=64) for lo, hi in pieces]
+        masked_gate = keep.tile([P, MASKED[1] - MASKED[0]], F32, name="masked_gate")
+        folded_gate = keep.tile([P, S - FOLDED[0]], F32, name="folded_gate")
+
+        def load_run(e, r):
+            t0, t1 = RUNS[e][r]
+            nc.sync.dma_start(turned_mask[e][r][:], a_planes[:, t0:t1, e * C : (e + 1) * C])
+
+        load_run(0, 0)
+        nc.sync.dma_start(offs_t[:], offs)
+        load_run(0, 1)
+        load_run(0, 2)
+        nc.sync.dma_start(gate_rows[:], gate[: P * P // S].rearrange("r (c j) -> (r c) j", j=P))
+        load_run(1, 0)
+        nc.sync.dma_start(saved[0][:], a_planes[:, :, MASKED[0] : middle])
+        load_run(1, 1)
+        nc.sync.dma_start(saved[1][:], a_planes[:, :, middle : MASKED[1]])
+        nc.sync.dma_start(masked_gate[:], gate[:, MASKED[0] : MASKED[1]])
+        nc.sync.dma_start(folded_gate[:], gate[:, FOLDED[0] :])
+        nc.sync.dma_start(saved[2][:], a_planes[:, :, FOLDED[0] :])
         w1_words = w1t_words[:, 0].rearrange("e p k -> p e k").bitcast(I32)
         nc.sync.dma_start(w1[:, : E - 1].bitcast(I32), w1_words[:, : E - 1])
-        nc.sync.dma_start(w1[:, E - 1, 2 * P :].bitcast(I32), w1_words[:, E - 1, P // 2 :])
+        nc.sync.dma_start(w1[:, E - 1, 2 * P : 6 * P].bitcast(I32), w1_words[:, E - 1, P // 2 : 3 * P // 2])
+        w1_end = keep.tile([P, 2 * P], U8, name="w1_end", align_bytes=64)
+        nc.sync.dma_start(w1_end[:].bitcast(I32), w1_words[:, E - 1, 3 * P // 2 :])
         w1_last = keep.tile([P, 2 * P], U8, name="w1_last", align_bytes=64)
         nc.sync.dma_start(w1_last[:].bitcast(I32), w1_words[:, E - 1, : P // 2])
         for q in range(QUADRANTS):
@@ -118,95 +133,97 @@ def tile_moe_sdb_relu_kernel(
                 else:
                     nc.scalar.copy(dc[t][:, cols], acc[:])
 
-        gate_bank = banks.tile([P, P], F32, name="gate_bank", tag="bank3")
+        gate_bank = banks.tile([P, P], F32, name="gate_bank", tag=f"bank{HELD - 1}")
         nc.tensor.transpose(gate_bank[:], gate_rows[:], identity[:])
-        slot_gate = keep.tile([P, S // P], F32, name="slot_gate")
-        nc.scalar.copy(slot_gate[:], gate_bank[:, : S // P])
 
-        ring = [0]
+        def weave_out(x):
+            return x.rearrange("p (c i) t -> p c t i", i=RUN)
 
-        def next_bank(shape):
-            ring[0] += 1
-            return banks.tile(shape, F32, name="turning", tag=f"bank{ring[0] % 3}")
+        def weave_in(x):
+            return x.rearrange("p t (c i) -> p c t i", i=RUN)
 
-        def make_mask(g, h):
-            if (g, h) == (0, 0):
-                for plane in first_planes:
-                    nc.vector.tensor_scalar(plane[:], plane[:], 0.0, None, ALU.is_gt)
-            elif (g, h) in SCALAR_MASKS:
-                sign = keep.tile([P, 2, groups[g][1] - groups[g][0]], BF16, name="sign", tag=f"gated{g - 1}_0", align_bytes=64)
-                nc.scalar.activation(sign[:], saved[g][h][:], ACT.Sign)
-                nc.scalar.activation(saved[g][h][:], sign[:], ACT.Relu)
-            else:
-                nc.vector.tensor_scalar(saved[g][h][:], saved[g][h][:], 0.0, None, ALU.is_gt)
-
-        def gather(g):
-            lo, hi = groups[g]
-            picked = keep.tile([P, PACK, hi - lo], F32, name=f"picked{g}", tag=f"picked{g % 2}")
+        def gather(lo, hi, factors):
+            picked = keep.tile([P, PACK, hi - lo], F32, name=f"picked{lo}")
             entries = offs_t[:, lo // LIST_ROWS : hi // LIST_ROWS]
             for t in range(PACK):
-                factor = first_planes[t][:] if g == 0 and t < 2 else saved[g][t // 2][:, t % 2, :]
-                nc.vector.tensor_tensor(picked[:, t, :], dc[t][:].indirect(entries), factor, ALU.mult)
+                nc.vector.tensor_tensor(picked[:, t, :], dc[t][:].indirect(entries), factors[t], ALU.mult)
             return picked
 
-        def turn(g, picked):
-            lo, hi = groups[g]
-            rounded = keep.tile([P, hi - lo, PACK], BF16, name=f"woven{g}", align_bytes=64)
-            words = rounded[:].rearrange("p c t -> p (c t)").bitcast(F32)
-            gated = []
-            for blk in range((hi - lo) // P):
-                bank = next_bank([P, PACK, P])
-                for t in range(PACK):
-                    nc.tensor.transpose(bank[:, t, :], picked[:, t, blk * P : (blk + 1) * P], identity[:])
-                gated.append(keep.tile([P, 2, P, 2], BF16, name=f"gated{g}_{blk}", align_bytes=64))
-                col = lo // P + blk
-                nc.scalar.activation(
-                    gated[blk][:], bank[:].rearrange("s (u e) p -> s u p e", e=2), ACT.Copy, scale=slot_gate[:, col : col + 1]
-                )
-            for pair in range(len(gated) // 2):
-                bank = next_bank([P, 2, 2, P])
-                for j in range(2):
-                    pairs = gated[2 * pair + j][:].rearrange("s u p e -> s (u p e)").bitcast(F32)
-                    for u in range(2):
-                        nc.tensor.transpose(bank[:, j, u, :], pairs[:, u * P : (u + 1) * P], identity[:])
-                nc.scalar.copy(
-                    words[:, pair * BANK : (pair + 1) * BANK].rearrange("p (j s u) -> p j s u", j=2, u=2),
-                    bank[:].rearrange("p j u s -> p j s u"),
-                )
-            return rounded
+        for parts in turned_mask:
+            for part in parts:
+                nc.vector.tensor_scalar(part[:], part[:], 0.0, None, ALU.is_gt)
+        picked_turned = []
+        for e, runs in enumerate(RUNS):
+            planes = [turned_mask[e][r][:, t - t0, :] for r, (t0, t1) in enumerate(runs) for t in range(t0, t1)]
+            picked_turned.append(gather(e * C, (e + 1) * C, planes))
+        picked_masked = gather(*MASKED, [masked_gate[:]] * PACK)
+        for t in (0, PACK // 2):
+            part = saved[2][:, t : t + PACK // 2, :]
+            spread = folded_gate[:].unsqueeze(1).to_broadcast([P, PACK // 2, S - FOLDED[0]])
+            nc.vector.scalar_tensor_tensor(part, part, 0.0, spread, ALU.is_gt, ALU.mult)
+        picked_folded = gather(*FOLDED, [saved[2][:, t, :] for t in range(PACK)])
 
-        woven = []
-        for h in range(2):
-            make_mask(0, h)
-        for g in range(len(TURNED)):
-            picked = gather(g)
-            if g + 1 < len(TURNED):
-                for h in range(2):
-                    make_mask(g + 1, h)
-            woven.append(turn(g, picked))
-        width = DIRECT[1] - DIRECT[0]
-        for h in range(2):
-            part = saved[-1][h][:]
-            nc.vector.scalar_tensor_tensor(part, part, 0.0, direct_gate[:].unsqueeze(1).to_broadcast([P, 2, width]), ALU.is_gt, ALU.mult)
-        picked = gather(len(TURNED))
-        woven.append(keep.tile([P, width, PACK], BF16, name="woven_direct", tag=f"gated{len(TURNED) - 1}_1", align_bytes=64))
-        nc.scalar.copy(
-            woven[-1][:].rearrange("p (c i) t -> p c t i", i=RUN), picked[:].rearrange("p t (c i) -> p c t i", i=RUN)
-        )
+        active = keep.tile([P, MASKED[1] - MASKED[0], PACK], BF16, name="active")
+        masked_parts = [slice(lo - MASKED[0], hi - MASKED[0]) for lo, hi in pieces[:2]]
+        signs = [keep.tile([P, hi - lo, PACK], BF16, name=f"sign{lo}", align_bytes=64) for lo, hi in pieces[:2]]
+        for g in range(len(signs)):
+            nc.scalar.activation(weave_out(signs[g][:]), weave_in(saved[g][:]), ACT.Sign)
+        for g, part in enumerate(masked_parts):
+            nc.scalar.activation(active[:, part], signs[g][:], ACT.Relu)
 
-        codes = keep.tile([P, S], I32, name="codes", tag=f"gated{len(TURNED) - 1}_0", align_bytes=64)
-        scales = keep.tile([P, S], U8, name="scales", align_bytes=64)
-        for g, (lo, hi) in enumerate(groups):
-            nc.vector.quantize_mx(
-                out=codes[:, lo:hi].bitcast(E5M2), scales=scales[:, lo:hi], in_=woven[g][:].rearrange("p c t -> p (c t)")
+        blocks = TURNED[1] // P
+        slot_gate = keep.tile([P, blocks], F32, name="slot_gate", tag=f"sign{middle}", align_bytes=64)
+        nc.scalar.copy(slot_gate[:], gate_bank[:, :blocks])
+        turned_words = [keep.tile([P, 2 * C], F32, name=f"turned_words{e}", align_bytes=64) for e in range(len(RUNS))]
+        per_expert = C // P
+        gated = []
+        for blk in range(blocks):
+            if HELD - 1 <= blk < blocks - 1:
+                bank = psum.tile([P, PACK, P], F32, name="turning", tag="acc")
+            else:
+                bank = banks.tile([P, PACK, P], F32, name="turning", tag=f"bank{min(blk, HELD - 1)}")
+            source = picked_turned[blk // per_expert]
+            for t in range(PACK):
+                nc.tensor.transpose(bank[:, t, :], source[:, t, blk % per_expert * P : (blk % per_expert + 1) * P], identity[:])
+            gated.append(keep.tile([P, 2, P, 2], BF16, name=f"gated{blk}", align_bytes=64))
+            nc.scalar.activation(
+                gated[blk][:], bank[:].rearrange("s (u r) p -> s u p r", r=2), ACT.Copy, scale=slot_gate[:, blk : blk + 1]
+            )
+        for pair in range(blocks // 2):
+            bank = banks.tile([P, 2, 2, P], F32, name="returning", tag=f"bank{pair}")
+            for j in range(2):
+                row_pairs = gated[2 * pair + j][:].rearrange("s u p r -> s (u p r)").bitcast(F32)
+                for u in range(2):
+                    nc.tensor.transpose(bank[:, j, u, :], row_pairs[:, u * P : (u + 1) * P], identity[:])
+            nc.scalar.copy(
+                turned_words[pair // 2][:, pair % 2 * BANK : (pair % 2 + 1) * BANK].rearrange("p (j s u) -> p j s u", j=2, u=2),
+                bank[:].rearrange("p j u s -> p j s u"),
             )
 
+        woven_rest = keep.tile([P, S - MASKED[0], PACK], BF16, name="woven_rest", tag=f"gated{len(gated) - 1}", align_bytes=64)
+        nc.scalar.copy(weave_out(woven_rest[:, : FOLDED[0] - MASKED[0]]), weave_in(picked_masked[:]))
+        nc.scalar.copy(weave_out(woven_rest[:, FOLDED[0] - MASKED[0] :]), weave_in(picked_folded[:]))
+
+        codes = keep.tile([P, S], I32, name="codes", tag=f"gated{len(gated) - 2}", align_bytes=64)
+        scales = keep.tile([P, S], U8, name="scales", align_bytes=64)
+
+        def quantise(lo, hi, values):
+            nc.vector.quantize_mx(out=codes[:, lo:hi].bitcast(E5M2), scales=scales[:, lo:hi], in_=values)
+
+        for e, words in enumerate(turned_words):
+            quantise(e * C, (e + 1) * C, words[:].bitcast(BF16))
+        for part in masked_parts:
+            nc.vector.tensor_tensor(woven_rest[:, part], woven_rest[:, part], active[:, part], ALU.mult)
+        for lo in range(MASKED[0], S, C):
+            quantise(lo, lo + C, woven_rest[:, lo - MASKED[0] : lo + C - MASKED[0]].rearrange("p c t -> p (c t)"))
+
         dx = [
-            keep.tile([P, S], F32, name="dx0", tag=f"picked{len(TURNED) % 2}"),
+            keep.tile([P, S], F32, name="dx0", tag=f"picked{FOLDED[0]}"),
             keep.tile([P, S], F32, name="dx1", tag="w1_last", align_bytes=64),
-            keep.tile([P, S], F32, name="dx2", tag=f"woven{len(TURNED) - 1}", align_bytes=64),
+            keep.tile([P, S], F32, name="dx2", tag="active"),
             keep.tile([P, S], F32, name="dx3"),
         ]
+        apart = {(E - 1, 0): w1_last[:], (E - 1, K // P - 1): w1_end[:]}
         for b in range(K // P):
             for e in range(E):
                 cols = slice(e * C, (e + 1) * C)
@@ -216,7 +233,7 @@ def tile_moe_sdb_relu_kernel(
                     product = banks.tile([P, BANK], F32, name="product", tag=f"bank{e}")
                 nc.tensor.matmul_mx(
                     out=product[:],
-                    lhsT=(w1_last[:] if (e, b) == (E - 1, 0) else w1[:, e, 2 * b * P : 2 * (b + 1) * P]).bitcast(E2M1),
+                    lhsT=apart.get((e, b), w1[:, e, 2 * b * P : 2 * (b + 1) * P]).bitcast(E2M1),
                     lhsT_scale=w1s[:, e, b * P : (b + 1) * P],
                     rhs=codes[:, cols].bitcast(E5M2),
                     rhs_scale=scales[:, cols],
@@ -228,13 +245,25 @@ def tile_moe_sdb_relu_kernel(
                 else:
                     nc.scalar.copy(dx[b][:, cols], product[:])
 
-        for b in range(K // P):
-            first = keep.tile([P, T], F32, name=f"first{b}")
-            for lo, hi in ((0, T // 2), (T // 2, T)):
-                nc.vector.tensor_copy(first[:, lo:hi], dx[b][:].indirect(pos1_t[:, lo // LIST_ROWS : hi // LIST_ROWS]))
-            cuts = [0, T // 2, T] if b < K // P - 1 else TAIL_CUTS
+        first = [keep.tile([P, T], F32, name=f"first{b}") for b in range(K // P)]
+
+        def fetch_first(b, cuts):
             for lo, hi in zip(cuts, cuts[1:]):
-                total = keep.tile([P, hi - lo], F32, name=f"res{b}_{lo}")
+                nc.vector.tensor_copy(first[b][:, lo:hi], dx[b][:].indirect(pos1_t[:, lo // LIST_ROWS : hi // LIST_ROWS]))
+
+        def add_second(b, cuts, tag=None):
+            for lo, hi in zip(cuts, cuts[1:]):
+                total = keep.tile([P, hi - lo], F32, name=f"res{b}_{lo}", tag=tag or f"res{b}_{lo}", align_bytes=64)
                 second = dx[b][:].indirect(pos2_t[:, lo // LIST_ROWS : hi // LIST_ROWS])
-                nc.vector.tensor_tensor(total[:], second, first[:, lo:hi], ALU.add)
+                nc.vector.tensor_tensor(total[:], second, first[b][:, lo:hi], ALU.add)
                 nc.sync.dma_start(out[b * P : (b + 1) * P, lo:hi], total[:])
+
+        token_halves = [0, T // 2, T]
+        fetch_first(0, token_halves)
+        add_second(0, token_halves)
+        fetch_first(1, [0, T])
+        fetch_first(2, [0, T])
+        add_second(1, [0, T], "w1_end")
+        add_second(2, [0, T])
+        fetch_first(3, token_halves)
+        add_second(3, TAIL_CUTS)

@@ -24,12 +24,12 @@ QUADRANTS = 4
 BANK = 512
 LIST_ROWS = 16
 RUN = 4
-HELD = 4
-TURNED = (0, 2 * C)
-MASKED = (TURNED[1], 3 * C + C // 2)
-FOLDED = (MASKED[1], S)
-RUNS = [[(0, 1), (1, 2), (2, PACK)], [(0, 2), (2, PACK)]]
+
+GROUPS = [5,5,3,2]
+BLOCKS = sum(GROUPS)
+DIRECT = BLOCKS * P
 TAIL_CUTS = [0, 512, 832, 960, T]
+BANK_BYTES = 2048
 
 
 def tile_moe_sdb_relu_kernel(
@@ -38,8 +38,13 @@ def tile_moe_sdb_relu_kernel(
     nc = tc.nc
     with ExitStack() as ctx:
         keep = ctx.enter_context(tc.tile_pool(name="keep", bufs=1))
-        psum = ctx.enter_context(tc.psum_pool(name="psum", bufs=HELD))
-        banks = ctx.enter_context(tc.psum_pool(name="banks", bufs=1))
+        psum = ctx.enter_context(tc.psum_pool(name="psum", bufs=1))
+
+        def banks(name, start, shape):
+            return psum.tile(shape, F32, name=name, offset=start * BANK_BYTES)
+
+        pair_at = [4, 0, 2]
+        single_at = [7, 5]
 
         offs_t = keep.tile([P, S // LIST_ROWS], U16, name="offs_t")
         pos1_t = keep.tile([P, T // LIST_ROWS], U16, name="pos1_t")
@@ -72,31 +77,24 @@ def tile_moe_sdb_relu_kernel(
             load_scale_rows(dys, dy_scales[0], q)
         a_planes = a.rearrange("(p t) j -> p t j", t=PACK)
         gate_rows = keep.tile([P, P], F32, name="gate_rows")
-        turned_mask = [
-            [keep.tile([P, t1 - t0, C], F32, name=f"turned_mask{e}_{t0}") for t0, t1 in runs] for e, runs in enumerate(RUNS)
+        edges = [P * sum(GROUPS[:g]) for g in range(len(GROUPS) + 1)]
+
+        pieces = [
+            (0, 640, 0, 1, False), (0, 640, 1, 2, False), (0, 640, 2, 4, False),
+            (640, 1280, 1, 2, True), (640, 1280, 2, 4, True), (640, 1280, 0, 1, False),
+            (1280, 1920, 0, 2, False), (1280, 1920, 2, 4, False),
         ]
-        middle = MASKED[0] + C
-        pieces = [(MASKED[0], middle), (middle, MASKED[1]), FOLDED]
-        saved = [keep.tile([P, PACK, hi - lo], F32, name=f"saved{lo}", align_bytes=64) for lo, hi in pieces]
-        masked_gate = keep.tile([P, MASKED[1] - MASKED[0]], F32, name="masked_gate")
-        folded_gate = keep.tile([P, S - FOLDED[0]], F32, name="folded_gate")
-
-        def load_run(e, r):
-            t0, t1 = RUNS[e][r]
-            nc.sync.dma_start(turned_mask[e][r][:], a_planes[:, t0:t1, e * C : (e + 1) * C])
-
-        load_run(0, 0)
-        nc.sync.dma_start(offs_t[:], offs)
-        load_run(0, 1)
-        load_run(0, 2)
-        nc.sync.dma_start(gate_rows[:], gate[: P * P // S].rearrange("r (c j) -> (r c) j", j=P))
-        load_run(1, 0)
-        nc.sync.dma_start(saved[0][:], a_planes[:, :, MASKED[0] : middle])
-        load_run(1, 1)
-        nc.sync.dma_start(saved[1][:], a_planes[:, :, middle : MASKED[1]])
-        nc.sync.dma_start(masked_gate[:], gate[:, MASKED[0] : MASKED[1]])
-        nc.sync.dma_start(folded_gate[:], gate[:, FOLDED[0] :])
-        nc.sync.dma_start(saved[2][:], a_planes[:, :, FOLDED[0] :])
+        saved = [keep.tile([P, t1 - t0, hi - lo], F32, name=f"saved{lo}_{t0}", align_bytes=64) for lo, hi, t0, t1, by_scalar in pieces]
+        for n, (lo, hi, t0, t1, by_scalar) in enumerate(pieces):
+            nc.sync.dma_start(saved[n][:], a_planes[:, t0:t1, lo:hi])
+            if n == 0:
+                nc.sync.dma_start(offs_t[:], offs)
+            if n == 2:
+                nc.sync.dma_start(gate_rows[:], gate[: P * P // S].rearrange("r (c j) -> (r c) j", j=P))
+        folded = keep.tile([P, PACK, S - DIRECT], F32, name="folded")
+        folded_gate = keep.tile([P, S - DIRECT], F32, name="folded_gate")
+        nc.sync.dma_start(folded_gate[:], gate[:, DIRECT:])
+        nc.sync.dma_start(folded[:], a_planes[:, :, DIRECT:])
         w1_words = w1t_words[:, 0].rearrange("e p k -> p e k").bitcast(I32)
         nc.sync.dma_start(w1[:, : E - 1].bitcast(I32), w1_words[:, : E - 1])
         nc.sync.dma_start(w1[:, E - 1, 2 * P : 6 * P].bitcast(I32), w1_words[:, E - 1, P // 2 : 3 * P // 2])
@@ -118,7 +116,7 @@ def tile_moe_sdb_relu_kernel(
         for t in range(PACK):
             for h in range(T // BANK):
                 cols = slice(h * BANK, (h + 1) * BANK)
-                acc = psum.tile([P, BANK], F32, name="acc")
+                acc = banks(f"acc{t}_{h}", pair_at[t % 3] + h, [P, BANK])
                 nc.tensor.matmul_mx(
                     out=acc[:],
                     lhsT=w2[:, t * P : (t + 1) * P].bitcast(E4M3),
@@ -133,14 +131,23 @@ def tile_moe_sdb_relu_kernel(
                 else:
                     nc.scalar.copy(dc[t][:, cols], acc[:])
 
-        gate_bank = banks.tile([P, P], F32, name="gate_bank", tag=f"bank{HELD - 1}")
+        gate_bank = banks("gate_bank", 6, [P, P])
         nc.tensor.transpose(gate_bank[:], gate_rows[:], identity[:])
 
-        def weave_out(x):
-            return x.rearrange("p (c i) t -> p c t i", i=RUN)
+        mine = [n for n, piece in enumerate(pieces) if piece[4]]
+        signs = {}
+        for n in mine:
+            lo, hi, t0, t1, by_scalar = pieces[n]
+            signs[n] = keep.tile([P, t1 - t0, hi - lo], BF16, name=f"sign{n}", tag="held" if n == mine[-1] else f"sign{n}", align_bytes=64)
+            nc.scalar.activation(signs[n][:], saved[n][:], ACT.Sign)
+        for n in mine:
+            nc.scalar.activation(saved[n][:], signs[n][:], ACT.Relu)
 
-        def weave_in(x):
-            return x.rearrange("p t (c i) -> p c t i", i=RUN)
+        def factor(t, lo, hi):
+            for n, (p_lo, p_hi, t0, t1, by_scalar) in enumerate(pieces):
+                if p_lo <= lo and hi <= p_hi and t0 <= t < t1:
+                    return saved[n][:, t - t0, lo - p_lo : hi - p_lo]
+            raise ValueError("no piece")
 
         def gather(lo, hi, factors):
             picked = keep.tile([P, PACK, hi - lo], F32, name=f"picked{lo}")
@@ -149,88 +156,106 @@ def tile_moe_sdb_relu_kernel(
                 nc.vector.tensor_tensor(picked[:, t, :], dc[t][:].indirect(entries), factors[t], ALU.mult)
             return picked
 
-        for parts in turned_mask:
-            for part in parts:
-                nc.vector.tensor_scalar(part[:], part[:], 0.0, None, ALU.is_gt)
-        picked_turned = []
-        for e, runs in enumerate(RUNS):
-            planes = [turned_mask[e][r][:, t - t0, :] for r, (t0, t1) in enumerate(runs) for t in range(t0, t1)]
-            picked_turned.append(gather(e * C, (e + 1) * C, planes))
-        picked_masked = gather(*MASKED, [masked_gate[:]] * PACK)
+        picked = []
+        for lo, hi in zip(edges, edges[1:]):
+            for n, (p_lo, p_hi, t0, t1, by_scalar) in enumerate(pieces):
+                if p_lo == lo and not by_scalar:
+                    nc.vector.tensor_scalar(saved[n][:], saved[n][:], 0.0, None, ALU.is_gt)
+            picked.append(gather(lo, hi, [factor(t, lo, hi) for t in range(PACK)]))
         for t in (0, PACK // 2):
-            part = saved[2][:, t : t + PACK // 2, :]
-            spread = folded_gate[:].unsqueeze(1).to_broadcast([P, PACK // 2, S - FOLDED[0]])
+            part = folded[:, t : t + PACK // 2, :]
+            spread = folded_gate[:].unsqueeze(1).to_broadcast([P, PACK // 2, S - DIRECT])
             nc.vector.scalar_tensor_tensor(part, part, 0.0, spread, ALU.is_gt, ALU.mult)
-        picked_folded = gather(*FOLDED, [saved[2][:, t, :] for t in range(PACK)])
+        picked_folded = gather(DIRECT, S, [folded[:, t, :] for t in range(PACK)])
 
-        active = keep.tile([P, MASKED[1] - MASKED[0], PACK], BF16, name="active")
-        masked_parts = [slice(lo - MASKED[0], hi - MASKED[0]) for lo, hi in pieces[:2]]
-        signs = [keep.tile([P, hi - lo, PACK], BF16, name=f"sign{lo}", align_bytes=64) for lo, hi in pieces[:2]]
-        for g in range(len(signs)):
-            nc.scalar.activation(weave_out(signs[g][:]), weave_in(saved[g][:]), ACT.Sign)
-        for g, part in enumerate(masked_parts):
-            nc.scalar.activation(active[:, part], signs[g][:], ACT.Relu)
+        slot_gate = keep.tile([P, BLOCKS], F32, name="slot_gate", tag="held", align_bytes=64)
+        nc.scalar.copy(slot_gate[:], gate_bank[:, :BLOCKS])
+        words = keep.tile([P, 2 * DIRECT], F32, name="words", align_bytes=64)
+        pairs = []
+        for lo, hi in zip(edges, edges[1:]):
+            first_block, end_block = lo // P, hi // P
+            pairs.extend(list(range(max(b, first_block), b + 2)) for b in range(first_block - (end_block - first_block) % 2, end_block, 2))
+        gated = {}
 
-        blocks = TURNED[1] // P
-        slot_gate = keep.tile([P, blocks], F32, name="slot_gate", tag=f"sign{middle}", align_bytes=64)
-        nc.scalar.copy(slot_gate[:], gate_bank[:, :blocks])
-        turned_words = [keep.tile([P, 2 * C], F32, name=f"turned_words{e}", align_bytes=64) for e in range(len(RUNS))]
-        per_expert = C // P
-        gated = []
-        for blk in range(blocks):
-            if HELD - 1 <= blk < blocks - 1:
-                bank = psum.tile([P, PACK, P], F32, name="turning", tag="acc")
+        def turn(k):
+            if k < len(pairs) - 1:
+                both = banks(f"turning{k}", 2 * (k % 2), [P, 2, PACK, P])
+                bank = [both[:, j] for j in range(2)]
             else:
-                bank = banks.tile([P, PACK, P], F32, name="turning", tag=f"bank{min(blk, HELD - 1)}")
-            source = picked_turned[blk // per_expert]
-            for t in range(PACK):
-                nc.tensor.transpose(bank[:, t, :], source[:, t, blk % per_expert * P : (blk % per_expert + 1) * P], identity[:])
-            gated.append(keep.tile([P, 2, P, 2], BF16, name=f"gated{blk}", align_bytes=64))
+                bank = [banks(f"turning{k}_{j}", 2 * (k % 2) + j, [P, PACK, P])[:] for j in range(2)]
+            gated[k] = keep.tile([P, len(pairs[k]), 2, P, 2], BF16, name=f"gated{k}", align_bytes=64)
+            for j, blk in enumerate(pairs[k]):
+                g = max(n for n, edge in enumerate(edges) if edge <= blk * P)
+                at = blk * P - edges[g]
+                for t in range(PACK):
+                    nc.tensor.transpose(bank[j][:, t, :], picked[g][:, t, at : at + P], identity[:])
+            return bank
+
+        def apply_gate(k, j, bank):
+            blk = pairs[k][j]
             nc.scalar.activation(
-                gated[blk][:], bank[:].rearrange("s (u r) p -> s u p r", r=2), ACT.Copy, scale=slot_gate[:, blk : blk + 1]
+                gated[k][:, j], bank[j].rearrange("s (u r) p -> s u p r", r=2), ACT.Copy, scale=slot_gate[:, blk : blk + 1]
             )
-        for pair in range(blocks // 2):
-            bank = banks.tile([P, 2, 2, P], F32, name="returning", tag=f"bank{pair}")
-            for j in range(2):
-                row_pairs = gated[2 * pair + j][:].rearrange("s u p r -> s (u p r)").bitcast(F32)
+
+        def turn_back(k):
+            n = len(pairs[k])
+            bank = banks(f"returning{k}", single_at[k % 2], [P, n, 2, P])
+            for j in range(n):
+                row_pairs = gated[k][:, j].rearrange("s u p r -> s (u p r)").bitcast(F32)
                 for u in range(2):
                     nc.tensor.transpose(bank[:, j, u, :], row_pairs[:, u * P : (u + 1) * P], identity[:])
+            return bank
+
+        def copy_back(k, bank):
+            n = len(pairs[k])
+            lo = 2 * P * pairs[k][0]
             nc.scalar.copy(
-                turned_words[pair // 2][:, pair % 2 * BANK : (pair % 2 + 1) * BANK].rearrange("p (j s u) -> p j s u", j=2, u=2),
-                bank[:].rearrange("p j u s -> p j s u"),
+                words[:, lo : lo + 2 * P * n].rearrange("p (j s u) -> p j s u", j=n, u=2), bank[:].rearrange("p j u s -> p j s u")
             )
 
-        woven_rest = keep.tile([P, S - MASKED[0], PACK], BF16, name="woven_rest", tag=f"gated{len(gated) - 1}", align_bytes=64)
-        nc.scalar.copy(weave_out(woven_rest[:, : FOLDED[0] - MASKED[0]]), weave_in(picked_masked[:]))
-        nc.scalar.copy(weave_out(woven_rest[:, FOLDED[0] - MASKED[0] :]), weave_in(picked_folded[:]))
+        ahead = 2
+        turned = {k: turn(k) for k in range(ahead)}
+        back = {}
+        for k in range(len(pairs)):
+            for j in range(len(pairs[k])):
+                apply_gate(k, j, turned[k])
+                if j == len(pairs[k]) - 1 and k > 0:
+                    copy_back(k - 1, back[k - 1])
+            back[k] = turn_back(k)
+            if k + ahead < len(pairs):
+                turned[k + ahead] = turn(k + ahead)
+        woven = keep.tile([P, S - DIRECT, PACK], BF16, name="woven", tag="held", align_bytes=64)
+        nc.scalar.copy(
+            woven[:].rearrange("p (c i) t -> p c t i", i=RUN), picked_folded[:].rearrange("p t (c i) -> p c t i", i=RUN)
+        )
+        copy_back(len(pairs) - 1, back[len(pairs) - 1])
 
-        codes = keep.tile([P, S], I32, name="codes", tag=f"gated{len(gated) - 2}", align_bytes=64)
+        codes = keep.tile([P, S], I32, name="codes", tag=f"gated{len(pairs) - 2}", align_bytes=64)
         scales = keep.tile([P, S], U8, name="scales", align_bytes=64)
 
         def quantise(lo, hi, values):
             nc.vector.quantize_mx(out=codes[:, lo:hi].bitcast(E5M2), scales=scales[:, lo:hi], in_=values)
 
-        for e, words in enumerate(turned_words):
-            quantise(e * C, (e + 1) * C, words[:].bitcast(BF16))
-        for part in masked_parts:
-            nc.vector.tensor_tensor(woven_rest[:, part], woven_rest[:, part], active[:, part], ALU.mult)
-        for lo in range(MASKED[0], S, C):
-            quantise(lo, lo + C, woven_rest[:, lo - MASKED[0] : lo + C - MASKED[0]].rearrange("p c t -> p (c t)"))
+        last = pairs[-1][0] * P
+        cuts = [0, C, 2 * C, 3 * C, last]
+        for lo, hi in zip(cuts, cuts[1:]):
+            quantise(lo, hi, words[:, 2 * lo : 2 * hi].bitcast(BF16))
+        quantise(DIRECT, S, woven[:].rearrange("p c t -> p (c t)"))
+        quantise(last, DIRECT, words[:, 2 * last :].bitcast(BF16))
 
         dx = [
-            keep.tile([P, S], F32, name="dx0", tag=f"picked{FOLDED[0]}"),
+            keep.tile([P, S], F32, name="dx0", tag=f"picked{DIRECT}"),
             keep.tile([P, S], F32, name="dx1", tag="w1_last", align_bytes=64),
-            keep.tile([P, S], F32, name="dx2", tag="active"),
+            keep.tile([P, S], F32, name="dx2"),
             keep.tile([P, S], F32, name="dx3"),
         ]
+        end = len(pairs) - 1
+        product_at = [2 * (end % 2) + 1, single_at[(end - 1) % 2], single_at[end % 2], 2 * (end % 2)]
         apart = {(E - 1, 0): w1_last[:], (E - 1, K // P - 1): w1_end[:]}
         for b in range(K // P):
             for e in range(E):
                 cols = slice(e * C, (e + 1) * C)
-                if b:
-                    product = psum.tile([P, BANK], F32, name="product", tag="acc")
-                else:
-                    product = banks.tile([P, BANK], F32, name="product", tag=f"bank{e}")
+                product = banks(f"product{b}_{e}", product_at[e], [P, BANK])
                 nc.tensor.matmul_mx(
                     out=product[:],
                     lhsT=apart.get((e, b), w1[:, e, 2 * b * P : 2 * (b + 1) * P]).bitcast(E2M1),

@@ -25,9 +25,10 @@ BANK = 512
 LIST_ROWS = 16
 RUN = 4
 
-GROUPS = [5,5,3,2]
-BLOCKS = sum(GROUPS)
-DIRECT = BLOCKS * P
+GROUPS = [(0, 5), (5, 10), (10, 13), (13, 15)]
+ORDER = [(0, 1, 2, 3), (0, 3, 1, 2), (0, 1, 2, 3), (0, 1, 2, 3)]
+FOLD_LO, FOLD_HI = 15 * P, 16 * P
+FOLDED = FOLD_HI - FOLD_LO
 TAIL_CUTS = [0, 512, 832, 960, T]
 BANK_BYTES = 2048
 
@@ -38,6 +39,7 @@ def tile_moe_sdb_relu_kernel(
     nc = tc.nc
     with ExitStack() as ctx:
         keep = ctx.enter_context(tc.tile_pool(name="keep", bufs=1))
+        shared = ctx.enter_context(tc.tile_pool(name="shared", bufs=1))
         psum = ctx.enter_context(tc.psum_pool(name="psum", bufs=1))
 
         def banks(name, start, shape):
@@ -77,24 +79,26 @@ def tile_moe_sdb_relu_kernel(
             load_scale_rows(dys, dy_scales[0], q)
         a_planes = a.rearrange("(p t) j -> p t j", t=PACK)
         gate_rows = keep.tile([P, P], F32, name="gate_rows")
-        edges = [P * sum(GROUPS[:g]) for g in range(len(GROUPS) + 1)]
-
         pieces = [
-            (0, 640, 0, 1, False), (0, 640, 1, 2, False), (0, 640, 2, 4, False),
-            (640, 1280, 1, 2, True), (640, 1280, 2, 4, True), (640, 1280, 0, 1, False),
-            (1280, 1920, 0, 2, False), (1280, 1920, 2, 4, False),
+            (0, 640, 0, 1, "vector", None), (0, 640, 1, 2, "vector", None), (0, 640, 2, 4, "vector", None),
+            (640, 1280, 0, 1, "scalar", None), (640, 1280, 1, 3, "scalar", None), (640, 1280, 3, 4, "vector", None),
+            (1280, 1664, 0, 2, "vector", (1, 2)), (1280, 1664, 2, 4, "vector", (2, 1)), (1664, 1920, 0, 4, "vector", (2, 3)),
         ]
-        saved = [keep.tile([P, t1 - t0, hi - lo], F32, name=f"saved{lo}_{t0}", align_bytes=64) for lo, hi, t0, t1, by_scalar in pieces]
-        for n, (lo, hi, t0, t1, by_scalar) in enumerate(pieces):
+        saved = [
+            keep.tile([P, t1 - t0, hi - lo], F32, name=f"saved{lo}_{t0}", align_bytes=64)
+            for lo, hi, t0, t1, who, heir in pieces
+        ]
+        for n, (lo, hi, t0, t1, who, heir) in enumerate(pieces):
             nc.sync.dma_start(saved[n][:], a_planes[:, t0:t1, lo:hi])
             if n == 0:
                 nc.sync.dma_start(offs_t[:], offs)
             if n == 2:
                 nc.sync.dma_start(gate_rows[:], gate[: P * P // S].rearrange("r (c j) -> (r c) j", j=P))
-        folded = keep.tile([P, PACK, S - DIRECT], F32, name="folded")
-        folded_gate = keep.tile([P, S - DIRECT], F32, name="folded_gate")
-        nc.sync.dma_start(folded_gate[:], gate[:, DIRECT:])
-        nc.sync.dma_start(folded[:], a_planes[:, :, DIRECT:])
+        last_group = len(GROUPS) - 1
+        folded_saved = keep.tile([P, PACK, FOLDED], F32, name="folded_saved", align_bytes=64)
+        folded_gate = keep.tile([P, FOLDED], F32, name="folded_gate")
+        nc.sync.dma_start(folded_gate[:], gate[:, FOLD_LO:FOLD_HI])
+        nc.sync.dma_start(folded_saved[:], a_planes[:, :, FOLD_LO:FOLD_HI])
         w1_words = w1t_words[:, 0].rearrange("e p k -> p e k").bitcast(I32)
         nc.sync.dma_start(w1[:, : E - 1].bitcast(I32), w1_words[:, : E - 1])
         nc.sync.dma_start(w1[:, E - 1, 2 * P : 6 * P].bitcast(I32), w1_words[:, E - 1, P // 2 : 3 * P // 2])
@@ -134,46 +138,64 @@ def tile_moe_sdb_relu_kernel(
         gate_bank = banks("gate_bank", 6, [P, P])
         nc.tensor.transpose(gate_bank[:], gate_rows[:], identity[:])
 
-        mine = [n for n, piece in enumerate(pieces) if piece[4]]
+        mine = [n for n, piece in enumerate(pieces) if piece[4] == "scalar"]
         signs = {}
         for n in mine:
-            lo, hi, t0, t1, by_scalar = pieces[n]
-            signs[n] = keep.tile([P, t1 - t0, hi - lo], BF16, name=f"sign{n}", tag="held" if n == mine[-1] else f"sign{n}", align_bytes=64)
+            lo, hi, t0, t1, who, heir = pieces[n]
+            if n == mine[-1]:
+                signs[n] = shared.tile([P, t1 - t0, hi - lo], BF16, name=f"sign{n}", offset=0, align_bytes=64)
+            else:
+                signs[n] = keep.tile([P, t1 - t0, hi - lo], BF16, name=f"sign{n}", tag="picked1_3", align_bytes=64)
             nc.scalar.activation(signs[n][:], saved[n][:], ACT.Sign)
         for n in mine:
             nc.scalar.activation(saved[n][:], signs[n][:], ACT.Relu)
 
+        mask_of = {n: saved[n] for n in mine}
+
+        def make_mask(n):
+            lo, hi, t0, t1, who, heir = pieces[n]
+            if heir is None:
+                mask_of[n] = saved[n]
+            elif heir == (2, 1):
+                mask_of[n] = keep.tile([P, t1 - t0, hi - lo], F32, name=f"mask{n}", tag="saved640_1", align_bytes=64)
+            else:
+                mask_of[n] = shared.tile([P, t1 - t0, hi - lo], F32, name=f"mask{n}", offset=1024, align_bytes=64)
+            nc.vector.tensor_scalar(mask_of[n][:], saved[n][:], 0.0, None, ALU.is_gt)
+
         def factor(t, lo, hi):
-            for n, (p_lo, p_hi, t0, t1, by_scalar) in enumerate(pieces):
+            for n, (p_lo, p_hi, t0, t1, who, heir) in enumerate(pieces):
                 if p_lo <= lo and hi <= p_hi and t0 <= t < t1:
-                    return saved[n][:, t - t0, lo - p_lo : hi - p_lo]
+                    return mask_of[n][:, t - t0, lo - p_lo : hi - p_lo]
             raise ValueError("no piece")
 
-        def gather(lo, hi, factors):
-            picked = keep.tile([P, PACK, hi - lo], F32, name=f"picked{lo}")
-            entries = offs_t[:, lo // LIST_ROWS : hi // LIST_ROWS]
-            for t in range(PACK):
-                nc.vector.tensor_tensor(picked[:, t, :], dc[t][:].indirect(entries), factors[t], ALU.mult)
-            return picked
+        def entries(lo, hi):
+            return offs_t[:, lo // LIST_ROWS : hi // LIST_ROWS]
 
-        picked = []
-        for lo, hi in zip(edges, edges[1:]):
-            for n, (p_lo, p_hi, t0, t1, by_scalar) in enumerate(pieces):
-                if p_lo == lo and not by_scalar:
-                    nc.vector.tensor_scalar(saved[n][:], saved[n][:], 0.0, None, ALU.is_gt)
-            picked.append(gather(lo, hi, [factor(t, lo, hi) for t in range(PACK)]))
-        for t in (0, PACK // 2):
-            part = folded[:, t : t + PACK // 2, :]
-            spread = folded_gate[:].unsqueeze(1).to_broadcast([P, PACK // 2, S - DIRECT])
-            nc.vector.scalar_tensor_tensor(part, part, 0.0, spread, ALU.is_gt, ALU.mult)
-        picked_folded = gather(DIRECT, S, [folded[:, t, :] for t in range(PACK)])
+        for n, piece in enumerate(pieces):
+            if piece[4] == "vector" and piece[5] is None:
+                make_mask(n)
+        picked = {}
+        for g, (first_block, end_block) in enumerate(GROUPS):
+            lo, hi = first_block * P, end_block * P
+            for t in ORDER[g]:
+                for n, piece in enumerate(pieces):
+                    if piece[5] == (g, t):
+                        make_mask(n)
+                if (g, t) == (last_group, PACK - 1):
+                    folded = keep.tile([P, PACK, FOLDED], F32, name="folded", tag="saved640_1", align_bytes=64)
+                    spread = folded_gate[:].unsqueeze(1).to_broadcast([P, PACK, FOLDED])
+                    nc.vector.scalar_tensor_tensor(folded[:], folded_saved[:], 0.0, spread, ALU.is_gt, ALU.mult)
+                picked[g, t] = keep.tile([P, hi - lo], F32, name=f"picked{g}_{t}", align_bytes=64)
+                nc.vector.tensor_tensor(picked[g, t][:], dc[t][:].indirect(entries(lo, hi)), factor(t, lo, hi), ALU.mult)
+        picked_folded = keep.tile([P, PACK, FOLDED], F32, name="picked_folded", align_bytes=64)
+        for t in range(PACK):
+            nc.vector.tensor_tensor(picked_folded[:, t, :], dc[t][:].indirect(entries(FOLD_LO, FOLD_HI)), folded[:, t, :], ALU.mult)
 
-        slot_gate = keep.tile([P, BLOCKS], F32, name="slot_gate", tag="held", align_bytes=64)
-        nc.scalar.copy(slot_gate[:], gate_bank[:, :BLOCKS])
-        words = keep.tile([P, 2 * DIRECT], F32, name="words", align_bytes=64)
+        slot_gate = shared.tile([P, S // P], F32, name="slot_gate", offset=0, align_bytes=64)
+        nc.scalar.copy(slot_gate[:], gate_bank[:, : S // P])
+        words = keep.tile([P, 2 * FOLD_LO], F32, name="words", align_bytes=64)
         pairs = []
-        for lo, hi in zip(edges, edges[1:]):
-            first_block, end_block = lo // P, hi // P
+        for first_block, end_block in GROUPS:
             pairs.extend(list(range(max(b, first_block), b + 2)) for b in range(first_block - (end_block - first_block) % 2, end_block, 2))
         gated = {}
 
@@ -185,10 +207,10 @@ def tile_moe_sdb_relu_kernel(
                 bank = [banks(f"turning{k}_{j}", 2 * (k % 2) + j, [P, PACK, P])[:] for j in range(2)]
             gated[k] = keep.tile([P, len(pairs[k]), 2, P, 2], BF16, name=f"gated{k}", align_bytes=64)
             for j, blk in enumerate(pairs[k]):
-                g = max(n for n, edge in enumerate(edges) if edge <= blk * P)
-                at = blk * P - edges[g]
-                for t in range(PACK):
-                    nc.tensor.transpose(bank[j][:, t, :], picked[g][:, t, at : at + P], identity[:])
+                g = max(n for n, group in enumerate(GROUPS) if group[0] <= blk)
+                at = (blk - GROUPS[g][0]) * P
+                for t in ORDER[g]:
+                    nc.tensor.transpose(bank[j][:, t, :], picked[g, t][:, at : at + P], identity[:])
             return bank
 
         def apply_gate(k, j, bank):
@@ -224,11 +246,11 @@ def tile_moe_sdb_relu_kernel(
             back[k] = turn_back(k)
             if k + ahead < len(pairs):
                 turned[k + ahead] = turn(k + ahead)
-        woven = keep.tile([P, S - DIRECT, PACK], BF16, name="woven", tag="held", align_bytes=64)
+        copy_back(len(pairs) - 1, back[len(pairs) - 1])
+        woven = shared.tile([P, FOLDED, PACK], BF16, name="woven", offset=0, align_bytes=64)
         nc.scalar.copy(
             woven[:].rearrange("p (c i) t -> p c t i", i=RUN), picked_folded[:].rearrange("p t (c i) -> p c t i", i=RUN)
         )
-        copy_back(len(pairs) - 1, back[len(pairs) - 1])
 
         codes = keep.tile([P, S], I32, name="codes", tag=f"gated{len(pairs) - 2}", align_bytes=64)
         scales = keep.tile([P, S], U8, name="scales", align_bytes=64)
@@ -236,15 +258,13 @@ def tile_moe_sdb_relu_kernel(
         def quantise(lo, hi, values):
             nc.vector.quantize_mx(out=codes[:, lo:hi].bitcast(E5M2), scales=scales[:, lo:hi], in_=values)
 
-        last = pairs[-1][0] * P
-        cuts = [0, C, 2 * C, 3 * C, last]
+        cuts = [0, C, 2 * C, 3 * C, pairs[-1][0] * P, FOLD_LO]
         for lo, hi in zip(cuts, cuts[1:]):
             quantise(lo, hi, words[:, 2 * lo : 2 * hi].bitcast(BF16))
-        quantise(DIRECT, S, woven[:].rearrange("p c t -> p (c t)"))
-        quantise(last, DIRECT, words[:, 2 * last :].bitcast(BF16))
+        quantise(FOLD_LO, FOLD_HI, woven[:].rearrange("p c t -> p (c t)"))
 
         dx = [
-            keep.tile([P, S], F32, name="dx0", tag=f"picked{DIRECT}"),
+            keep.tile([P, S], F32, name="dx0", tag="picked_folded", align_bytes=64),
             keep.tile([P, S], F32, name="dx1", tag="w1_last", align_bytes=64),
             keep.tile([P, S], F32, name="dx2"),
             keep.tile([P, S], F32, name="dx3"),
@@ -252,23 +272,29 @@ def tile_moe_sdb_relu_kernel(
         end = len(pairs) - 1
         product_at = [2 * (end % 2) + 1, single_at[(end - 1) % 2], single_at[end % 2], 2 * (end % 2)]
         apart = {(E - 1, 0): w1_last[:], (E - 1, K // P - 1): w1_end[:]}
+        def multiply(b, e, lo, at):
+            product = banks(f"product{b}_{e}_{lo}", at, [P, BANK])
+            nc.tensor.matmul_mx(
+                out=product[:],
+                lhsT=apart.get((e, b), w1[:, e, 2 * b * P : 2 * (b + 1) * P]).bitcast(E2M1),
+                lhsT_scale=w1s[:, e, b * P : (b + 1) * P],
+                rhs=codes[:, lo : lo + BANK].bitcast(E5M2),
+                rhs_scale=scales[:, lo : lo + BANK],
+                start=True,
+                stop=True,
+            )
+            return product
+
         for b in range(K // P):
             for e in range(E):
-                cols = slice(e * C, (e + 1) * C)
-                product = banks(f"product{b}_{e}", product_at[e], [P, BANK])
-                nc.tensor.matmul_mx(
-                    out=product[:],
-                    lhsT=apart.get((e, b), w1[:, e, 2 * b * P : 2 * (b + 1) * P]).bitcast(E2M1),
-                    lhsT_scale=w1s[:, e, b * P : (b + 1) * P],
-                    rhs=codes[:, cols].bitcast(E5M2),
-                    rhs_scale=scales[:, cols],
-                    start=True,
-                    stop=True,
-                )
-                if (e, b) == (E - 2, 0):
-                    nc.vector.tensor_copy(dx[b][:, cols], product[:])
+                lo = e * C
+                if (e, b) == (E - 1, 0):
+                    early = multiply(b, e, FOLD_LO - BANK, product_at[e])
+                    nc.vector.tensor_copy(dx[b][:, lo:FOLD_LO], early[:, BANK - (FOLD_LO - lo) :])
+                    late = multiply(b, e, lo, 4)
+                    nc.scalar.copy(dx[b][:, FOLD_LO:], late[:, FOLD_LO - lo :])
                 else:
-                    nc.scalar.copy(dx[b][:, cols], product[:])
+                    nc.scalar.copy(dx[b][:, lo : lo + C], multiply(b, e, lo, product_at[e])[:])
 
         first = [keep.tile([P, T], F32, name=f"first{b}") for b in range(K // P)]
 
@@ -289,6 +315,6 @@ def tile_moe_sdb_relu_kernel(
         fetch_first(1, [0, T])
         fetch_first(2, [0, T])
         add_second(1, [0, T], "w1_end")
+        fetch_first(3, [0, T])
         add_second(2, [0, T])
-        fetch_first(3, token_halves)
         add_second(3, TAIL_CUTS)

@@ -39,7 +39,6 @@ def tile_moe_sdb_relu_kernel(
     nc = tc.nc
     with ExitStack() as ctx:
         keep = ctx.enter_context(tc.tile_pool(name="keep", bufs=1))
-        shared = ctx.enter_context(tc.tile_pool(name="shared", bufs=1))
         psum = ctx.enter_context(tc.psum_pool(name="psum", bufs=1))
 
         def banks(name, start, shape):
@@ -86,10 +85,15 @@ def tile_moe_sdb_relu_kernel(
         ]
         saved = [
             keep.tile([P, t1 - t0, hi - lo], F32, name=f"saved{lo}_{t0}", align_bytes=64)
+            if lo != 1280 else None
             for lo, hi, t0, t1, who, heir in pieces
         ]
+        whole = keep.tile([P, PACK, 384], F32, name="whole", align_bytes=64)
         for n, (lo, hi, t0, t1, who, heir) in enumerate(pieces):
-            nc.sync.dma_start(saved[n][:], a_planes[:, t0:t1, lo:hi])
+            if lo != 1280:
+                nc.sync.dma_start(saved[n][:], a_planes[:, t0:t1, lo:hi])
+            elif t0 == 0:
+                nc.sync.dma_start(whole[:], a_planes[:, :, lo:hi])
             if n == 0:
                 nc.sync.dma_start(offs_t[:], offs)
             if n == 2:
@@ -143,24 +147,28 @@ def tile_moe_sdb_relu_kernel(
         for n in mine:
             lo, hi, t0, t1, who, heir = pieces[n]
             if n == mine[-1]:
-                signs[n] = shared.tile([P, t1 - t0, hi - lo], BF16, name=f"sign{n}", offset=0, align_bytes=64)
+                signs[n] = keep.tile([P, t1 - t0, hi - lo], BF16, name=f"sign{n}", tag="held", align_bytes=64)
             else:
                 signs[n] = keep.tile([P, t1 - t0, hi - lo], BF16, name=f"sign{n}", tag="picked1_3", align_bytes=64)
             nc.scalar.activation(signs[n][:], saved[n][:], ACT.Sign)
         for n in mine:
             nc.scalar.activation(saved[n][:], signs[n][:], ACT.Relu)
 
-        mask_of = {n: saved[n] for n in mine}
+        mask_of = {n: saved[n][:] for n in mine}
+        mask_and_gate = keep.tile([P, 2 * 384 + S // P], F32, name="mask_and_gate", tag="held", align_bytes=64)
+        slot_gate = mask_and_gate[:, 2 * 384 :]
 
         def make_mask(n):
             lo, hi, t0, t1, who, heir = pieces[n]
             if heir is None:
-                mask_of[n] = saved[n]
+                mask_of[n] = saved[n][:]
+            elif heir == (1, 2):
+                mask_of[n] = mask_and_gate[:, : 2 * 384].rearrange("p (t j) -> p t j", t=2)
             elif heir == (2, 1):
-                mask_of[n] = keep.tile([P, t1 - t0, hi - lo], F32, name=f"mask{n}", tag="saved640_1", align_bytes=64)
+                mask_of[n] = keep.tile([P, t1 - t0, hi - lo], F32, name=f"mask{n}", tag="saved640_1", align_bytes=64)[:]
             else:
-                mask_of[n] = shared.tile([P, t1 - t0, hi - lo], F32, name=f"mask{n}", offset=1024, align_bytes=64)
-            nc.vector.tensor_scalar(mask_of[n][:], saved[n][:], 0.0, None, ALU.is_gt)
+                mask_of[n] = keep.tile([P, t1 - t0, hi - lo], F32, name=f"mask{n}", tag="whole", align_bytes=64)[:]
+            nc.vector.tensor_scalar(mask_of[n], whole[:, t0:t1] if lo == 1280 else saved[n][:], 0.0, None, ALU.is_gt)
 
         def factor(t, lo, hi):
             for n, (p_lo, p_hi, t0, t1, who, heir) in enumerate(pieces):
@@ -191,12 +199,11 @@ def tile_moe_sdb_relu_kernel(
         for t in range(PACK):
             nc.vector.tensor_tensor(picked_folded[:, t, :], dc[t][:].indirect(entries(FOLD_LO, FOLD_HI)), folded[:, t, :], ALU.mult)
 
-        slot_gate = shared.tile([P, S // P], F32, name="slot_gate", offset=0, align_bytes=64)
-        nc.scalar.copy(slot_gate[:], gate_bank[:, : S // P])
+        nc.scalar.copy(slot_gate, gate_bank[:, : S // P])
         words = keep.tile([P, 2 * FOLD_LO], F32, name="words", align_bytes=64)
         pairs = []
         for first_block, end_block in GROUPS:
-            pairs.extend(list(range(max(b, first_block), b + 2)) for b in range(first_block - (end_block - first_block) % 2, end_block, 2))
+            pairs.extend(list(range(b, min(b + 2, end_block))) for b in range(first_block, end_block, 2))
         gated = {}
 
         def turn(k):
@@ -206,10 +213,10 @@ def tile_moe_sdb_relu_kernel(
             else:
                 bank = [banks(f"turning{k}_{j}", 2 * (k % 2) + j, [P, PACK, P])[:] for j in range(2)]
             gated[k] = keep.tile([P, len(pairs[k]), 2, P, 2], BF16, name=f"gated{k}", align_bytes=64)
-            for j, blk in enumerate(pairs[k]):
-                g = max(n for n, group in enumerate(GROUPS) if group[0] <= blk)
-                at = (blk - GROUPS[g][0]) * P
-                for t in ORDER[g]:
+            g = max(n for n, group in enumerate(GROUPS) if group[0] <= pairs[k][0])
+            for t in ORDER[g]:
+                for j, blk in enumerate(pairs[k]):
+                    at = (blk - GROUPS[g][0]) * P
                     nc.tensor.transpose(bank[j][:, t, :], picked[g, t][:, at : at + P], identity[:])
             return bank
 
@@ -247,7 +254,7 @@ def tile_moe_sdb_relu_kernel(
             if k + ahead < len(pairs):
                 turned[k + ahead] = turn(k + ahead)
         copy_back(len(pairs) - 1, back[len(pairs) - 1])
-        woven = shared.tile([P, FOLDED, PACK], BF16, name="woven", offset=0, align_bytes=64)
+        woven = keep.tile([P, FOLDED, PACK], BF16, name="woven", tag="held", align_bytes=64)
         nc.scalar.copy(
             woven[:].rearrange("p (c i) t -> p c t i", i=RUN), picked_folded[:].rearrange("p t (c i) -> p c t i", i=RUN)
         )
@@ -258,10 +265,12 @@ def tile_moe_sdb_relu_kernel(
         def quantise(lo, hi, values):
             nc.vector.quantize_mx(out=codes[:, lo:hi].bitcast(E5M2), scales=scales[:, lo:hi], in_=values)
 
-        cuts = [0, C, 2 * C, 3 * C, pairs[-1][0] * P, FOLD_LO]
+        last = pairs[-1][0] * P
+        cuts = [0, 2 * C, 3 * C, last]
         for lo, hi in zip(cuts, cuts[1:]):
             quantise(lo, hi, words[:, 2 * lo : 2 * hi].bitcast(BF16))
         quantise(FOLD_LO, FOLD_HI, woven[:].rearrange("p c t -> p (c t)"))
+        quantise(last, FOLD_LO, words[:, 2 * last :].bitcast(BF16))
 
         dx = [
             keep.tile([P, S], F32, name="dx0", tag="picked_folded", align_bytes=64),
@@ -288,11 +297,8 @@ def tile_moe_sdb_relu_kernel(
         for b in range(K // P):
             for e in range(E):
                 lo = e * C
-                if (e, b) == (E - 1, 0):
-                    early = multiply(b, e, FOLD_LO - BANK, product_at[e])
-                    nc.vector.tensor_copy(dx[b][:, lo:FOLD_LO], early[:, BANK - (FOLD_LO - lo) :])
-                    late = multiply(b, e, lo, 4)
-                    nc.scalar.copy(dx[b][:, FOLD_LO:], late[:, FOLD_LO - lo :])
+                if (e, b) == (E - 2, 0):
+                    nc.vector.tensor_copy(dx[b][:, lo : lo + C], multiply(b, e, lo, product_at[e])[:])
                 else:
                     nc.scalar.copy(dx[b][:, lo : lo + C], multiply(b, e, lo, product_at[e])[:])
 

@@ -168,9 +168,16 @@ def tile_moe_sdb_relu_kernel(
                 mask_of[n] = keep.tile([P, t1 - t0, hi - lo], F32, name=f"mask{n}", tag="saved640_1", align_bytes=64)[:]
             else:
                 mask_of[n] = keep.tile([P, t1 - t0, hi - lo], F32, name=f"mask{n}", tag="whole", align_bytes=64)[:]
-            nc.vector.tensor_scalar(mask_of[n], whole[:, t0:t1] if lo == 1280 else saved[n][:], 0.0, None, ALU.is_gt)
+            if lo == 1664:
+                nc.vector.tensor_scalar(mask_of[n][:, :2], saved[n][:, :2], 0.0, None, ALU.is_gt)
+            else:
+                nc.vector.tensor_scalar(mask_of[n], whole[:, t0:t1] if lo == 1280 else saved[n][:], 0.0, None, ALU.is_gt)
+
+        late_masks = {}
 
         def factor(t, lo, hi):
+            if lo == 1664 and t in late_masks:
+                return late_masks[t][:]
             for n, (p_lo, p_hi, t0, t1, who, heir) in enumerate(pieces):
                 if p_lo <= lo and hi <= p_hi and t0 <= t < t1:
                     return mask_of[n][:, t - t0, lo - p_lo : hi - p_lo]
@@ -183,21 +190,22 @@ def tile_moe_sdb_relu_kernel(
             if piece[4] == "vector" and piece[5] is None:
                 make_mask(n)
         picked = {}
-        for g, (first_block, end_block) in enumerate(GROUPS):
-            lo, hi = first_block * P, end_block * P
+
+        def gather_group(g):
+            lo, hi = GROUPS[g][0] * P, GROUPS[g][1] * P
             for t in ORDER[g]:
                 for n, piece in enumerate(pieces):
                     if piece[5] == (g, t):
                         make_mask(n)
                 if (g, t) == (last_group, PACK - 1):
-                    folded = keep.tile([P, PACK, FOLDED], F32, name="folded", tag="saved640_1", align_bytes=64)
                     spread = folded_gate[:].unsqueeze(1).to_broadcast([P, PACK, FOLDED])
                     nc.vector.scalar_tensor_tensor(folded[:], folded_saved[:], 0.0, spread, ALU.is_gt, ALU.mult)
                 picked[g, t] = keep.tile([P, hi - lo], F32, name=f"picked{g}_{t}", align_bytes=64)
                 nc.vector.tensor_tensor(picked[g, t][:], dc[t][:].indirect(entries(lo, hi)), factor(t, lo, hi), ALU.mult)
-        picked_folded = keep.tile([P, PACK, FOLDED], F32, name="picked_folded", align_bytes=64)
-        for t in range(PACK):
-            nc.vector.tensor_tensor(picked_folded[:, t, :], dc[t][:].indirect(entries(FOLD_LO, FOLD_HI)), folded[:, t, :], ALU.mult)
+
+        for g in range(last_group):
+            gather_group(g)
+        folded = keep.tile([P, PACK, FOLDED], F32, name="folded", tag="saved640_1", align_bytes=64)
 
         nc.scalar.copy(slot_gate, gate_bank[:, : S // P])
         words = keep.tile([P, 2 * FOLD_LO], F32, name="words", align_bytes=64)
@@ -251,6 +259,17 @@ def tile_moe_sdb_relu_kernel(
                 if j == len(pairs[k]) - 1 and k > 0:
                     copy_back(k - 1, back[k - 1])
             back[k] = turn_back(k)
+            if k == 2:
+                late_signs = keep.tile([P, 2, 2 * P], BF16, name="late_signs", tag="gated1", align_bytes=64)
+                for t in (2, 3):
+                    nc.scalar.activation(late_signs[:, t - 2], saved[-1][:, t], ACT.Sign)
+                for t in (2, 3):
+                    late_masks[t] = keep.tile([P, 2 * P], F32, name=f"late_mask{t}", align_bytes=64)
+                    nc.scalar.activation(late_masks[t][:], late_signs[:, t - 2], ACT.Relu)
+                gather_group(last_group)
+                picked_folded = keep.tile([P, PACK, FOLDED], F32, name="picked_folded", tag="late_mask2", align_bytes=64)
+                for t in range(PACK):
+                    nc.vector.tensor_tensor(picked_folded[:, t, :], dc[t][:].indirect(entries(FOLD_LO, FOLD_HI)), folded[:, t, :], ALU.mult)
             if k + ahead < len(pairs):
                 turned[k + ahead] = turn(k + ahead)
         copy_back(len(pairs) - 1, back[len(pairs) - 1])
@@ -273,7 +292,7 @@ def tile_moe_sdb_relu_kernel(
         quantise(last, FOLD_LO, words[:, 2 * last :].bitcast(BF16))
 
         dx = [
-            keep.tile([P, S], F32, name="dx0", tag="picked_folded", align_bytes=64),
+            keep.tile([P, S], F32, name="dx0", tag="late_mask2", align_bytes=64),
             keep.tile([P, S], F32, name="dx1", tag="w1_last", align_bytes=64),
             keep.tile([P, S], F32, name="dx2"),
             keep.tile([P, S], F32, name="dx3"),

@@ -81,7 +81,7 @@ def tile_moe_sdb_relu_kernel(
         pieces = [
             (0, 640, 0, 1, "vector", None), (0, 640, 1, 2, "vector", None), (0, 640, 2, 4, "vector", None),
             (640, 1280, 0, 1, "scalar", None), (640, 1280, 1, 3, "scalar", None), (640, 1280, 3, 4, "vector", None),
-            (1280, 1664, 0, 2, "vector", (1, 2)), (1280, 1664, 2, 4, "vector", (2, 1)), (1664, 1920, 0, 4, "vector", (2, 3)),
+            (1280, 1664, 0, 2, "vector", (1, 2)), (1280, 1664, 2, 4, "vector", (2, 1)), (1664, 1920, 0, 4, "late", None),
         ]
         saved = [
             keep.tile([P, t1 - t0, hi - lo], F32, name=f"saved{lo}_{t0}", align_bytes=64)
@@ -168,16 +168,13 @@ def tile_moe_sdb_relu_kernel(
                 mask_of[n] = keep.tile([P, t1 - t0, hi - lo], F32, name=f"mask{n}", tag="saved640_1", align_bytes=64)[:]
             else:
                 mask_of[n] = keep.tile([P, t1 - t0, hi - lo], F32, name=f"mask{n}", tag="whole", align_bytes=64)[:]
-            if lo == 1664:
-                nc.vector.tensor_scalar(mask_of[n][:, :2], saved[n][:, :2], 0.0, None, ALU.is_gt)
-            else:
-                nc.vector.tensor_scalar(mask_of[n], whole[:, t0:t1] if lo == 1280 else saved[n][:], 0.0, None, ALU.is_gt)
+            nc.vector.tensor_scalar(mask_of[n], whole[:, t0:t1] if lo == 1280 else saved[n][:], 0.0, None, ALU.is_gt)
 
         late_masks = {}
 
         def factor(t, lo, hi):
-            if lo == 1664 and t in late_masks:
-                return late_masks[t][:]
+            if lo == 1664:
+                return late_masks[t // 2][:, t % 2]
             for n, (p_lo, p_hi, t0, t1, who, heir) in enumerate(pieces):
                 if p_lo <= lo and hi <= p_hi and t0 <= t < t1:
                     return mask_of[n][:, t - t0, lo - p_lo : hi - p_lo]
@@ -199,13 +196,14 @@ def tile_moe_sdb_relu_kernel(
                         make_mask(n)
                 if (g, t) == (last_group, PACK - 1):
                     spread = folded_gate[:].unsqueeze(1).to_broadcast([P, PACK, FOLDED])
-                    nc.vector.scalar_tensor_tensor(folded[:], folded_saved[:], 0.0, spread, ALU.is_gt, ALU.mult)
+                    folded[0] = keep.tile([P, PACK, FOLDED], F32, name="folded", tag="late_mask0", align_bytes=64)
+                    nc.vector.scalar_tensor_tensor(folded[0][:], folded_saved[:], 0.0, spread, ALU.is_gt, ALU.mult)
                 picked[g, t] = keep.tile([P, hi - lo], F32, name=f"picked{g}_{t}", align_bytes=64)
                 nc.vector.tensor_tensor(picked[g, t][:], dc[t][:].indirect(entries(lo, hi)), factor(t, lo, hi), ALU.mult)
 
         for g in range(last_group):
             gather_group(g)
-        folded = keep.tile([P, PACK, FOLDED], F32, name="folded", tag="saved640_1", align_bytes=64)
+        folded = {}
 
         nc.scalar.copy(slot_gate, gate_bank[:, : S // P])
         words = keep.tile([P, 2 * FOLD_LO], F32, name="words", align_bytes=64)
@@ -259,17 +257,17 @@ def tile_moe_sdb_relu_kernel(
                 if j == len(pairs[k]) - 1 and k > 0:
                     copy_back(k - 1, back[k - 1])
             back[k] = turn_back(k)
+            if k == 1:
+                late_signs = keep.tile([P, 2, 2, 2 * P], BF16, name="late_signs", tag="gated0", align_bytes=64)
+                nc.scalar.activation(late_signs[:].rearrange("p u r j -> p (u r) j"), saved[-1][:], ACT.Sign)
             if k == 2:
-                late_signs = keep.tile([P, 2, 2 * P], BF16, name="late_signs", tag="gated1", align_bytes=64)
-                for t in (2, 3):
-                    nc.scalar.activation(late_signs[:, t - 2], saved[-1][:, t], ACT.Sign)
-                for t in (2, 3):
-                    late_masks[t] = keep.tile([P, 2 * P], F32, name=f"late_mask{t}", align_bytes=64)
-                    nc.scalar.activation(late_masks[t][:], late_signs[:, t - 2], ACT.Relu)
+                for u in range(2):
+                    late_masks[u] = keep.tile([P, 2, 2 * P], F32, name=f"late_mask{u}", align_bytes=64)
+                    nc.scalar.activation(late_masks[u][:], late_signs[:, u], ACT.Relu)
                 gather_group(last_group)
-                picked_folded = keep.tile([P, PACK, FOLDED], F32, name="picked_folded", tag="late_mask2", align_bytes=64)
+                picked_folded = keep.tile([P, PACK, FOLDED], F32, name="picked_folded", align_bytes=64)
                 for t in range(PACK):
-                    nc.vector.tensor_tensor(picked_folded[:, t, :], dc[t][:].indirect(entries(FOLD_LO, FOLD_HI)), folded[:, t, :], ALU.mult)
+                    nc.vector.tensor_tensor(picked_folded[:, t, :], dc[t][:].indirect(entries(FOLD_LO, FOLD_HI)), folded[0][:, t, :], ALU.mult)
             if k + ahead < len(pairs):
                 turned[k + ahead] = turn(k + ahead)
         copy_back(len(pairs) - 1, back[len(pairs) - 1])
@@ -285,14 +283,14 @@ def tile_moe_sdb_relu_kernel(
             nc.vector.quantize_mx(out=codes[:, lo:hi].bitcast(E5M2), scales=scales[:, lo:hi], in_=values)
 
         last = pairs[-1][0] * P
-        cuts = [0, 2 * C, 3 * C, last]
+        cuts = [0, C, 2 * C, 3 * C, last]
         for lo, hi in zip(cuts, cuts[1:]):
             quantise(lo, hi, words[:, 2 * lo : 2 * hi].bitcast(BF16))
         quantise(FOLD_LO, FOLD_HI, woven[:].rearrange("p c t -> p (c t)"))
         quantise(last, FOLD_LO, words[:, 2 * last :].bitcast(BF16))
 
         dx = [
-            keep.tile([P, S], F32, name="dx0", tag="late_mask2", align_bytes=64),
+            keep.tile([P, S], F32, name="dx0", tag="picked_folded", align_bytes=64),
             keep.tile([P, S], F32, name="dx1", tag="w1_last", align_bytes=64),
             keep.tile([P, S], F32, name="dx2"),
             keep.tile([P, S], F32, name="dx3"),

@@ -45,7 +45,7 @@ def tile_moe_sdb_relu_kernel(
             return psum.tile(shape, F32, name=name, offset=start * BANK_BYTES)
 
         pair_at = [4, 0, 2]
-        single_at = [7, 5]
+        single_at = [7, 5, 6]
 
         offs_t = keep.tile([P, S // LIST_ROWS], U16, name="offs_t")
         pos1_t = keep.tile([P, T // LIST_ROWS], U16, name="pos1_t")
@@ -212,29 +212,30 @@ def tile_moe_sdb_relu_kernel(
             pairs.extend(list(range(b, min(b + 2, end_block))) for b in range(first_block, end_block, 2))
         gated = {}
 
-        def turn(k):
-            if k < len(pairs) - 1:
-                both = banks(f"turning{k}", 2 * (k % 2), [P, 2, PACK, P])
-                bank = [both[:, j] for j in range(2)]
-            else:
-                bank = [banks(f"turning{k}_{j}", 2 * (k % 2) + j, [P, PACK, P])[:] for j in range(2)]
-            gated[k] = keep.tile([P, len(pairs[k]), 2, P, 2], BF16, name=f"gated{k}", align_bytes=64)
-            g = max(n for n, group in enumerate(GROUPS) if group[0] <= pairs[k][0])
-            for t in ORDER[g]:
-                for j, blk in enumerate(pairs[k]):
-                    at = (blk - GROUPS[g][0]) * P
-                    nc.tensor.transpose(bank[j][:, t, :], picked[g, t][:, at : at + P], identity[:])
-            return bank
+        turned = {}
 
-        def apply_gate(k, j, bank):
+        def turn(*units):
+            for first_block, end_block, at_bank in units:
+                unit = banks(f"turning{first_block}", at_bank, [P, end_block - first_block, PACK, P])
+                for blk in range(first_block, end_block):
+                    turned[blk] = unit[:, blk - first_block]
+            g = max(n for n, group in enumerate(GROUPS) if group[0] <= units[0][0])
+            for t in ORDER[g]:
+                for blk in range(units[0][0], units[-1][1]):
+                    at = (blk - GROUPS[g][0]) * P
+                    nc.tensor.transpose(turned[blk][:, t, :], picked[g, t][:, at : at + P], identity[:])
+
+        def apply_gate(k, j):
             blk = pairs[k][j]
+            if j == 0:
+                gated[k] = keep.tile([P, len(pairs[k]), 2, P, 2], BF16, name=f"gated{k}", align_bytes=64)
             nc.scalar.activation(
-                gated[k][:, j], bank[j].rearrange("s (u r) p -> s u p r", r=2), ACT.Copy, scale=slot_gate[:, blk : blk + 1]
+                gated[k][:, j], turned[blk].rearrange("s (u r) p -> s u p r", r=2), ACT.Copy, scale=slot_gate[:, blk : blk + 1]
             )
 
         def turn_back(k):
             n = len(pairs[k])
-            bank = banks(f"returning{k}", single_at[k % 2], [P, n, 2, P])
+            bank = banks(f"returning{k}", single_at[k % 3], [P, n, 2, P])
             for j in range(n):
                 row_pairs = gated[k][:, j].rearrange("s u p r -> s (u p r)").bitcast(F32)
                 for u in range(2):
@@ -248,14 +249,16 @@ def tile_moe_sdb_relu_kernel(
                 words[:, lo : lo + 2 * P * n].rearrange("p (j s u) -> p j s u", j=n, u=2), bank[:].rearrange("p j u s -> p j s u")
             )
 
-        ahead = 2
-        turned = {k: turn(k) for k in range(ahead)}
+        turn((0, 4, 0), (4, 5, 4))
+        follows = {1: [(5, 7, 0), (7, 9, 2)], 2: [(9, 10, 4)], 3: [(10, 12, 0)], 5: [(12, 13, 4)], 6: [(13, 15, 0)]}
         back = {}
         for k in range(len(pairs)):
             for j in range(len(pairs[k])):
-                apply_gate(k, j, turned[k])
-                if j == len(pairs[k]) - 1 and k > 0:
-                    copy_back(k - 1, back[k - 1])
+                apply_gate(k, j)
+            if k == 6:
+                copy_back(k - 2, back[k - 2])
+            if k > 0 and k != 5:
+                copy_back(k - 1, back[k - 1])
             back[k] = turn_back(k)
             if k == 1:
                 late_signs = keep.tile([P, 2, 2, 2 * P], BF16, name="late_signs", tag="gated0", align_bytes=64)
@@ -268,15 +271,15 @@ def tile_moe_sdb_relu_kernel(
                 picked_folded = keep.tile([P, PACK, FOLDED], F32, name="picked_folded", align_bytes=64)
                 for t in range(PACK):
                     nc.vector.tensor_tensor(picked_folded[:, t, :], dc[t][:].indirect(entries(FOLD_LO, FOLD_HI)), folded[0][:, t, :], ALU.mult)
-            if k + ahead < len(pairs):
-                turned[k + ahead] = turn(k + ahead)
+            if k in follows:
+                turn(*follows[k])
         copy_back(len(pairs) - 1, back[len(pairs) - 1])
         woven = keep.tile([P, FOLDED, PACK], BF16, name="woven", tag="held", align_bytes=64)
         nc.scalar.copy(
             woven[:].rearrange("p (c i) t -> p c t i", i=RUN), picked_folded[:].rearrange("p t (c i) -> p c t i", i=RUN)
         )
 
-        codes = keep.tile([P, S], I32, name="codes", tag=f"gated{len(pairs) - 2}", align_bytes=64)
+        codes = keep.tile([P, S], I32, name="codes", tag=f"gated{len(pairs) - 4}", align_bytes=64)
         scales = keep.tile([P, S], U8, name="scales", align_bytes=64)
 
         def quantise(lo, hi, values):
@@ -296,7 +299,7 @@ def tile_moe_sdb_relu_kernel(
             keep.tile([P, S], F32, name="dx3"),
         ]
         end = len(pairs) - 1
-        product_at = [2 * (end % 2) + 1, single_at[(end - 1) % 2], single_at[end % 2], 2 * (end % 2)]
+        product_at = [1, single_at[(end - 1) % 3], single_at[end % 3], 0]
         apart = {(E - 1, 0): w1_last[:], (E - 1, K // P - 1): w1_end[:]}
         def multiply(b, e, lo, at):
             product = banks(f"product{b}_{e}_{lo}", at, [P, BANK])

@@ -1,7 +1,6 @@
 from contextlib import ExitStack
 
 import concourse.mybir as mybir
-from concourse.masks import make_identity
 
 K, T, E, C, H, N = 512, 1024, 4, 512, 512, 512
 S = E * C
@@ -22,15 +21,11 @@ P = 128
 PACK = 4
 QUADRANTS = 4
 BANK = 512
-LIST_ROWS = 16
-RUN = 4
-
-GROUPS = [(0, 5), (5, 10), (10, 13), (13, 15)]
-ORDER = [(0, 1, 2, 3), (0, 3, 1, 2), (0, 1, 2, 3), (0, 1, 2, 3)]
-FOLD_LO, FOLD_HI = 15 * P, 16 * P
-FOLDED = FOLD_HI - FOLD_LO
-TAIL_CUTS = [0, 512, 832, 960, T]
+BANKS = 8
 BANK_BYTES = 2048
+LIST_ROWS = 16
+RUN = 2
+TAIL_CUTS = [0, 512, 832, 960, T]
 
 
 def tile_moe_sdb_relu_kernel(
@@ -41,11 +36,8 @@ def tile_moe_sdb_relu_kernel(
         keep = ctx.enter_context(tc.tile_pool(name="keep", bufs=1))
         psum = ctx.enter_context(tc.psum_pool(name="psum", bufs=1))
 
-        def banks(name, start, shape):
-            return psum.tile(shape, F32, name=name, offset=start * BANK_BYTES)
-
-        pair_at = [4, 0, 2]
-        single_at = [7, 5, 6]
+        def bank(name, at):
+            return psum.tile([P, BANK], F32, name=name, offset=at * BANK_BYTES)
 
         offs_t = keep.tile([P, S // LIST_ROWS], U16, name="offs_t")
         pos1_t = keep.tile([P, T // LIST_ROWS], U16, name="pos1_t")
@@ -60,8 +52,6 @@ def tile_moe_sdb_relu_kernel(
         w1 = keep.tile([P, E, 2 * K], U8, name="w1", align_bytes=64)
         w1s = keep.tile([P, E, K], U8, name="w1s", align_bytes=64)
         dc = [keep.tile([P, T], F32, name=f"dc{t}") for t in range(PACK)]
-        identity = keep.tile([P, P], F32, name="identity")
-        make_identity(nc, identity[:])
 
         nc.vector.memset(w2s_raw[:].bitcast(I32), 0)
 
@@ -76,40 +66,14 @@ def tile_moe_sdb_relu_kernel(
         nc.sync.dma_start(dy[:], dy_words[0].rearrange("p n t -> p (n t)").bitcast(I32))
         for q in range(QUADRANTS // 2, QUADRANTS):
             load_scale_rows(dys, dy_scales[0], q)
+        nc.sync.dma_start(offs_t[:], offs)
         a_planes = a.rearrange("(p t) j -> p t j", t=PACK)
-        gate_rows = keep.tile([P, P], F32, name="gate_rows")
-        pieces = [
-            (0, 640, 0, 1, "vector", None), (0, 640, 1, 2, "vector", None), (0, 640, 2, 4, "vector", None),
-            (640, 1280, 0, 1, "scalar", None), (640, 1280, 1, 3, "scalar", None), (640, 1280, 3, 4, "vector", None),
-            (1280, 1664, 0, 2, "vector", (1, 2)), (1280, 1664, 2, 4, "vector", (2, 1)), (1664, 1920, 0, 4, "late", None),
-        ]
-        saved = [
-            keep.tile([P, t1 - t0, hi - lo], F32, name=f"saved{lo}_{t0}", align_bytes=64)
-            if lo != 1280 else None
-            for lo, hi, t0, t1, who, heir in pieces
-        ]
-        whole = keep.tile([P, PACK, 384], F32, name="whole", align_bytes=64)
-        for n, (lo, hi, t0, t1, who, heir) in enumerate(pieces):
-            if lo != 1280:
-                nc.sync.dma_start(saved[n][:], a_planes[:, t0:t1, lo:hi])
-            elif t0 == 0:
-                nc.sync.dma_start(whole[:], a_planes[:, :, lo:hi])
-            if n == 0:
-                nc.sync.dma_start(offs_t[:], offs)
-            if n == 2:
-                nc.sync.dma_start(gate_rows[:], gate[: P * P // S].rearrange("r (c j) -> (r c) j", j=P))
-        last_group = len(GROUPS) - 1
-        folded_saved = keep.tile([P, PACK, FOLDED], F32, name="folded_saved", align_bytes=64)
-        folded_gate = keep.tile([P, FOLDED], F32, name="folded_gate")
-        nc.sync.dma_start(folded_gate[:], gate[:, FOLD_LO:FOLD_HI])
-        nc.sync.dma_start(folded_saved[:], a_planes[:, :, FOLD_LO:FOLD_HI])
-        w1_words = w1t_words[:, 0].rearrange("e p k -> p e k").bitcast(I32)
-        nc.sync.dma_start(w1[:, : E - 1].bitcast(I32), w1_words[:, : E - 1])
-        nc.sync.dma_start(w1[:, E - 1, 2 * P : 6 * P].bitcast(I32), w1_words[:, E - 1, P // 2 : 3 * P // 2])
-        w1_end = keep.tile([P, 2 * P], U8, name="w1_end", align_bytes=64)
-        nc.sync.dma_start(w1_end[:].bitcast(I32), w1_words[:, E - 1, 3 * P // 2 :])
-        w1_last = keep.tile([P, 2 * P], U8, name="w1_last", align_bytes=64)
-        nc.sync.dma_start(w1_last[:].bitcast(I32), w1_words[:, E - 1, : P // 2])
+        factor = [keep.tile([P, PACK, C], F32, name=f"factor{e}", align_bytes=64) for e in range(E)]
+        gates = [keep.tile([P, C], F32, name=f"gates{e}", align_bytes=64) for e in range(E)]
+        for e in range(E):
+            nc.sync.dma_start(gates[e][:], gate[:, e * C : (e + 1) * C])
+            nc.sync.dma_start(factor[e][:], a_planes[:, :, e * C : (e + 1) * C])
+        nc.sync.dma_start(w1[:].bitcast(I32), w1t_words[:, 0].rearrange("e p k -> p e k").bitcast(I32))
         for q in range(QUADRANTS):
             load_scale_rows(w1s, w1t_scales[:, 0].rearrange("e b k -> b e k"), q)
         nc.sync.dma_start(pos1_t[:], pos1)
@@ -124,7 +88,7 @@ def tile_moe_sdb_relu_kernel(
         for t in range(PACK):
             for h in range(T // BANK):
                 cols = slice(h * BANK, (h + 1) * BANK)
-                acc = banks(f"acc{t}_{h}", pair_at[t % 3] + h, [P, BANK])
+                acc = bank(f"acc{t}_{h}", 2 * t + h)
                 nc.tensor.matmul_mx(
                     out=acc[:],
                     lhsT=w2[:, t * P : (t + 1) * P].bitcast(E4M3),
@@ -134,213 +98,74 @@ def tile_moe_sdb_relu_kernel(
                     start=True,
                     stop=True,
                 )
-                if h == 0 and t == 0:
-                    nc.vector.tensor_copy(dc[t][:, cols], acc[:])
-                else:
+                if h == 1 and t == 0:
                     nc.scalar.copy(dc[t][:, cols], acc[:])
+                else:
+                    nc.vector.tensor_copy(dc[t][:, cols], acc[:])
 
-        gate_bank = banks("gate_bank", 6, [P, P])
-        nc.tensor.transpose(gate_bank[:], gate_rows[:], identity[:])
+        def entries(tile, lo, hi):
+            return tile[:, lo // LIST_ROWS : hi // LIST_ROWS]
 
-        mine = [n for n, piece in enumerate(pieces) if piece[4] == "scalar"]
-        signs = {}
-        for n in mine:
-            lo, hi, t0, t1, who, heir = pieces[n]
-            if n == mine[-1]:
-                signs[n] = keep.tile([P, t1 - t0, hi - lo], BF16, name=f"sign{n}", tag="held", align_bytes=64)
-            else:
-                signs[n] = keep.tile([P, t1 - t0, hi - lo], BF16, name=f"sign{n}", tag="picked1_3", align_bytes=64)
-            nc.scalar.activation(signs[n][:], saved[n][:], ACT.Sign)
-        for n in mine:
-            nc.scalar.activation(saved[n][:], signs[n][:], ACT.Relu)
+        picked = [keep.tile([P, PACK, C], F32, name=f"picked{e}", align_bytes=64) for e in range(E)]
+        for e in range(E):
+            for t in range(PACK):
+                nc.scalar.activation(picked[e][:, t, :], dc[t][:].indirect(entries(offs_t, e * C, (e + 1) * C)), ACT.Copy)
 
-        mask_of = {n: saved[n][:] for n in mine}
-        mask_and_gate = keep.tile([P, 2 * 384 + S // P], F32, name="mask_and_gate", tag="held", align_bytes=64)
-        slot_gate = mask_and_gate[:, 2 * 384 :]
+        woven = [keep.tile([P, C, PACK], BF16, name=f"woven{e}", align_bytes=64) for e in range(E)]
+        codes = [keep.tile([P, C], I32, name=f"codes{e}", align_bytes=64) for e in range(E)]
+        scales = [keep.tile([P, C], U8, name=f"scales{e}", align_bytes=64) for e in range(E)]
+        dx = [keep.tile([P, S], F32, name=f"dx{b}") for b in range(K // P)]
 
-        def make_mask(n):
-            lo, hi, t0, t1, who, heir = pieces[n]
-            if heir is None:
-                mask_of[n] = saved[n][:]
-            elif heir == (1, 2):
-                mask_of[n] = mask_and_gate[:, : 2 * 384].rearrange("p (t j) -> p t j", t=2)
-            elif heir == (2, 1):
-                mask_of[n] = keep.tile([P, t1 - t0, hi - lo], F32, name=f"mask{n}", tag="saved640_1", align_bytes=64)[:]
-            else:
-                mask_of[n] = keep.tile([P, t1 - t0, hi - lo], F32, name=f"mask{n}", tag="whole", align_bytes=64)[:]
-            nc.vector.tensor_scalar(mask_of[n], whole[:, t0:t1] if lo == 1280 else saved[n][:], 0.0, None, ALU.is_gt)
+        def fold(e):
+            spread = gates[e][:].unsqueeze(1).to_broadcast([P, PACK, C])
+            nc.vector.scalar_tensor_tensor(factor[e][:], factor[e][:], 0.0, spread, ALU.is_gt, ALU.mult)
 
-        late_masks = {}
-
-        def factor(t, lo, hi):
-            if lo == 1664:
-                return late_masks[t // 2][:, t % 2]
-            for n, (p_lo, p_hi, t0, t1, who, heir) in enumerate(pieces):
-                if p_lo <= lo and hi <= p_hi and t0 <= t < t1:
-                    return mask_of[n][:, t - t0, lo - p_lo : hi - p_lo]
-            raise ValueError("no piece")
-
-        def entries(lo, hi):
-            return offs_t[:, lo // LIST_ROWS : hi // LIST_ROWS]
-
-        for n, piece in enumerate(pieces):
-            if piece[4] == "vector" and piece[5] is None:
-                make_mask(n)
-        picked = {}
-
-        def gather_group(g):
-            lo, hi = GROUPS[g][0] * P, GROUPS[g][1] * P
-            for t in ORDER[g]:
-                for n, piece in enumerate(pieces):
-                    if piece[5] == (g, t):
-                        make_mask(n)
-                if (g, t) == (last_group, PACK - 1):
-                    spread = folded_gate[:].unsqueeze(1).to_broadcast([P, PACK, FOLDED])
-                    folded[0] = keep.tile([P, PACK, FOLDED], F32, name="folded", tag="late_mask0", align_bytes=64)
-                    nc.vector.scalar_tensor_tensor(folded[0][:], folded_saved[:], 0.0, spread, ALU.is_gt, ALU.mult)
-                picked[g, t] = keep.tile([P, hi - lo], F32, name=f"picked{g}_{t}", align_bytes=64)
-                nc.vector.tensor_tensor(picked[g, t][:], dc[t][:].indirect(entries(lo, hi)), factor(t, lo, hi), ALU.mult)
-
-        for g in range(last_group):
-            gather_group(g)
-        folded = {}
-
-        nc.scalar.copy(slot_gate, gate_bank[:, : S // P])
-        words = keep.tile([P, 2 * FOLD_LO], F32, name="words", align_bytes=64)
-        pairs = []
-        for first_block, end_block in GROUPS:
-            pairs.extend(list(range(b, min(b + 2, end_block))) for b in range(first_block, end_block, 2))
-        gated = {}
-
-        turned = {}
-
-        def turn(*units):
-            for first_block, end_block, at_bank in units:
-                unit = banks(f"turning{first_block}", at_bank, [P, end_block - first_block, PACK, P])
-                for blk in range(first_block, end_block):
-                    turned[blk] = unit[:, blk - first_block]
-            g = max(n for n, group in enumerate(GROUPS) if group[0] <= units[0][0])
-            for t in ORDER[g]:
-                for blk in range(units[0][0], units[-1][1]):
-                    at = (blk - GROUPS[g][0]) * P
-                    nc.tensor.transpose(turned[blk][:, t, :], picked[g, t][:, at : at + P], identity[:])
-
-        def apply_gate(k, j):
-            blk = pairs[k][j]
-            if j == 0:
-                gated[k] = keep.tile([P, len(pairs[k]), 2, P, 2], BF16, name=f"gated{k}", align_bytes=64)
-            nc.scalar.activation(
-                gated[k][:, j], turned[blk].rearrange("s (u r) p -> s u p r", r=2), ACT.Copy, scale=slot_gate[:, blk : blk + 1]
+        def weave(e):
+            nc.vector.tensor_tensor(
+                woven[e][:].rearrange("p (c i) t -> p c t i", i=RUN),
+                picked[e][:].rearrange("p t (c i) -> p c t i", i=RUN),
+                factor[e][:].rearrange("p t (c i) -> p c t i", i=RUN),
+                ALU.mult,
             )
 
-        def turn_back(k):
-            n = len(pairs[k])
-            bank = banks(f"returning{k}", single_at[k % 3], [P, n, 2, P])
-            for j in range(n):
-                row_pairs = gated[k][:, j].rearrange("s u p r -> s (u p r)").bitcast(F32)
-                for u in range(2):
-                    nc.tensor.transpose(bank[:, j, u, :], row_pairs[:, u * P : (u + 1) * P], identity[:])
-            return bank
+        def quantise(e):
+            nc.vector.quantize_mx(out=codes[e][:].bitcast(E5M2), scales=scales[e][:], in_=woven[e][:].rearrange("p c t -> p (c t)"))
 
-        def copy_back(k, bank):
-            n = len(pairs[k])
-            lo = 2 * P * pairs[k][0]
-            nc.scalar.copy(
-                words[:, lo : lo + 2 * P * n].rearrange("p (j s u) -> p j s u", j=n, u=2), bank[:].rearrange("p j u s -> p j s u")
-            )
-
-        turn((0, 4, 0), (4, 5, 4))
-        follows = {1: [(5, 7, 0), (7, 9, 2)], 2: [(9, 10, 4)], 3: [(10, 12, 0)], 5: [(12, 13, 4)], 6: [(13, 15, 0)]}
-        back = {}
-        for k in range(len(pairs)):
-            for j in range(len(pairs[k])):
-                apply_gate(k, j)
-            if k == 6:
-                copy_back(k - 2, back[k - 2])
-            if k > 0 and k != 5:
-                copy_back(k - 1, back[k - 1])
-            back[k] = turn_back(k)
-            if k == 1:
-                late_signs = keep.tile([P, 2, 2, 2 * P], BF16, name="late_signs", tag="gated0", align_bytes=64)
-                nc.scalar.activation(late_signs[:].rearrange("p u r j -> p (u r) j"), saved[-1][:], ACT.Sign)
-            if k == 2:
-                for u in range(2):
-                    late_masks[u] = keep.tile([P, 2, 2 * P], F32, name=f"late_mask{u}", align_bytes=64)
-                    nc.scalar.activation(late_masks[u][:], late_signs[:, u], ACT.Relu)
-                gather_group(last_group)
-                picked_folded = keep.tile([P, PACK, FOLDED], F32, name="picked_folded", align_bytes=64)
-                for t in range(PACK):
-                    nc.vector.tensor_tensor(picked_folded[:, t, :], dc[t][:].indirect(entries(FOLD_LO, FOLD_HI)), folded[0][:, t, :], ALU.mult)
-            if k in follows:
-                turn(*follows[k])
-        copy_back(len(pairs) - 1, back[len(pairs) - 1])
-        woven = keep.tile([P, FOLDED, PACK], BF16, name="woven", tag="held", align_bytes=64)
-        nc.scalar.copy(
-            woven[:].rearrange("p (c i) t -> p c t i", i=RUN), picked_folded[:].rearrange("p t (c i) -> p c t i", i=RUN)
-        )
-
-        codes = keep.tile([P, S], I32, name="codes", tag=f"gated{len(pairs) - 4}", align_bytes=64)
-        scales = keep.tile([P, S], U8, name="scales", align_bytes=64)
-
-        def quantise(lo, hi, values):
-            nc.vector.quantize_mx(out=codes[:, lo:hi].bitcast(E5M2), scales=scales[:, lo:hi], in_=values)
-
-        last = pairs[-1][0] * P
-        cuts = [0, C, 2 * C, 3 * C, last]
-        for lo, hi in zip(cuts, cuts[1:]):
-            quantise(lo, hi, words[:, 2 * lo : 2 * hi].bitcast(BF16))
-        quantise(FOLD_LO, FOLD_HI, woven[:].rearrange("p c t -> p (c t)"))
-        quantise(last, FOLD_LO, words[:, 2 * last :].bitcast(BF16))
-
-        dx = [
-            keep.tile([P, S], F32, name="dx0", tag="picked_folded", align_bytes=64),
-            keep.tile([P, S], F32, name="dx1", tag="w1_last", align_bytes=64),
-            keep.tile([P, S], F32, name="dx2"),
-            keep.tile([P, S], F32, name="dx3"),
-        ]
-        end = len(pairs) - 1
-        product_at = [1, single_at[(end - 1) % 3], single_at[end % 3], 0]
-        apart = {(E - 1, 0): w1_last[:], (E - 1, K // P - 1): w1_end[:]}
-        def multiply(b, e, lo, at):
-            product = banks(f"product{b}_{e}_{lo}", at, [P, BANK])
+        def multiply(b, e):
+            product = bank(f"product{b}_{e}", (PACK * e + b) % BANKS)
             nc.tensor.matmul_mx(
                 out=product[:],
-                lhsT=apart.get((e, b), w1[:, e, 2 * b * P : 2 * (b + 1) * P]).bitcast(E2M1),
+                lhsT=w1[:, e, 2 * b * P : 2 * (b + 1) * P].bitcast(E2M1),
                 lhsT_scale=w1s[:, e, b * P : (b + 1) * P],
-                rhs=codes[:, lo : lo + BANK].bitcast(E5M2),
-                rhs_scale=scales[:, lo : lo + BANK],
+                rhs=codes[e][:].bitcast(E5M2),
+                rhs_scale=scales[e][:],
                 start=True,
                 stop=True,
             )
             return product
 
-        for b in range(K // P):
-            for e in range(E):
-                lo = e * C
-                if (e, b) == (E - 2, 0):
-                    nc.vector.tensor_copy(dx[b][:, lo : lo + C], multiply(b, e, lo, product_at[e])[:])
+        fold(0)
+        for e in range(E):
+            weave(e)
+            if e + 1 < E:
+                fold(e + 1)
+            quantise(e)
+        for e in range(E):
+            for b in range(K // P):
+                if e == E - 1:
+                    nc.vector.tensor_copy(dx[b][:, e * C : (e + 1) * C], multiply(b, e)[:])
                 else:
-                    nc.scalar.copy(dx[b][:, lo : lo + C], multiply(b, e, lo, product_at[e])[:])
+                    nc.scalar.copy(dx[b][:, e * C : (e + 1) * C], multiply(b, e)[:])
 
-        first = [keep.tile([P, T], F32, name=f"first{b}") for b in range(K // P)]
-
-        def fetch_first(b, cuts):
+        halves = [0, T // 2, T]
+        for b in range(K // P):
+            first = [keep.tile([P, T // 2], F32, name=f"first{b}_{h}") for h in range(2)]
+            for h in range(2):
+                nc.scalar.activation(first[h][:], dx[b][:].indirect(entries(pos1_t, halves[h], halves[h + 1])), ACT.Copy)
+            cuts = TAIL_CUTS if b == K // P - 1 else halves
             for lo, hi in zip(cuts, cuts[1:]):
-                nc.vector.tensor_copy(first[b][:, lo:hi], dx[b][:].indirect(pos1_t[:, lo // LIST_ROWS : hi // LIST_ROWS]))
-
-        def add_second(b, cuts, tag=None):
-            for lo, hi in zip(cuts, cuts[1:]):
-                total = keep.tile([P, hi - lo], F32, name=f"res{b}_{lo}", tag=tag or f"res{b}_{lo}", align_bytes=64)
-                second = dx[b][:].indirect(pos2_t[:, lo // LIST_ROWS : hi // LIST_ROWS])
-                nc.vector.tensor_tensor(total[:], second, first[b][:, lo:hi], ALU.add)
+                total = keep.tile([P, hi - lo], F32, name=f"total{b}_{lo}", align_bytes=64)
+                h = lo // (T // 2)
+                at = lo - halves[h]
+                nc.vector.tensor_tensor(total[:], dx[b][:].indirect(entries(pos2_t, lo, hi)), first[h][:, at : at + hi - lo], ALU.add)
                 nc.sync.dma_start(out[b * P : (b + 1) * P, lo:hi], total[:])
-
-        token_halves = [0, T // 2, T]
-        fetch_first(0, token_halves)
-        add_second(0, token_halves)
-        fetch_first(1, [0, T])
-        fetch_first(2, [0, T])
-        add_second(1, [0, T], "w1_end")
-        fetch_first(3, [0, T])
-        add_second(2, [0, T])
-        add_second(3, TAIL_CUTS)

@@ -25,7 +25,8 @@ BANKS = 8
 BANK_BYTES = 2048
 LIST_ROWS = 16
 RUN = 2
-TAIL_CUTS = [0, 512, 832, 960, T]
+TAIL_CUTS = [0, 256, 512, 768, 960, T]
+GROUPS = [0, 448, 992, 1536, S]
 
 
 def tile_moe_sdb_relu_kernel(
@@ -66,13 +67,17 @@ def tile_moe_sdb_relu_kernel(
         nc.sync.dma_start(dy[:], dy_words[0].rearrange("p n t -> p (n t)").bitcast(I32))
         for q in range(QUADRANTS // 2, QUADRANTS):
             load_scale_rows(dys, dy_scales[0], q)
-        nc.sync.dma_start(offs_t[:], offs)
         a_planes = a.rearrange("(p t) j -> p t j", t=PACK)
-        factor = [keep.tile([P, PACK, C], F32, name=f"factor{e}", align_bytes=64) for e in range(E)]
-        gates = [keep.tile([P, C], F32, name=f"gates{e}", align_bytes=64) for e in range(E)]
-        for e in range(E):
-            nc.sync.dma_start(gates[e][:], gate[:, e * C : (e + 1) * C])
-            nc.sync.dma_start(factor[e][:], a_planes[:, :, e * C : (e + 1) * C])
+        groups = list(zip(GROUPS, GROUPS[1:]))
+        factor = [keep.tile([P, PACK, hi - lo], F32, name=f"factor{lo}", align_bytes=64) for lo, hi in groups]
+        gates = [keep.tile([P, hi - lo], F32, name=f"gates{lo}", align_bytes=64) for lo, hi in groups]
+        for g, (lo, hi) in enumerate(groups):
+            if g == 0:
+                nc.sync.dma_start(factor[g][:, :2], a_planes[:, :2, lo:hi])
+                nc.sync.dma_start(offs_t[:], offs)
+            nc.sync.dma_start(gates[g][:], gate[:, lo:hi])
+            first_plane = 2 if g == 0 else 0
+            nc.sync.dma_start(factor[g][:, first_plane:], a_planes[:, first_plane:, lo:hi])
         nc.sync.dma_start(w1[:].bitcast(I32), w1t_words[:, 0].rearrange("e p k -> p e k").bitcast(I32))
         for q in range(QUADRANTS):
             load_scale_rows(w1s, w1t_scales[:, 0].rearrange("e b k -> b e k"), q)
@@ -98,41 +103,45 @@ def tile_moe_sdb_relu_kernel(
                     start=True,
                     stop=True,
                 )
-                if h == 1 and t == 0:
-                    nc.scalar.copy(dc[t][:, cols], acc[:])
-                else:
-                    nc.vector.tensor_copy(dc[t][:, cols], acc[:])
+                nc.scalar.copy(dc[t][:, cols], acc[:])
 
         def entries(tile, lo, hi):
             return tile[:, lo // LIST_ROWS : hi // LIST_ROWS]
 
-        picked = [keep.tile([P, PACK, C], F32, name=f"picked{e}", align_bytes=64) for e in range(E)]
-        for e in range(E):
+        heirs = ["picked0", "dy", "w2", "dys"]
+        picked = [
+            keep.tile([P, PACK, hi - lo], F32, name=f"picked{g}", tag=heirs[g], align_bytes=64) for g, (lo, hi) in enumerate(groups)
+        ]
+        for g, (lo, hi) in enumerate(groups):
             for t in range(PACK):
-                nc.scalar.activation(picked[e][:, t, :], dc[t][:].indirect(entries(offs_t, e * C, (e + 1) * C)), ACT.Copy)
+                if g == 0:
+                    nc.vector.tensor_tensor(picked[g][:, t, :], dc[t][:].indirect(entries(offs_t, lo, hi)), gates[g][:], ALU.mult)
+                else:
+                    nc.scalar.activation(picked[g][:, t, :], dc[t][:].indirect(entries(offs_t, lo, hi)), ACT.Copy)
 
-        woven = [keep.tile([P, C, PACK], BF16, name=f"woven{e}", align_bytes=64) for e in range(E)]
+        woven = keep.tile([P, S * PACK], BF16, name="woven", align_bytes=64)
         codes = [keep.tile([P, C], I32, name=f"codes{e}", align_bytes=64) for e in range(E)]
         scales = [keep.tile([P, C], U8, name=f"scales{e}", align_bytes=64) for e in range(E)]
         dx = [keep.tile([P, S], F32, name=f"dx{b}") for b in range(K // P)]
 
-        def fold(e):
-            spread = gates[e][:].unsqueeze(1).to_broadcast([P, PACK, C])
-            nc.vector.scalar_tensor_tensor(factor[e][:], factor[e][:], 0.0, spread, ALU.is_gt, ALU.mult)
+        def fold(g):
+            spread = gates[g][:].unsqueeze(1).to_broadcast(list(factor[g].shape))
+            nc.vector.scalar_tensor_tensor(factor[g][:], factor[g][:], 0.0, spread, ALU.is_gt, ALU.mult)
 
-        def weave(e):
+        def weave(g):
+            lo, hi = groups[g]
             nc.vector.tensor_tensor(
-                woven[e][:].rearrange("p (c i) t -> p c t i", i=RUN),
-                picked[e][:].rearrange("p t (c i) -> p c t i", i=RUN),
-                factor[e][:].rearrange("p t (c i) -> p c t i", i=RUN),
+                woven[:, lo * PACK : hi * PACK].rearrange("p (c i t) -> p c t i", i=RUN, t=PACK),
+                picked[g][:].rearrange("p t (c i) -> p c t i", i=RUN),
+                factor[g][:].rearrange("p t (c i) -> p c t i", i=RUN),
                 ALU.mult,
             )
 
         def quantise(e):
-            nc.vector.quantize_mx(out=codes[e][:].bitcast(E5M2), scales=scales[e][:], in_=woven[e][:].rearrange("p c t -> p (c t)"))
+            nc.vector.quantize_mx(out=codes[e][:].bitcast(E5M2), scales=scales[e][:], in_=woven[:, e * C * PACK : (e + 1) * C * PACK])
 
         def multiply(b, e):
-            product = bank(f"product{b}_{e}", (PACK * e + b) % BANKS)
+            product = bank(f"product{b}_{e}", reused.get((e, b), PACK * e + b))
             nc.tensor.matmul_mx(
                 out=product[:],
                 lhsT=w1[:, e, 2 * b * P : 2 * (b + 1) * P].bitcast(E2M1),
@@ -144,28 +153,43 @@ def tile_moe_sdb_relu_kernel(
             )
             return product
 
-        fold(0)
-        for e in range(E):
-            weave(e)
-            if e + 1 < E:
-                fold(e + 1)
-            quantise(e)
+        for lo in (0, 2):
+            nc.vector.tensor_scalar(factor[0][:, lo : lo + 2], factor[0][:, lo : lo + 2], 0.0, None, ALU.is_gt)
+        weave(0)
+        fold(1)
+        weave(1)
+        fold(2)
+        quantise(0)
+        weave(2)
+        fold(3)
+        quantise(1)
+        quantise(2)
+        weave(3)
+        quantise(3)
+        on_vector = [(2, 2), (3, 0), (3, 1), (3, 2)]
+        late = [(3, 3)]
+        reused = {(2, 0): 0, (2, 1): 1, (2, 2): 2, (2, 3): 3, (3, 0): 4, (3, 1): 5, (3, 2): 6, (3, 3): 5}
+
+        def empty(e, b):
+            if (e, b) in on_vector:
+                nc.vector.tensor_copy(dx[b][:, e * C : (e + 1) * C], multiply(b, e)[:])
+            else:
+                nc.scalar.copy(dx[b][:, e * C : (e + 1) * C], multiply(b, e)[:])
+
         for e in range(E):
             for b in range(K // P):
-                if e == E - 1:
-                    nc.vector.tensor_copy(dx[b][:, e * C : (e + 1) * C], multiply(b, e)[:])
-                else:
-                    nc.scalar.copy(dx[b][:, e * C : (e + 1) * C], multiply(b, e)[:])
+                if (e, b) not in late:
+                    empty(e, b)
 
         halves = [0, T // 2, T]
         for b in range(K // P):
-            first = [keep.tile([P, T // 2], F32, name=f"first{b}_{h}") for h in range(2)]
-            for h in range(2):
-                nc.scalar.activation(first[h][:], dx[b][:].indirect(entries(pos1_t, halves[h], halves[h + 1])), ACT.Copy)
+            if b == K // P - 1:
+                for e, row_block in late:
+                    empty(e, row_block)
             cuts = TAIL_CUTS if b == K // P - 1 else halves
             for lo, hi in zip(cuts, cuts[1:]):
+                first = keep.tile([P, hi - lo], F32, name=f"first{b}_{lo}")
+                nc.scalar.activation(first[:], dx[b][:].indirect(entries(pos1_t, lo, hi)), ACT.Copy)
                 total = keep.tile([P, hi - lo], F32, name=f"total{b}_{lo}", align_bytes=64)
-                h = lo // (T // 2)
-                at = lo - halves[h]
-                nc.vector.tensor_tensor(total[:], dx[b][:].indirect(entries(pos2_t, lo, hi)), first[h][:, at : at + hi - lo], ALU.add)
+                nc.vector.tensor_tensor(total[:], dx[b][:].indirect(entries(pos2_t, lo, hi)), first[:], ALU.add)
                 nc.sync.dma_start(out[b * P : (b + 1) * P, lo:hi], total[:])

@@ -26,7 +26,6 @@ BANK_BYTES = 2048
 LIST_ROWS = 16
 RUN = 2
 TAIL_CUTS = [0, 256, 512, 768, 960, T]
-GROUPS = [0, 448, 992, 1536, S]
 
 
 def tile_moe_sdb_relu_kernel(
@@ -35,6 +34,7 @@ def tile_moe_sdb_relu_kernel(
     nc = tc.nc
     with ExitStack() as ctx:
         keep = ctx.enter_context(tc.tile_pool(name="keep", bufs=1))
+        overlay = ctx.enter_context(tc.tile_pool(name="overlay", bufs=1))
         psum = ctx.enter_context(tc.psum_pool(name="psum", bufs=1))
 
         def bank(name, at):
@@ -54,6 +54,11 @@ def tile_moe_sdb_relu_kernel(
         w1s = keep.tile([P, E, K], U8, name="w1s", align_bytes=64)
         dc = [keep.tile([P, T], F32, name=f"dc{t}") for t in range(PACK)]
 
+        identity = keep.tile([P, P], F32, name="identity")
+        distance = keep.tile([P, P], F32, name="distance")
+        nc.gpsimd.iota(distance[:], [[1, P]], base=0, channel_multiplier=-1, allow_small_or_imprecise_dtypes=True)
+        nc.gpsimd.tensor_scalar(identity[:], distance[:], 0.0, 1.0, ALU.is_equal, ALU.mult)
+
         nc.vector.memset(w2s_raw[:].bitcast(I32), 0)
 
         def load_scale_rows(tile, rows, q):
@@ -68,16 +73,18 @@ def tile_moe_sdb_relu_kernel(
         for q in range(QUADRANTS // 2, QUADRANTS):
             load_scale_rows(dys, dy_scales[0], q)
         a_planes = a.rearrange("(p t) j -> p t j", t=PACK)
-        groups = list(zip(GROUPS, GROUPS[1:]))
-        factor = [keep.tile([P, PACK, hi - lo], F32, name=f"factor{lo}", align_bytes=64) for lo, hi in groups]
-        gates = [keep.tile([P, hi - lo], F32, name=f"gates{lo}", align_bytes=64) for lo, hi in groups]
-        for g, (lo, hi) in enumerate(groups):
-            if g == 0:
-                nc.sync.dma_start(factor[g][:, :2], a_planes[:, :2, lo:hi])
-                nc.sync.dma_start(offs_t[:], offs)
-            nc.sync.dma_start(gates[g][:], gate[:, lo:hi])
-            first_plane = 2 if g == 0 else 0
-            nc.sync.dma_start(factor[g][:, first_plane:], a_planes[:, first_plane:, lo:hi])
+        groups = [(e * C, (e + 1) * C) for e in range(E)]
+        factor = [keep.tile([P, PACK, C], F32, name=f"factor{e}", align_bytes=64) for e in range(E)]
+        saved = factor[: E - 1] + [overlay.tile([P, PACK, C], F32, name="saved_last", offset=4096, align_bytes=64)]
+        first_gate = keep.tile([P, C], F32, name="first_gate", align_bytes=64)
+        gate_rows = keep.tile([P, P], F32, name="gate_rows")
+        nc.sync.dma_start(saved[0][:, :2], a_planes[:, :2, :C])
+        nc.sync.dma_start(offs_t[:], offs)
+        nc.sync.dma_start(first_gate[:], gate[:, :C])
+        nc.sync.dma_start(gate_rows[:], gate[: P * P // S].rearrange("r (c j) -> (r c) j", j=P))
+        nc.sync.dma_start(saved[0][:, 2:], a_planes[:, 2:, :C])
+        for e in range(1, E):
+            nc.sync.dma_start(saved[e][:], a_planes[:, :, e * C : (e + 1) * C])
         nc.sync.dma_start(w1[:].bitcast(I32), w1t_words[:, 0].rearrange("e p k -> p e k").bitcast(I32))
         for q in range(QUADRANTS):
             load_scale_rows(w1s, w1t_scales[:, 0].rearrange("e b k -> b e k"), q)
@@ -93,7 +100,7 @@ def tile_moe_sdb_relu_kernel(
         for t in range(PACK):
             for h in range(T // BANK):
                 cols = slice(h * BANK, (h + 1) * BANK)
-                acc = bank(f"acc{t}_{h}", 2 * t + h)
+                acc = bank(f"acc{t}_{h}", (2 * t + h) % 5)
                 nc.tensor.matmul_mx(
                     out=acc[:],
                     lhsT=w2[:, t * P : (t + 1) * P].bitcast(E4M3),
@@ -104,6 +111,15 @@ def tile_moe_sdb_relu_kernel(
                     stop=True,
                 )
                 nc.scalar.copy(dc[t][:, cols], acc[:])
+
+        turned = bank("turned", 3)
+        nc.tensor.transpose(turned[:, :P], gate_rows[:], identity[:])
+        gate_columns = keep.tile([P, S // P], F32, name="gate_columns")
+        nc.vector.tensor_copy(gate_columns[:], turned[:, : S // P])
+        gates = [first_gate] + [bank(f"gates{e}", 4 + e) for e in range(1, E)]
+        for blk in range(C // P, S // P):
+            e, at = divmod(blk * P, C)
+            nc.tensor.transpose(gates[e][:, at : at + P], gate_columns[:, blk : blk + 1].to_broadcast([P, P]), identity[:])
 
         def entries(tile, lo, hi):
             return tile[:, lo // LIST_ROWS : hi // LIST_ROWS]
@@ -119,26 +135,25 @@ def tile_moe_sdb_relu_kernel(
                 else:
                     nc.scalar.activation(picked[g][:, t, :], dc[t][:].indirect(entries(offs_t, lo, hi)), ACT.Copy)
 
-        woven = keep.tile([P, S * PACK], BF16, name="woven", align_bytes=64)
-        codes = [keep.tile([P, C], I32, name=f"codes{e}", align_bytes=64) for e in range(E)]
+        woven = {0: keep.tile([P, C * PACK], BF16, name="woven0", align_bytes=64)}
+        codes = {e: keep.tile([P, C], I32, name=f"codes{e}", align_bytes=64) for e in (2, 3)}
         scales = [keep.tile([P, C], U8, name=f"scales{e}", align_bytes=64) for e in range(E)]
         dx = [keep.tile([P, S], F32, name=f"dx{b}") for b in range(K // P)]
 
         def fold(g):
             spread = gates[g][:].unsqueeze(1).to_broadcast(list(factor[g].shape))
-            nc.vector.scalar_tensor_tensor(factor[g][:], factor[g][:], 0.0, spread, ALU.is_gt, ALU.mult)
+            nc.vector.scalar_tensor_tensor(factor[g][:], saved[g][:], 0.0, spread, ALU.is_gt, ALU.mult)
 
-        def weave(g):
-            lo, hi = groups[g]
-            nc.vector.tensor_tensor(
-                woven[:, lo * PACK : hi * PACK].rearrange("p (c i t) -> p c t i", i=RUN, t=PACK),
+        def weave(engine, g):
+            engine.tensor_tensor(
+                woven[g][:].rearrange("p (c i t) -> p c t i", i=RUN, t=PACK),
                 picked[g][:].rearrange("p t (c i) -> p c t i", i=RUN),
                 factor[g][:].rearrange("p t (c i) -> p c t i", i=RUN),
                 ALU.mult,
             )
 
         def quantise(e):
-            nc.vector.quantize_mx(out=codes[e][:].bitcast(E5M2), scales=scales[e][:], in_=woven[:, e * C * PACK : (e + 1) * C * PACK])
+            nc.vector.quantize_mx(out=codes[e][:].bitcast(E5M2), scales=scales[e][:], in_=woven[e][:])
 
         def multiply(b, e):
             product = bank(f"product{b}_{e}", reused.get((e, b), PACK * e + b))
@@ -155,18 +170,23 @@ def tile_moe_sdb_relu_kernel(
 
         for lo in (0, 2):
             nc.vector.tensor_scalar(factor[0][:, lo : lo + 2], factor[0][:, lo : lo + 2], 0.0, None, ALU.is_gt)
-        weave(0)
         fold(1)
-        weave(1)
+        weave(nc.vector, 0)
+        woven[1] = keep.tile([P, C * PACK], BF16, name="woven1", tag="picked0", align_bytes=64)
+        weave(nc.gpsimd, 1)
         fold(2)
-        quantise(0)
-        weave(2)
         fold(3)
+        woven[3] = overlay.tile([P, C * PACK], BF16, name="woven3", offset=12288, align_bytes=64)
+        woven[2] = overlay.tile([P, C * PACK], BF16, name="woven2", offset=4096, align_bytes=64)
+        codes[0] = overlay.tile([P, C], I32, name="codes0", offset=8192, align_bytes=64)
+        codes[1] = overlay.tile([P, C], I32, name="codes1", offset=10240, align_bytes=64)
+        quantise(0)
+        weave(nc.vector, 2)
         quantise(1)
         quantise(2)
-        weave(3)
+        weave(nc.vector, 3)
         quantise(3)
-        on_vector = [(2, 2), (3, 0), (3, 1), (3, 2)]
+        on_vector = [(2, 2), (2, 3), (3, 0), (3, 1), (3, 2)]
         late = [(3, 3)]
         reused = {(2, 0): 0, (2, 1): 1, (2, 2): 2, (2, 3): 3, (3, 0): 4, (3, 1): 5, (3, 2): 6, (3, 3): 5}
 

@@ -54,12 +54,12 @@ def tile_moe_sdb_relu_kernel(
         w1s = keep.tile([P, E, K], U8, name="w1s", align_bytes=64)
         dc = [keep.tile([P, T], F32, name=f"dc{t}") for t in range(PACK)]
 
+        nc.gpsimd.memset(w2s_raw[:].bitcast(I32), 0)
         identity = keep.tile([P, P], F32, name="identity")
         distance = keep.tile([P, P], F32, name="distance")
         nc.gpsimd.iota(distance[:], [[1, P]], base=0, channel_multiplier=-1, allow_small_or_imprecise_dtypes=True)
         nc.gpsimd.tensor_scalar(identity[:], distance[:], 0.0, 1.0, ALU.is_equal, ALU.mult)
 
-        nc.vector.memset(w2s_raw[:].bitcast(I32), 0)
 
         def load_scale_rows(tile, rows, q):
             nc.sync.dma_start(tile[32 * q : 32 * q + 4].bitcast(I32), rows[4 * q : 4 * q + 4].bitcast(I32))
@@ -76,13 +76,14 @@ def tile_moe_sdb_relu_kernel(
         groups = [(e * C, (e + 1) * C) for e in range(E)]
         factor = [keep.tile([P, PACK, C], F32, name=f"factor{e}", align_bytes=64) for e in range(E)]
         saved = factor[: E - 1] + [overlay.tile([P, PACK, C], F32, name="saved_last", offset=4096, align_bytes=64)]
-        first_gate = keep.tile([P, C], F32, name="first_gate", align_bytes=64)
         gate_rows = keep.tile([P, P], F32, name="gate_rows")
-        nc.sync.dma_start(saved[0][:, :2], a_planes[:, :2, :C])
-        nc.sync.dma_start(offs_t[:], offs)
-        nc.sync.dma_start(first_gate[:], gate[:, :C])
-        nc.sync.dma_start(gate_rows[:], gate[: P * P // S].rearrange("r (c j) -> (r c) j", j=P))
-        nc.sync.dma_start(saved[0][:, 2:], a_planes[:, 2:, :C])
+        pieces = [(0, 1), (1, 2), (2, PACK)]
+        for t0, t1 in pieces:
+            nc.sync.dma_start(saved[0][:, t0:t1], a_planes[:, t0:t1, :C])
+            if t0 == 0:
+                nc.sync.dma_start(offs_t[:], offs)
+            if t0 == 1:
+                nc.sync.dma_start(gate_rows[:], gate[: P * P // S].rearrange("r (c j) -> (r c) j", j=P))
         for e in range(1, E):
             nc.sync.dma_start(saved[e][:], a_planes[:, :, e * C : (e + 1) * C])
         nc.sync.dma_start(w1[:].bitcast(I32), w1t_words[:, 0].rearrange("e p k -> p e k").bitcast(I32))
@@ -100,7 +101,7 @@ def tile_moe_sdb_relu_kernel(
         for t in range(PACK):
             for h in range(T // BANK):
                 cols = slice(h * BANK, (h + 1) * BANK)
-                acc = bank(f"acc{t}_{h}", (2 * t + h) % 5)
+                acc = bank(f"acc{t}_{h}", (2 * t + h) % 4)
                 nc.tensor.matmul_mx(
                     out=acc[:],
                     lhsT=w2[:, t * P : (t + 1) * P].bitcast(E4M3),
@@ -112,14 +113,17 @@ def tile_moe_sdb_relu_kernel(
                 )
                 nc.scalar.copy(dc[t][:, cols], acc[:])
 
-        turned = bank("turned", 3)
+        turned = bank("turned", 0)
         nc.tensor.transpose(turned[:, :P], gate_rows[:], identity[:])
         gate_columns = keep.tile([P, S // P], F32, name="gate_columns")
-        nc.vector.tensor_copy(gate_columns[:], turned[:, : S // P])
-        gates = [first_gate] + [bank(f"gates{e}", 4 + e) for e in range(1, E)]
-        for blk in range(C // P, S // P):
-            e, at = divmod(blk * P, C)
-            nc.tensor.transpose(gates[e][:, at : at + P], gate_columns[:, blk : blk + 1].to_broadcast([P, P]), identity[:])
+        nc.scalar.copy(gate_columns[:], turned[:, : S // P])
+        gates = [bank(f"gates{e}", 4 + e) for e in range(E)]
+        for e in (1, 0, 2, 3):
+            for at in range(0, C, P):
+                blk = (e * C + at) // P
+                nc.tensor.transpose(gates[e][:, at : at + P], gate_columns[:, blk : blk + 1].to_broadcast([P, P]), identity[:])
+        for t0, t1 in pieces:
+            nc.vector.tensor_scalar(factor[0][:, t0:t1], saved[0][:, t0:t1], 0.0, None, ALU.is_gt)
 
         def entries(tile, lo, hi):
             return tile[:, lo // LIST_ROWS : hi // LIST_ROWS]
@@ -131,7 +135,7 @@ def tile_moe_sdb_relu_kernel(
         for g, (lo, hi) in enumerate(groups):
             for t in range(PACK):
                 if g == 0:
-                    nc.vector.tensor_tensor(picked[g][:, t, :], dc[t][:].indirect(entries(offs_t, lo, hi)), gates[g][:], ALU.mult)
+                    nc.vector.tensor_tensor(picked[g][:, t, :], dc[t][:].indirect(entries(offs_t, lo, hi)), factor[g][:, t, :], ALU.mult)
                 else:
                     nc.scalar.activation(picked[g][:, t, :], dc[t][:].indirect(entries(offs_t, lo, hi)), ACT.Copy)
 
@@ -145,10 +149,11 @@ def tile_moe_sdb_relu_kernel(
             nc.vector.scalar_tensor_tensor(factor[g][:], saved[g][:], 0.0, spread, ALU.is_gt, ALU.mult)
 
         def weave(engine, g):
+            other = factor[g][:] if g > 0 else gates[g][:].unsqueeze(1).to_broadcast([P, PACK, C])
             engine.tensor_tensor(
                 woven[g][:].rearrange("p (c i t) -> p c t i", i=RUN, t=PACK),
                 picked[g][:].rearrange("p t (c i) -> p c t i", i=RUN),
-                factor[g][:].rearrange("p t (c i) -> p c t i", i=RUN),
+                other.rearrange("p t (c i) -> p c t i", i=RUN),
                 ALU.mult,
             )
 
@@ -168,11 +173,9 @@ def tile_moe_sdb_relu_kernel(
             )
             return product
 
-        for lo in (0, 2):
-            nc.vector.tensor_scalar(factor[0][:, lo : lo + 2], factor[0][:, lo : lo + 2], 0.0, None, ALU.is_gt)
         fold(1)
         weave(nc.vector, 0)
-        woven[1] = keep.tile([P, C * PACK], BF16, name="woven1", tag="picked0", align_bytes=64)
+        woven[1] = keep.tile([P, C * PACK], BF16, name="woven1", align_bytes=64)
         weave(nc.gpsimd, 1)
         fold(2)
         fold(3)

@@ -21,10 +21,14 @@ P = 128
 PACK = 4
 QUADRANTS = 4
 BANK = 512
-BANKS = 8
 BANK_BYTES = 2048
+DC_BANKS = 4
 LIST_ROWS = 16
-RUN = 2
+ROW_BLOCKS = K // P
+RUN = 4
+KIB = 1024
+
+HALVES = [0, T // 2, T]
 TAIL_CUTS = [0, 256, 512, 768, 960, T]
 
 
@@ -55,11 +59,11 @@ def tile_moe_sdb_relu_kernel(
         dc = [keep.tile([P, T], F32, name=f"dc{t}") for t in range(PACK)]
 
         nc.gpsimd.memset(w2s_raw[:].bitcast(I32), 0)
+
         identity = keep.tile([P, P], F32, name="identity")
         distance = keep.tile([P, P], F32, name="distance")
         nc.gpsimd.iota(distance[:], [[1, P]], base=0, channel_multiplier=-1, allow_small_or_imprecise_dtypes=True)
         nc.gpsimd.tensor_scalar(identity[:], distance[:], 0.0, 1.0, ALU.is_equal, ALU.mult)
-
 
         def load_scale_rows(tile, rows, q):
             nc.sync.dma_start(tile[32 * q : 32 * q + 4].bitcast(I32), rows[4 * q : 4 * q + 4].bitcast(I32))
@@ -72,13 +76,13 @@ def tile_moe_sdb_relu_kernel(
         nc.sync.dma_start(dy[:], dy_words[0].rearrange("p n t -> p (n t)").bitcast(I32))
         for q in range(QUADRANTS // 2, QUADRANTS):
             load_scale_rows(dys, dy_scales[0], q)
+
         a_planes = a.rearrange("(p t) j -> p t j", t=PACK)
-        groups = [(e * C, (e + 1) * C) for e in range(E)]
         factor = [keep.tile([P, PACK, C], F32, name=f"factor{e}", align_bytes=64) for e in range(E)]
-        saved = factor[: E - 1] + [overlay.tile([P, PACK, C], F32, name="saved_last", offset=4096, align_bytes=64)]
+        saved = factor[: E - 1] + [overlay.tile([P, PACK, C], F32, name="saved_last", offset=4 * KIB, align_bytes=64)]
         gate_rows = keep.tile([P, P], F32, name="gate_rows")
-        pieces = [(0, 1), (1, 2), (2, PACK)]
-        for t0, t1 in pieces:
+        plane_pieces = [(0, 1), (1, 2), (2, PACK)]
+        for t0, t1 in plane_pieces:
             nc.sync.dma_start(saved[0][:, t0:t1], a_planes[:, t0:t1, :C])
             if t0 == 0:
                 nc.sync.dma_start(offs_t[:], offs)
@@ -93,15 +97,15 @@ def tile_moe_sdb_relu_kernel(
         nc.sync.dma_start(pos2_t[:], pos2)
 
         nc.vector.tensor_copy(w2[:].rearrange("p (t m) -> p t m", t=PACK), w2_raw[:].rearrange("p (m t) -> p t m", t=PACK))
-        for lo, hi in ((0, 1), (1, PACK)):
+        for t0, t1 in ((0, 1), (1, PACK)):
             nc.vector.tensor_copy(
-                w2s[:].rearrange("p (t m) -> p t m", t=PACK)[:, lo:hi], w2s_raw[:].rearrange("p (m t) -> p t m", t=PACK)[:, lo:hi]
+                w2s[:].rearrange("p (t m) -> p t m", t=PACK)[:, t0:t1], w2s_raw[:].rearrange("p (m t) -> p t m", t=PACK)[:, t0:t1]
             )
 
         for t in range(PACK):
             for h in range(T // BANK):
                 cols = slice(h * BANK, (h + 1) * BANK)
-                acc = bank(f"acc{t}_{h}", (2 * t + h) % 4)
+                acc = bank(f"acc{t}_{h}", (2 * t + h) % DC_BANKS)
                 nc.tensor.matmul_mx(
                     out=acc[:],
                     lhsT=w2[:, t * P : (t + 1) * P].bitcast(E4M3),
@@ -111,48 +115,53 @@ def tile_moe_sdb_relu_kernel(
                     start=True,
                     stop=True,
                 )
-                nc.scalar.copy(dc[t][:, cols], acc[:])
+                if (t, h) == (0, 0):
+                    nc.vector.tensor_copy(dc[t][:, cols], acc[:])
+                else:
+                    nc.scalar.copy(dc[t][:, cols], acc[:])
 
         turned = bank("turned", 0)
         nc.tensor.transpose(turned[:, :P], gate_rows[:], identity[:])
         gate_columns = keep.tile([P, S // P], F32, name="gate_columns")
         nc.scalar.copy(gate_columns[:], turned[:, : S // P])
-        gates = [bank(f"gates{e}", 4 + e) for e in range(E)]
+        gates = [bank(f"gates{e}", DC_BANKS + e) for e in range(E)]
         for e in (1, 0, 2, 3):
             for at in range(0, C, P):
                 blk = (e * C + at) // P
                 nc.tensor.transpose(gates[e][:, at : at + P], gate_columns[:, blk : blk + 1].to_broadcast([P, P]), identity[:])
-        for t0, t1 in pieces:
+
+        for t0, t1 in plane_pieces:
             nc.vector.tensor_scalar(factor[0][:, t0:t1], saved[0][:, t0:t1], 0.0, None, ALU.is_gt)
 
         def entries(tile, lo, hi):
             return tile[:, lo // LIST_ROWS : hi // LIST_ROWS]
 
-        heirs = ["picked0", "dy", "w2", "dys"]
-        picked = [
-            keep.tile([P, PACK, hi - lo], F32, name=f"picked{g}", tag=heirs[g], align_bytes=64) for g, (lo, hi) in enumerate(groups)
-        ]
-        for g, (lo, hi) in enumerate(groups):
+        tags = ["picked0", "dy", "w2", "dys"]
+        picked = [keep.tile([P, PACK, C], F32, name=f"picked{e}", tag=tags[e], align_bytes=64) for e in range(E)]
+        for e in range(E):
             for t in range(PACK):
-                if g == 0:
-                    nc.vector.tensor_tensor(picked[g][:, t, :], dc[t][:].indirect(entries(offs_t, lo, hi)), factor[g][:, t, :], ALU.mult)
+                window = dc[t][:].indirect(entries(offs_t, e * C, (e + 1) * C))
+                if e == 0:
+                    nc.vector.tensor_tensor(picked[e][:, t, :], window, factor[e][:, t, :], ALU.mult)
                 else:
-                    nc.scalar.activation(picked[g][:, t, :], dc[t][:].indirect(entries(offs_t, lo, hi)), ACT.Copy)
+                    nc.scalar.activation(picked[e][:, t, :], window, ACT.Copy)
 
         woven = {0: keep.tile([P, C * PACK], BF16, name="woven0", align_bytes=64)}
         codes = {e: keep.tile([P, C], I32, name=f"codes{e}", align_bytes=64) for e in (2, 3)}
         scales = [keep.tile([P, C], U8, name=f"scales{e}", align_bytes=64) for e in range(E)]
-        dx = [keep.tile([P, S], F32, name=f"dx{b}") for b in range(K // P)]
+        dx = [keep.tile([P, S], F32, name=f"dx{b}") for b in range(ROW_BLOCKS)]
 
-        def fold(g):
-            spread = gates[g][:].unsqueeze(1).to_broadcast(list(factor[g].shape))
-            nc.vector.scalar_tensor_tensor(factor[g][:], saved[g][:], 0.0, spread, ALU.is_gt, ALU.mult)
+        def gate_planes(e):
+            return gates[e][:].unsqueeze(1).to_broadcast([P, PACK, C])
 
-        def weave(engine, g):
-            other = factor[g][:] if g > 0 else gates[g][:].unsqueeze(1).to_broadcast([P, PACK, C])
+        def fold(e):
+            nc.vector.scalar_tensor_tensor(factor[e][:], saved[e][:], 0.0, gate_planes(e), ALU.is_gt, ALU.mult)
+
+        def weave(engine, e):
+            other = gate_planes(e) if e == 0 else factor[e][:]
             engine.tensor_tensor(
-                woven[g][:].rearrange("p (c i t) -> p c t i", i=RUN, t=PACK),
-                picked[g][:].rearrange("p t (c i) -> p c t i", i=RUN),
+                woven[e][:].rearrange("p (c i t) -> p c t i", i=RUN, t=PACK),
+                picked[e][:].rearrange("p t (c i) -> p c t i", i=RUN),
                 other.rearrange("p t (c i) -> p c t i", i=RUN),
                 ALU.mult,
             )
@@ -160,8 +169,28 @@ def tile_moe_sdb_relu_kernel(
         def quantise(e):
             nc.vector.quantize_mx(out=codes[e][:].bitcast(E5M2), scales=scales[e][:], in_=woven[e][:])
 
-        def multiply(b, e):
-            product = bank(f"product{b}_{e}", reused.get((e, b), PACK * e + b))
+        fold(1)
+        weave(nc.vector, 0)
+        woven[1] = keep.tile([P, C * PACK], BF16, name="woven1", align_bytes=64)
+        weave(nc.gpsimd, 1)
+        fold(2)
+        fold(3)
+        woven[3] = overlay.tile([P, C * PACK], BF16, name="woven3", offset=12 * KIB, align_bytes=64)
+        woven[2] = overlay.tile([P, C * PACK], BF16, name="woven2", offset=4 * KIB, align_bytes=64)
+        codes[0] = overlay.tile([P, C], I32, name="codes0", offset=8 * KIB, align_bytes=64)
+        codes[1] = overlay.tile([P, C], I32, name="codes1", offset=10 * KIB, align_bytes=64)
+        quantise(0)
+        weave(nc.vector, 2)
+        quantise(1)
+        quantise(2)
+        weave(nc.vector, 3)
+        quantise(3)
+
+        last = (E - 1, ROW_BLOCKS - 1)
+
+        def multiply(e, b):
+            at = (ROW_BLOCKS * e + b) % (2 * ROW_BLOCKS) if (e, b) != last else ROW_BLOCKS + 1
+            product = bank(f"product{b}_{e}", at)
             nc.tensor.matmul_mx(
                 out=product[:],
                 lhsT=w1[:, e, 2 * b * P : 2 * (b + 1) * P].bitcast(E2M1),
@@ -173,43 +202,29 @@ def tile_moe_sdb_relu_kernel(
             )
             return product
 
-        fold(1)
-        weave(nc.vector, 0)
-        woven[1] = keep.tile([P, C * PACK], BF16, name="woven1", align_bytes=64)
-        weave(nc.gpsimd, 1)
-        fold(2)
-        fold(3)
-        woven[3] = overlay.tile([P, C * PACK], BF16, name="woven3", offset=12288, align_bytes=64)
-        woven[2] = overlay.tile([P, C * PACK], BF16, name="woven2", offset=4096, align_bytes=64)
-        codes[0] = overlay.tile([P, C], I32, name="codes0", offset=8192, align_bytes=64)
-        codes[1] = overlay.tile([P, C], I32, name="codes1", offset=10240, align_bytes=64)
-        quantise(0)
-        weave(nc.vector, 2)
-        quantise(1)
-        quantise(2)
-        weave(nc.vector, 3)
-        quantise(3)
-        on_vector = [(2, 2), (2, 3), (3, 0), (3, 1), (3, 2)]
-        late = [(3, 3)]
-        reused = {(2, 0): 0, (2, 1): 1, (2, 2): 2, (2, 3): 3, (3, 0): 4, (3, 1): 5, (3, 2): 6, (3, 3): 5}
+        on_vector = [(2, 3), (3, 0), (3, 1), (3, 2)]
+        halved = (2, 2)
 
         def empty(e, b):
-            if (e, b) in on_vector:
-                nc.vector.tensor_copy(dx[b][:, e * C : (e + 1) * C], multiply(b, e)[:])
+            product = multiply(e, b)
+            slots = dx[b][:, e * C : (e + 1) * C]
+            if (e, b) == halved:
+                nc.vector.tensor_copy(slots[:, : C // 2], product[:, : C // 2])
+                nc.scalar.copy(slots[:, C // 2 :], product[:, C // 2 :])
+            elif (e, b) in on_vector:
+                nc.vector.tensor_copy(slots, product[:])
             else:
-                nc.scalar.copy(dx[b][:, e * C : (e + 1) * C], multiply(b, e)[:])
+                nc.scalar.copy(slots, product[:])
 
         for e in range(E):
-            for b in range(K // P):
-                if (e, b) not in late:
+            for b in range(ROW_BLOCKS):
+                if (e, b) != last:
                     empty(e, b)
 
-        halves = [0, T // 2, T]
-        for b in range(K // P):
-            if b == K // P - 1:
-                for e, row_block in late:
-                    empty(e, row_block)
-            cuts = TAIL_CUTS if b == K // P - 1 else halves
+        for b in range(ROW_BLOCKS):
+            if b == ROW_BLOCKS - 1:
+                empty(*last)
+            cuts = TAIL_CUTS if b == ROW_BLOCKS - 1 else HALVES
             for lo, hi in zip(cuts, cuts[1:]):
                 first = keep.tile([P, hi - lo], F32, name=f"first{b}_{lo}")
                 nc.scalar.activation(first[:], dx[b][:].indirect(entries(pos1_t, lo, hi)), ACT.Copy)

@@ -25,7 +25,7 @@ BANK_BYTES = 2048
 DC_BANKS = 4
 LIST_ROWS = 16
 ROW_BLOCKS = K // P
-RUN = 4
+VECTOR_RUN, GPSIMD_RUN = 8, 4
 KIB = 1024
 
 HALVES = [0, T // 2, T]
@@ -157,12 +157,12 @@ def tile_moe_sdb_relu_kernel(
         def fold(e):
             nc.vector.scalar_tensor_tensor(factor[e][:], saved[e][:], 0.0, gate_planes(e), ALU.is_gt, ALU.mult)
 
-        def weave(engine, e):
+        def weave(engine, run, e):
             other = gate_planes(e) if e == 0 else factor[e][:]
             engine.tensor_tensor(
-                woven[e][:].rearrange("p (c i t) -> p c t i", i=RUN, t=PACK),
-                picked[e][:].rearrange("p t (c i) -> p c t i", i=RUN),
-                other.rearrange("p t (c i) -> p c t i", i=RUN),
+                woven[e][:].rearrange("p (c i t) -> p c t i", i=run, t=PACK),
+                picked[e][:].rearrange("p t (c i) -> p c t i", i=run),
+                other.rearrange("p t (c i) -> p c t i", i=run),
                 ALU.mult,
             )
 
@@ -170,9 +170,9 @@ def tile_moe_sdb_relu_kernel(
             nc.vector.quantize_mx(out=codes[e][:].bitcast(E5M2), scales=scales[e][:], in_=woven[e][:])
 
         fold(1)
-        weave(nc.vector, 0)
+        weave(nc.vector, VECTOR_RUN, 0)
         woven[1] = keep.tile([P, C * PACK], BF16, name="woven1", align_bytes=64)
-        weave(nc.gpsimd, 1)
+        weave(nc.gpsimd, GPSIMD_RUN, 1)
         fold(2)
         fold(3)
         woven[3] = overlay.tile([P, C * PACK], BF16, name="woven3", offset=12 * KIB, align_bytes=64)
@@ -180,10 +180,10 @@ def tile_moe_sdb_relu_kernel(
         codes[0] = overlay.tile([P, C], I32, name="codes0", offset=8 * KIB, align_bytes=64)
         codes[1] = overlay.tile([P, C], I32, name="codes1", offset=10 * KIB, align_bytes=64)
         quantise(0)
-        weave(nc.vector, 2)
+        weave(nc.vector, VECTOR_RUN, 2)
         quantise(1)
         quantise(2)
-        weave(nc.vector, 3)
+        weave(nc.vector, VECTOR_RUN, 3)
         quantise(3)
 
         last = (E - 1, ROW_BLOCKS - 1)

@@ -28,6 +28,9 @@ ROW_BLOCKS = K // P
 VECTOR_RUN, GPSIMD_RUN = 8, 4
 KIB = 1024
 
+GROUPS = [(0, 544), (544, 2 * C), (2 * C, 3 * C), (3 * C, S)]
+EARLY = 160
+
 HALVES = [0, T // 2, T]
 TAIL_CUTS = [0, 256, 512, 768, 960, T]
 
@@ -78,18 +81,20 @@ def tile_moe_sdb_relu_kernel(
             load_scale_rows(dys, dy_scales[0], q)
 
         a_planes = a.rearrange("(p t) j -> p t j", t=PACK)
-        factor = [keep.tile([P, PACK, C], F32, name=f"factor{e}", align_bytes=64) for e in range(E)]
-        saved = factor[: E - 1] + [overlay.tile([P, PACK, C], F32, name="saved_last", offset=4 * KIB, align_bytes=64)]
+        factor = [keep.tile([P, PACK, hi - lo], F32, name=f"factor{g}", align_bytes=64) for g, (lo, hi) in enumerate(GROUPS)]
+        saved = factor[:-1] + [overlay.tile([P, PACK, C], F32, name="saved_last", offset=0, align_bytes=64)]
         gate_rows = keep.tile([P, P], F32, name="gate_rows")
-        plane_pieces = [(0, 1), (1, 2), (2, PACK)]
-        for t0, t1 in plane_pieces:
-            nc.sync.dma_start(saved[0][:, t0:t1], a_planes[:, t0:t1, :C])
-            if t0 == 0:
+        early_gate = keep.tile([P, EARLY], F32, name="early_gate", align_bytes=64)
+        for t in range(PACK):
+            nc.sync.dma_start(saved[0][:, t], a_planes[:, t, : GROUPS[0][1]])
+            if t == 0:
                 nc.sync.dma_start(offs_t[:], offs)
-            if t0 == 1:
+            if t == 1:
                 nc.sync.dma_start(gate_rows[:], gate[: P * P // S].rearrange("r (c j) -> (r c) j", j=P))
-        for e in range(1, E):
-            nc.sync.dma_start(saved[e][:], a_planes[:, :, e * C : (e + 1) * C])
+        for g in range(1, len(GROUPS)):
+            nc.sync.dma_start(saved[g][:], a_planes[:, :, GROUPS[g][0] : GROUPS[g][1]])
+            if g == 1:
+                nc.sync.dma_start(early_gate[:], gate[:, :EARLY])
         nc.sync.dma_start(w1[:].bitcast(I32), w1t_words[:, 0].rearrange("e p k -> p e k").bitcast(I32))
         for q in range(QUADRANTS):
             load_scale_rows(w1s, w1t_scales[:, 0].rearrange("e b k -> b e k"), q)
@@ -103,11 +108,12 @@ def tile_moe_sdb_relu_kernel(
             )
 
         for t in range(PACK):
-            for h in range(T // BANK):
-                cols = slice(h * BANK, (h + 1) * BANK)
-                acc = bank(f"acc{t}_{h}", (2 * t + h) % DC_BANKS)
+            width = BANK // 2 if t == 0 else BANK
+            for h in range(T // width):
+                cols = slice(h * width, (h + 1) * width)
+                acc = bank(f"acc{t}_{h}", DC_BANKS + h if t == 0 else (2 * t + h) % DC_BANKS)[:, :width]
                 nc.tensor.matmul_mx(
-                    out=acc[:],
+                    out=acc,
                     lhsT=w2[:, t * P : (t + 1) * P].bitcast(E4M3),
                     lhsT_scale=w2s[:, t * P : (t + 1) * P],
                     rhs=dy[:, cols].bitcast(E5M2),
@@ -115,76 +121,84 @@ def tile_moe_sdb_relu_kernel(
                     start=True,
                     stop=True,
                 )
-                if (t, h) == (0, 0):
-                    nc.vector.tensor_copy(dc[t][:, cols], acc[:])
+                if t == 0 and h % 2 == 0:
+                    nc.vector.tensor_copy(dc[t][:, cols], acc)
                 else:
-                    nc.scalar.copy(dc[t][:, cols], acc[:])
+                    nc.scalar.copy(dc[t][:, cols], acc)
 
         turned = bank("turned", 0)
         nc.tensor.transpose(turned[:, :P], gate_rows[:], identity[:])
         gate_columns = keep.tile([P, S // P], F32, name="gate_columns")
-        nc.scalar.copy(gate_columns[:], turned[:, : S // P])
-        gates = [bank(f"gates{e}", DC_BANKS + e) for e in range(E)]
-        for e in (1, 0, 2, 3):
-            for at in range(0, C, P):
-                blk = (e * C + at) // P
-                nc.tensor.transpose(gates[e][:, at : at + P], gate_columns[:, blk : blk + 1].to_broadcast([P, P]), identity[:])
+        nc.scalar.copy(gate_columns[:, 1:], turned[:, 1 : S // P])
+        spans = [(EARLY, GROUPS[0][1])] + GROUPS[1:]
+        gates = {}
+        for g in (1, 0, 2, 3):
+            lo, hi = spans[g]
+            blocks = bank(f"gates{g}", DC_BANKS + g)
+            for n, blk in enumerate(range(lo // P, -(-hi // P))):
+                nc.tensor.transpose(blocks[:, n * P : (n + 1) * P], gate_columns[:, blk : blk + 1].to_broadcast([P, P]), identity[:])
+            gates[g] = blocks[:, lo % P : lo % P + hi - lo]
 
-        for t0, t1 in plane_pieces:
-            nc.vector.tensor_scalar(factor[0][:, t0:t1], saved[0][:, t0:t1], 0.0, None, ALU.is_gt)
+        for t in range(PACK):
+            nc.vector.tensor_scalar(factor[0][:, t], saved[0][:, t], 0.0, None, ALU.is_gt)
 
         def entries(tile, lo, hi):
             return tile[:, lo // LIST_ROWS : hi // LIST_ROWS]
 
         tags = ["picked0", "dy", "w2", "dys"]
-        picked = [keep.tile([P, PACK, C], F32, name=f"picked{e}", tag=tags[e], align_bytes=64) for e in range(E)]
-        for e in range(E):
+        picked = [
+            keep.tile([P, PACK, hi - lo], F32, name=f"picked{g}", tag=tags[g], align_bytes=64) for g, (lo, hi) in enumerate(GROUPS)
+        ]
+        for g, (lo, hi) in enumerate(GROUPS):
             for t in range(PACK):
-                window = dc[t][:].indirect(entries(offs_t, e * C, (e + 1) * C))
-                if e == 0:
-                    nc.vector.tensor_tensor(picked[e][:, t, :], window, factor[e][:, t, :], ALU.mult)
+                window = dc[t][:].indirect(entries(offs_t, lo, hi))
+                if g == 0:
+                    nc.vector.tensor_tensor(picked[g][:, t, :], window, factor[g][:, t, :], ALU.mult)
                 else:
-                    nc.scalar.activation(picked[e][:, t, :], window, ACT.Copy)
+                    nc.scalar.activation(picked[g][:, t, :], window, ACT.Copy)
 
-        woven = {0: keep.tile([P, C * PACK], BF16, name="woven0", align_bytes=64)}
+        woven_first = keep.tile([P, 2 * C * PACK], BF16, name="woven_first", align_bytes=64)
+        woven = {e: woven_first[:, e * C * PACK : (e + 1) * C * PACK] for e in range(2)}
         codes = {e: keep.tile([P, C], I32, name=f"codes{e}", align_bytes=64) for e in (2, 3)}
         scales = [keep.tile([P, C], U8, name=f"scales{e}", align_bytes=64) for e in range(E)]
-        dx = [keep.tile([P, S], F32, name=f"dx{b}") for b in range(ROW_BLOCKS)]
 
-        def gate_planes(e):
-            return gates[e][:].unsqueeze(1).to_broadcast([P, PACK, C])
+        def on_planes(row):
+            return row.unsqueeze(1).to_broadcast([P, PACK, row.shape[1]])
 
-        def fold(e):
-            nc.vector.scalar_tensor_tensor(factor[e][:], saved[e][:], 0.0, gate_planes(e), ALU.is_gt, ALU.mult)
+        def fold(g):
+            nc.vector.scalar_tensor_tensor(factor[g][:], saved[g][:], 0.0, on_planes(gates[g]), ALU.is_gt, ALU.mult)
 
-        def weave(engine, run, e):
-            other = gate_planes(e) if e == 0 else factor[e][:]
+        def weave(engine, run, result, planes, other):
             engine.tensor_tensor(
-                woven[e][:].rearrange("p (c i t) -> p c t i", i=run, t=PACK),
-                picked[e][:].rearrange("p t (c i) -> p c t i", i=run),
+                result.rearrange("p (c i t) -> p c t i", i=run, t=PACK),
+                planes.rearrange("p t (c i) -> p c t i", i=run),
                 other.rearrange("p t (c i) -> p c t i", i=run),
                 ALU.mult,
             )
 
         def quantise(e):
-            nc.vector.quantize_mx(out=codes[e][:].bitcast(E5M2), scales=scales[e][:], in_=woven[e][:])
+            nc.vector.quantize_mx(out=codes[e][:].bitcast(E5M2), scales=scales[e][:], in_=woven[e])
 
+        cut = GROUPS[0][1]
+        weave(nc.gpsimd, GPSIMD_RUN, woven_first[:, : EARLY * PACK], picked[0][:, :, :EARLY], on_planes(early_gate[:]))
         fold(1)
-        weave(nc.vector, VECTOR_RUN, 0)
-        woven[1] = keep.tile([P, C * PACK], BF16, name="woven1", align_bytes=64)
-        weave(nc.gpsimd, GPSIMD_RUN, 1)
+        weave(nc.vector, VECTOR_RUN, woven_first[:, EARLY * PACK : cut * PACK], picked[0][:, :, EARLY:], on_planes(gates[0]))
+        weave(nc.gpsimd, GPSIMD_RUN, woven_first[:, cut * PACK :], picked[1][:], factor[1][:])
         fold(2)
         fold(3)
-        woven[3] = overlay.tile([P, C * PACK], BF16, name="woven3", offset=12 * KIB, align_bytes=64)
-        woven[2] = overlay.tile([P, C * PACK], BF16, name="woven2", offset=4 * KIB, align_bytes=64)
-        codes[0] = overlay.tile([P, C], I32, name="codes0", offset=8 * KIB, align_bytes=64)
-        codes[1] = overlay.tile([P, C], I32, name="codes1", offset=10 * KIB, align_bytes=64)
+        woven[3] = keep.tile([P, C * PACK], BF16, name="woven3", align_bytes=64)[:]
+        woven[2] = overlay.tile([P, C * PACK], BF16, name="woven2", offset=4 * KIB, align_bytes=64)[:]
+        codes[0] = overlay.tile([P, C], I32, name="codes0", offset=0, align_bytes=64)
+        codes[1] = overlay.tile([P, C], I32, name="codes1", offset=2 * KIB, align_bytes=64)
         quantise(0)
-        weave(nc.vector, VECTOR_RUN, 2)
+        weave(nc.vector, VECTOR_RUN, woven[2], picked[2][:], factor[2][:])
         quantise(1)
         quantise(2)
-        weave(nc.vector, VECTOR_RUN, 3)
+        weave(nc.vector, VECTOR_RUN, woven[3], picked[3][:], factor[3][:])
         quantise(3)
+
+        dx = [keep.tile([P, S], F32, name=f"dx{b}") for b in range(ROW_BLOCKS - 1)]
+        dx.append(overlay.tile([P, S], F32, name="dx_last", offset=4 * KIB, align_bytes=64))
 
         last = (E - 1, ROW_BLOCKS - 1)
 
@@ -202,15 +216,15 @@ def tile_moe_sdb_relu_kernel(
             )
             return product
 
-        on_vector = [(2, 3), (3, 0), (3, 1), (3, 2)]
-        halved = (2, 2)
+        on_vector = [(1, 3), (3, 0), (3, 1), (3, 2)]
+        halved = (0, 3)
 
         def empty(e, b):
             product = multiply(e, b)
             slots = dx[b][:, e * C : (e + 1) * C]
             if (e, b) == halved:
-                nc.vector.tensor_copy(slots[:, : C // 2], product[:, : C // 2])
                 nc.scalar.copy(slots[:, C // 2 :], product[:, C // 2 :])
+                nc.vector.tensor_copy(slots[:, : C // 2], product[:, : C // 2])
             elif (e, b) in on_vector:
                 nc.vector.tensor_copy(slots, product[:])
             else:

@@ -28,11 +28,11 @@ ROW_BLOCKS = K // P
 VECTOR_RUN, GPSIMD_RUN = 8, 4
 KIB = 1024
 
-GROUPS = [(0, 544), (544, 2 * C), (2 * C, 3 * C), (3 * C, S)]
-EARLY = 160
+GROUPS = [(0, 576), (576, 2 * C), (2 * C, 3 * C), (3 * C, S)]
+EARLY = 176
 
 HALVES = [0, T // 2, T]
-TAIL_CUTS = [0, 256, 512, 768, 960, T]
+TAIL_CUTS = [0, 256, 512, 768, 896, T]
 
 
 def tile_moe_sdb_relu_kernel(
@@ -82,7 +82,7 @@ def tile_moe_sdb_relu_kernel(
 
         a_planes = a.rearrange("(p t) j -> p t j", t=PACK)
         factor = [keep.tile([P, PACK, hi - lo], F32, name=f"factor{g}", align_bytes=64) for g, (lo, hi) in enumerate(GROUPS)]
-        saved = factor[:-1] + [overlay.tile([P, PACK, C], F32, name="saved_last", offset=0, align_bytes=64)]
+        saved = factor[:2] + [overlay.tile([P, PACK, C], F32, name=f"saved{g}", offset=8 * KIB * (g - 2), align_bytes=64) for g in (2, 3)]
         gate_rows = keep.tile([P, P], F32, name="gate_rows")
         early_gate = keep.tile([P, EARLY], F32, name="early_gate", align_bytes=64)
         for t in range(PACK):
@@ -108,10 +108,10 @@ def tile_moe_sdb_relu_kernel(
             )
 
         for t in range(PACK):
-            width = BANK // 2 if t == 0 else BANK
+            width = BANK // 2 if t < 2 else BANK
             for h in range(T // width):
                 cols = slice(h * width, (h + 1) * width)
-                acc = bank(f"acc{t}_{h}", DC_BANKS + h if t == 0 else (2 * t + h) % DC_BANKS)[:, :width]
+                acc = bank(f"acc{t}_{h}", (DC_BANKS + h, h, h, 2 + h)[t])[:, :width]
                 nc.tensor.matmul_mx(
                     out=acc,
                     lhsT=w2[:, t * P : (t + 1) * P].bitcast(E4M3),
@@ -187,9 +187,9 @@ def tile_moe_sdb_relu_kernel(
         fold(2)
         fold(3)
         woven[3] = keep.tile([P, C * PACK], BF16, name="woven3", align_bytes=64)[:]
-        woven[2] = overlay.tile([P, C * PACK], BF16, name="woven2", offset=4 * KIB, align_bytes=64)[:]
+        woven[2] = overlay.tile([P, C * PACK], BF16, name="woven2", offset=12 * KIB, align_bytes=64)[:]
         codes[0] = overlay.tile([P, C], I32, name="codes0", offset=0, align_bytes=64)
-        codes[1] = overlay.tile([P, C], I32, name="codes1", offset=2 * KIB, align_bytes=64)
+        codes[1] = overlay.tile([P, C], I32, name="codes1", offset=8 * KIB, align_bytes=64)
         quantise(0)
         weave(nc.vector, VECTOR_RUN, woven[2], picked[2][:], factor[2][:])
         quantise(1)
@@ -198,7 +198,7 @@ def tile_moe_sdb_relu_kernel(
         quantise(3)
 
         dx = [keep.tile([P, S], F32, name=f"dx{b}") for b in range(ROW_BLOCKS - 1)]
-        dx.append(overlay.tile([P, S], F32, name="dx_last", offset=4 * KIB, align_bytes=64))
+        dx.append(overlay.tile([P, S], F32, name="dx_last", offset=12 * KIB, align_bytes=64))
 
         last = (E - 1, ROW_BLOCKS - 1)
 
@@ -243,5 +243,10 @@ def tile_moe_sdb_relu_kernel(
                 first = keep.tile([P, hi - lo], F32, name=f"first{b}_{lo}")
                 nc.scalar.activation(first[:], dx[b][:].indirect(entries(pos1_t, lo, hi)), ACT.Copy)
                 total = keep.tile([P, hi - lo], F32, name=f"total{b}_{lo}", align_bytes=64)
-                nc.vector.tensor_tensor(total[:], dx[b][:].indirect(entries(pos2_t, lo, hi)), first[:], ALU.add)
+                second = dx[b][:].indirect(entries(pos2_t, lo, hi))
+                if (b, hi) == (ROW_BLOCKS - 1, T):
+                    fetched = keep.tile([P, hi - lo], F32, name="fetched")
+                    nc.scalar.activation(fetched[:], second, ACT.Copy)
+                    second = fetched[:]
+                nc.vector.tensor_tensor(total[:], second, first[:], ALU.add)
                 nc.sync.dma_start(out[b * P : (b + 1) * P, lo:hi], total[:])

@@ -30,6 +30,7 @@ KIB = 1024
 
 GROUPS = [(0, 576), (576, 2 * C), (2 * C, 3 * C), (3 * C, S)]
 EARLY = 176
+SHARE = 320
 
 HALVES = [0, T // 2, T]
 TAIL_CUTS = [0, 256, 512, 768, 896, T]
@@ -73,9 +74,10 @@ def tile_moe_sdb_relu_kernel(
 
         for q in range(QUADRANTS // 2):
             load_scale_rows(dys, dy_scales[0], q)
-        nc.sync.dma_start(w2_raw[:], w2t_words[0].rearrange("p n t -> p (n t)").bitcast(I32))
         for q in range(QUADRANTS):
             load_scale_rows(w2s_raw, w2t_scales[0], q)
+            if q == 0:
+                nc.sync.dma_start(w2_raw[:], w2t_words[0].rearrange("p n t -> p (n t)").bitcast(I32))
         nc.sync.dma_start(dy[:], dy_words[0].rearrange("p n t -> p (n t)").bitcast(I32))
         for q in range(QUADRANTS // 2, QUADRANTS):
             load_scale_rows(dys, dy_scales[0], q)
@@ -87,9 +89,8 @@ def tile_moe_sdb_relu_kernel(
         early_gate = keep.tile([P, EARLY], F32, name="early_gate", align_bytes=64)
         for t in range(PACK):
             nc.sync.dma_start(saved[0][:, t], a_planes[:, t, : GROUPS[0][1]])
-            if t == 0:
+            if t == 2:
                 nc.sync.dma_start(offs_t[:], offs)
-            if t == 1:
                 nc.sync.dma_start(gate_rows[:], gate[: P * P // S].rearrange("r (c j) -> (r c) j", j=P))
         for g in range(1, len(GROUPS)):
             nc.sync.dma_start(saved[g][:], a_planes[:, :, GROUPS[g][0] : GROUPS[g][1]])
@@ -121,10 +122,7 @@ def tile_moe_sdb_relu_kernel(
                     start=True,
                     stop=True,
                 )
-                if t == 0 and h % 2 == 0:
-                    nc.vector.tensor_copy(dc[t][:, cols], acc)
-                else:
-                    nc.scalar.copy(dc[t][:, cols], acc)
+                nc.scalar.copy(dc[t][:, cols], acc)
 
         turned = bank("turned", 0)
         nc.tensor.transpose(turned[:, :P], gate_rows[:], identity[:])
@@ -223,8 +221,8 @@ def tile_moe_sdb_relu_kernel(
             product = multiply(e, b)
             slots = dx[b][:, e * C : (e + 1) * C]
             if (e, b) == halved:
-                nc.scalar.copy(slots[:, C // 2 :], product[:, C // 2 :])
-                nc.vector.tensor_copy(slots[:, : C // 2], product[:, : C // 2])
+                nc.scalar.copy(slots[:, SHARE:], product[:, SHARE:])
+                nc.vector.tensor_copy(slots[:, :SHARE], product[:, :SHARE])
             elif (e, b) in on_vector:
                 nc.vector.tensor_copy(slots, product[:])
             else:

@@ -64,10 +64,8 @@ def tile_moe_sdb_relu_kernel(
 
         nc.gpsimd.memset(w2s_raw[:].bitcast(I32), 0)
 
-        identity = keep.tile([P, P], F32, name="identity")
         distance = keep.tile([P, P], F32, name="distance")
         nc.gpsimd.iota(distance[:], [[1, P]], base=0, channel_multiplier=-1, allow_small_or_imprecise_dtypes=True)
-        nc.gpsimd.tensor_scalar(identity[:], distance[:], 0.0, 1.0, ALU.is_equal, ALU.mult)
 
         def load_scale_rows(tile, rows, q):
             nc.sync.dma_start(tile[32 * q : 32 * q + 4].bitcast(I32), rows[4 * q : 4 * q + 4].bitcast(I32))
@@ -108,6 +106,9 @@ def tile_moe_sdb_relu_kernel(
                 w2s[:].rearrange("p (t m) -> p t m", t=PACK)[:, t0:t1], w2s_raw[:].rearrange("p (m t) -> p t m", t=PACK)[:, t0:t1]
             )
 
+        identity = keep.tile([P, P], F32, name="identity", tag="w2s_raw")
+        nc.gpsimd.tensor_scalar(identity[:], distance[:], 0.0, 1.0, ALU.is_equal, ALU.mult)
+
         for t in range(PACK):
             width = BANK // 2 if t < 2 else BANK
             for h in range(T // width):
@@ -122,12 +123,15 @@ def tile_moe_sdb_relu_kernel(
                     start=True,
                     stop=True,
                 )
-                nc.scalar.copy(dc[t][:, cols], acc)
+                if (t, h) == (0, 0):
+                    nc.vector.tensor_copy(dc[t][:, cols], acc)
+                else:
+                    nc.scalar.copy(dc[t][:, cols], acc)
 
         turned = bank("turned", 0)
         nc.tensor.transpose(turned[:, :P], gate_rows[:], identity[:])
         gate_columns = keep.tile([P, S // P], F32, name="gate_columns")
-        nc.scalar.copy(gate_columns[:, 1:], turned[:, 1 : S // P])
+        nc.vector.tensor_copy(gate_columns[:, 1:], turned[:, 1 : S // P])
         spans = [(EARLY, GROUPS[0][1])] + GROUPS[1:]
         gates = {}
         for g in (1, 0, 2, 3):

from contextlib import ExitStack

import concourse.mybir as mybir

K, T, E, C, H, N = 512, 1024, 4, 512, 512, 512
S = E * C
FLOPS = 2 * N * H * T + 2 * H * K * S

F32 = mybir.dt.float32
BF16 = mybir.dt.bfloat16
I32 = mybir.dt.int32
U16 = mybir.dt.uint16
U8 = mybir.dt.uint8
E4M3 = mybir.dt.float8_e4m3fn_x4
E5M2 = mybir.dt.float8_e5m2_x4
E2M1 = mybir.dt.float4_e2m1fn_x4
ALU = mybir.AluOpType
ACT = mybir.ActivationFunctionType

P = 128
PACK = 4
QUADRANTS = 4
BANK = 512
BANK_BYTES = 2048
DC_BANKS = 4
LIST_ROWS = 16
ROW_BLOCKS = K // P
VECTOR_RUN, GPSIMD_RUN = 8, 4
KIB = 1024

GROUPS = [(0, 576), (576, 2 * C), (2 * C, 3 * C), (3 * C, S)]
EARLY = 176
SHARE = 320

HALVES = [0, T // 2, T]
TAIL_CUTS = [0, 256, 512, 768, 896, T]


def tile_moe_sdb_relu_kernel(
    tc, dy_words, dy_scales, w2t_words, w2t_scales, w1t_words, w1t_scales, a, gate, offs, pos1, pos2, out
):
    nc = tc.nc
    with ExitStack() as ctx:
        keep = ctx.enter_context(tc.tile_pool(name="keep", bufs=1))
        overlay = ctx.enter_context(tc.tile_pool(name="overlay", bufs=1))
        psum = ctx.enter_context(tc.psum_pool(name="psum", bufs=1))

        def bank(name, at):
            return psum.tile([P, BANK], F32, name=name, offset=at * BANK_BYTES)

        offs_t = keep.tile([P, S // LIST_ROWS], U16, name="offs_t")
        pos1_t = keep.tile([P, T // LIST_ROWS], U16, name="pos1_t")
        pos2_t = keep.tile([P, T // LIST_ROWS], U16, name="pos2_t")

        w2_raw = keep.tile([P, H], I32, name="w2_raw")
        w2s_raw = keep.tile([P, H], U8, name="w2s_raw")
        w2 = keep.tile([P, H], I32, name="w2", align_bytes=64)
        w2s = keep.tile([P, H], U8, name="w2s", align_bytes=64)
        dy = keep.tile([P, T], I32, name="dy", align_bytes=64)
        dys = keep.tile([P, T], U8, name="dys", align_bytes=64)
        w1 = keep.tile([P, E, 2 * K], U8, name="w1", align_bytes=64)
        w1s = keep.tile([P, E, K], U8, name="w1s", align_bytes=64)
        dc = [keep.tile([P, T], F32, name=f"dc{t}") for t in range(PACK)]

        nc.gpsimd.memset(w2s_raw[:].bitcast(I32), 0)

        distance = keep.tile([P, P], F32, name="distance")
        nc.gpsimd.iota(distance[:], [[1, P]], base=0, channel_multiplier=-1, allow_small_or_imprecise_dtypes=True)

        def load_scale_rows(tile, rows, q):
            nc.sync.dma_start(tile[32 * q : 32 * q + 4].bitcast(I32), rows[4 * q : 4 * q + 4].bitcast(I32))

        for q in range(QUADRANTS // 2):
            load_scale_rows(dys, dy_scales[0], q)
        for q in range(QUADRANTS):
            load_scale_rows(w2s_raw, w2t_scales[0], q)
            if q == 0:
                nc.sync.dma_start(w2_raw[:], w2t_words[0].rearrange("p n t -> p (n t)").bitcast(I32))
        nc.sync.dma_start(dy[:], dy_words[0].rearrange("p n t -> p (n t)").bitcast(I32))
        for q in range(QUADRANTS // 2, QUADRANTS):
            load_scale_rows(dys, dy_scales[0], q)

        a_planes = a.rearrange("(p t) j -> p t j", t=PACK)
        factor = [keep.tile([P, PACK, hi - lo], F32, name=f"factor{g}", align_bytes=64) for g, (lo, hi) in enumerate(GROUPS)]
        saved = factor[:2] + [overlay.tile([P, PACK, C], F32, name=f"saved{g}", offset=8 * KIB * (g - 2), align_bytes=64) for g in (2, 3)]
        gate_rows = keep.tile([P, P], F32, name="gate_rows")
        early_gate = keep.tile([P, EARLY], F32, name="early_gate", align_bytes=64)
        for t in range(PACK):
            nc.sync.dma_start(saved[0][:, t], a_planes[:, t, : GROUPS[0][1]])
            if t == 2:
                nc.sync.dma_start(offs_t[:], offs)
                nc.sync.dma_start(gate_rows[:], gate[: P * P // S].rearrange("r (c j) -> (r c) j", j=P))
        for g in range(1, len(GROUPS)):
            nc.sync.dma_start(saved[g][:], a_planes[:, :, GROUPS[g][0] : GROUPS[g][1]])
            if g == 1:
                nc.sync.dma_start(early_gate[:], gate[:, :EARLY])
        nc.sync.dma_start(w1[:].bitcast(I32), w1t_words[:, 0].rearrange("e p k -> p e k").bitcast(I32))
        for q in range(QUADRANTS):
            load_scale_rows(w1s, w1t_scales[:, 0].rearrange("e b k -> b e k"), q)
        nc.sync.dma_start(pos1_t[:], pos1)
        nc.sync.dma_start(pos2_t[:], pos2)

        nc.vector.tensor_copy(w2[:].rearrange("p (t m) -> p t m", t=PACK), w2_raw[:].rearrange("p (m t) -> p t m", t=PACK))
        for t0, t1 in ((0, 1), (1, PACK)):
            nc.vector.tensor_copy(
                w2s[:].rearrange("p (t m) -> p t m", t=PACK)[:, t0:t1], w2s_raw[:].rearrange("p (m t) -> p t m", t=PACK)[:, t0:t1]
            )

        identity = keep.tile([P, P], F32, name="identity", tag="w2s_raw")
        nc.gpsimd.tensor_scalar(identity[:], distance[:], 0.0, 1.0, ALU.is_equal, ALU.mult)

        for t in range(PACK):
            width = BANK // 2 if t < 2 else BANK
            for h in range(T // width):
                cols = slice(h * width, (h + 1) * width)
                acc = bank(f"acc{t}_{h}", (DC_BANKS + h, h, h, 2 + h)[t])[:, :width]
                nc.tensor.matmul_mx(
                    out=acc,
                    lhsT=w2[:, t * P : (t + 1) * P].bitcast(E4M3),
                    lhsT_scale=w2s[:, t * P : (t + 1) * P],
                    rhs=dy[:, cols].bitcast(E5M2),
                    rhs_scale=dys[:, cols],
                    start=True,
                    stop=True,
                )
                if (t, h) == (0, 0):
                    nc.vector.tensor_copy(dc[t][:, cols], acc)
                else:
                    nc.scalar.copy(dc[t][:, cols], acc)

        turned = bank("turned", 0)
        nc.tensor.transpose(turned[:, :P], gate_rows[:], identity[:])
        gate_columns = keep.tile([P, S // P], F32, name="gate_columns")
        nc.vector.tensor_copy(gate_columns[:, 1:], turned[:, 1 : S // P])
        spans = [(EARLY, GROUPS[0][1])] + GROUPS[1:]
        gates = {}
        for g in (1, 0, 2, 3):
            lo, hi = spans[g]
            blocks = bank(f"gates{g}", DC_BANKS + g)
            for n, blk in enumerate(range(lo // P, -(-hi // P))):
                nc.tensor.transpose(blocks[:, n * P : (n + 1) * P], gate_columns[:, blk : blk + 1].to_broadcast([P, P]), identity[:])
            gates[g] = blocks[:, lo % P : lo % P + hi - lo]

        for t in range(PACK):
            nc.vector.tensor_scalar(factor[0][:, t], saved[0][:, t], 0.0, None, ALU.is_gt)

        def entries(tile, lo, hi):
            return tile[:, lo // LIST_ROWS : hi // LIST_ROWS]

        tags = ["picked0", "dy", "w2", "dys"]
        picked = [
            keep.tile([P, PACK, hi - lo], F32, name=f"picked{g}", tag=tags[g], align_bytes=64) for g, (lo, hi) in enumerate(GROUPS)
        ]
        for g, (lo, hi) in enumerate(GROUPS):
            for t in range(PACK):
                window = dc[t][:].indirect(entries(offs_t, lo, hi))
                if g == 0:
                    nc.vector.tensor_tensor(picked[g][:, t, :], window, factor[g][:, t, :], ALU.mult)
                else:
                    nc.scalar.activation(picked[g][:, t, :], window, ACT.Copy)

        woven_first = keep.tile([P, 2 * C * PACK], BF16, name="woven_first", align_bytes=64)
        woven = {e: woven_first[:, e * C * PACK : (e + 1) * C * PACK] for e in range(2)}
        codes = {e: keep.tile([P, C], I32, name=f"codes{e}", align_bytes=64) for e in (2, 3)}
        scales = [keep.tile([P, C], U8, name=f"scales{e}", align_bytes=64) for e in range(E)]

        def on_planes(row):
            return row.unsqueeze(1).to_broadcast([P, PACK, row.shape[1]])

        def fold(g):
            nc.vector.scalar_tensor_tensor(factor[g][:], saved[g][:], 0.0, on_planes(gates[g]), ALU.is_gt, ALU.mult)

        def weave(engine, run, result, planes, other):
            engine.tensor_tensor(
                result.rearrange("p (c i t) -> p c t i", i=run, t=PACK),
                planes.rearrange("p t (c i) -> p c t i", i=run),
                other.rearrange("p t (c i) -> p c t i", i=run),
                ALU.mult,
            )

        def quantise(e):
            nc.vector.quantize_mx(out=codes[e][:].bitcast(E5M2), scales=scales[e][:], in_=woven[e])

        cut = GROUPS[0][1]
        weave(nc.gpsimd, GPSIMD_RUN, woven_first[:, : EARLY * PACK], picked[0][:, :, :EARLY], on_planes(early_gate[:]))
        fold(1)
        weave(nc.vector, VECTOR_RUN, woven_first[:, EARLY * PACK : cut * PACK], picked[0][:, :, EARLY:], on_planes(gates[0]))
        weave(nc.gpsimd, GPSIMD_RUN, woven_first[:, cut * PACK :], picked[1][:], factor[1][:])
        fold(2)
        fold(3)
        woven[3] = keep.tile([P, C * PACK], BF16, name="woven3", align_bytes=64)[:]
        woven[2] = overlay.tile([P, C * PACK], BF16, name="woven2", offset=12 * KIB, align_bytes=64)[:]
        codes[0] = overlay.tile([P, C], I32, name="codes0", offset=0, align_bytes=64)
        codes[1] = overlay.tile([P, C], I32, name="codes1", offset=8 * KIB, align_bytes=64)
        quantise(0)
        weave(nc.vector, VECTOR_RUN, woven[2], picked[2][:], factor[2][:])
        quantise(1)
        quantise(2)
        weave(nc.vector, VECTOR_RUN, woven[3], picked[3][:], factor[3][:])
        quantise(3)

        dx = [keep.tile([P, S], F32, name=f"dx{b}") for b in range(ROW_BLOCKS - 1)]
        dx.append(overlay.tile([P, S], F32, name="dx_last", offset=12 * KIB, align_bytes=64))

        last = (E - 1, ROW_BLOCKS - 1)

        def multiply(e, b):
            at = (ROW_BLOCKS * e + b) % (2 * ROW_BLOCKS) if (e, b) != last else ROW_BLOCKS + 1
            product = bank(f"product{b}_{e}", at)
            nc.tensor.matmul_mx(
                out=product[:],
                lhsT=w1[:, e, 2 * b * P : 2 * (b + 1) * P].bitcast(E2M1),
                lhsT_scale=w1s[:, e, b * P : (b + 1) * P],
                rhs=codes[e][:].bitcast(E5M2),
                rhs_scale=scales[e][:],
                start=True,
                stop=True,
            )
            return product

        on_vector = [(1, 3), (3, 0), (3, 1), (3, 2)]
        halved = (0, 3)

        def empty(e, b):
            product = multiply(e, b)
            slots = dx[b][:, e * C : (e + 1) * C]
            if (e, b) == halved:
                nc.scalar.copy(slots[:, SHARE:], product[:, SHARE:])
                nc.vector.tensor_copy(slots[:, :SHARE], product[:, :SHARE])
            elif (e, b) in on_vector:
                nc.vector.tensor_copy(slots, product[:])
            else:
                nc.scalar.copy(slots, product[:])

        for e in range(E):
            for b in range(ROW_BLOCKS):
                if (e, b) != last:
                    empty(e, b)

        for b in range(ROW_BLOCKS):
            if b == ROW_BLOCKS - 1:
                empty(*last)
            cuts = TAIL_CUTS if b == ROW_BLOCKS - 1 else HALVES
            for lo, hi in zip(cuts, cuts[1:]):
                first = keep.tile([P, hi - lo], F32, name=f"first{b}_{lo}")
                nc.scalar.activation(first[:], dx[b][:].indirect(entries(pos1_t, lo, hi)), ACT.Copy)
                total = keep.tile([P, hi - lo], F32, name=f"total{b}_{lo}", align_bytes=64)
                second = dx[b][:].indirect(entries(pos2_t, lo, hi))
                if (b, hi) == (ROW_BLOCKS - 1, T):
                    fetched = keep.tile([P, hi - lo], F32, name="fetched")
                    nc.scalar.activation(fetched[:], second, ACT.Copy)
                    second = fetched[:]
                nc.vector.tensor_tensor(total[:], second, first[:], ALU.add)
                nc.sync.dma_start(out[b * P : (b + 1) * P, lo:hi], total[:])
